import numpy as np, ml_dtypes
CORES = [25,29,65,69,153,157,193,197]
N = 8
import mx_ref
BF = ml_dtypes.bfloat16
def gcols(t, e):
    v = np.concatenate([t.reshape(8, 16, -1, 4), np.zeros((8, 16, 1, 4), BF)], axis=2)
    return np.ascontiguousarray(np.stack([v[g][:, e[g]] for g in range(8)])).reshape(128, -1)
def tile(rs):
    return np.stack(rs, axis=2).reshape(128, -1).astype(BF)
def cut(t, i, w=512):
    return t[:, w * i:w * i + w]
def pick(q, e):
    c = np.concatenate([q[0].reshape(128, -1, 4), np.zeros((128, 1, 4), np.uint8)], axis=1); s = np.concatenate([q[1], np.ones((16, 1), np.uint8)], axis=1)
    return (np.ascontiguousarray(c[:, e].reshape(128, -1)), np.ascontiguousarray(s[:, e]))
def join(*qs):
    return (np.concatenate([q[0] for q in qs], axis=1), np.concatenate([q[1] for q in qs], axis=1))
def put(q, e, v):
    c, s = q[0].reshape(128, -1, 4).copy(), q[1].copy(); c[:, e] = v[0].reshape(128, -1, 4); s[:, e] = v[1]
    return (c.reshape(128, -1), s)
def pk(c, s):
    return (np.ascontiguousarray(c), mx_ref.live(s))
def emit(q):
    return q[0], q[1]
def packed(v, rng):
    q = [mx_ref.quantize(np.ascontiguousarray(v[r])) for r in range(N)]
    return np.stack([a for a, b in q]), np.stack([mx_ref.plane(b, rng) for a, b in q])
def values_of_codes():
    e, c = np.zeros((128, 128, 4), np.float32), np.zeros((128, 2, 4), np.uint8)
    e[np.arange(128), np.arange(128), 0] = 1
    c[:127, :, 0] = np.arange(256).reshape(2, 128).T[:127]
    return mx_ref.matmul(mx_ref.quantize(e.reshape(128, 512).astype(BF)), (c.reshape(128, 8), np.full((16, 2), 127, np.uint8))).T.reshape(-1).astype(np.float64)
CODE_VALUE, SCALE_VALUE = values_of_codes(), 2.0 ** (np.arange(256) - 127.0)
def decode(q):
    return (CODE_VALUE[q[0]].reshape(16, 8, -1, 4) * SCALE_VALUE[q[1]][:, None, :, None] + 0.0).reshape(128, -1).astype(np.float32)
def f(rng, *shape):
    return mx_ref.flush((rng.standard_normal(shape, dtype=np.float32) * np.exp2(rng.integers(-2, 3, shape[:-1] + (1,)))).astype(BF))
def wide(rng, *shape, cols=0):
    v = rng.standard_normal(shape, dtype=np.float32) * np.exp2(rng.integers(-12, 13, shape)).astype(np.float32)
    if cols: v *= np.repeat(np.exp2(rng.integers(-cols, cols + 1, shape[:-2] + (1, shape[-1] // 4))) * (rng.random(shape[:-2] + (1, shape[-1] // 4)) > 0.0625), 4, axis=-1).astype(np.float32)
    return mx_ref.flush(v.astype(BF))
C, K, A, P, L, R = 480, 6, 64, 224, 96, 3
DECIDE = (16 * np.arange(8)[:, None] + np.arange(8)).reshape(-1)
def address(s):
    a = np.zeros((8, s.shape[1]), np.int64)
    for i in range(K): a |= (s[i::16] > 0).astype(np.int64) << i
    return a
def match(ad):
    e = np.argsort(ad, kind="stable")
    e = e[ad[e] >= 0]
    s = ad[e]
    k = (np.arange(len(e)) - np.searchsorted(s, s)) % 2
    two = np.flatnonzero(k)
    two = two[np.argsort(e[two])][:P]
    pair, wait = np.full((2, P), -1), np.full(A, -1)
    pair[0, :len(two)] = e[two - 1]
    pair[1, :len(two)] = e[two]
    last = np.flatnonzero((k == 0) & (np.append(s, -1)[1:] != s))
    wait[s[last]] = e[last]
    return pair, wait
def big(v):
    v = v.astype(np.float32)
    v[np.abs(v) < np.float32(2.0 ** -16)] = 0
    return v.astype(BF)
def numbers_of(rng):
    return {"x": big(f(rng, N, 128, 4 * C)), "u": np.array(f(rng, N, 128, 512)), "v": np.array(f(rng, N, 128, 512))}
def weights(rng, w):
    c, p = packed(w, rng)
    return {"wc": c, "ws": p}
def setup_inputs(rng):
    return {**numbers_of(rng), **weights(rng, big(f(rng, N, 128, 2048)))}
def setup_inputs_one(rng):
    d = numbers_of(rng)
    e = rng.permutation(N) % 4
    x = d["x"].reshape(N, 8, 16, C, 4)
    for r in range(N):
        k = rng.permutation(C) % 3
        if e[r] == 0: k = np.zeros(C, int)
        if e[r] == 1: k = np.full(C, 2)
        a = x[r][:, :8, :3].copy()
        a[:, :, 2] = 0
        x[r][:, :8] = a[:, :, k]
    u = d["u"].reshape(N, 8, 16, 128, 4)
    u[:, :, 8:, DECIDE] = 0
    w = big(f(rng, N, 128, 2048)).reshape(N, 8, 16, 4, 8, 16, 4)
    w[:, :, 8:, :, :, :8] = 0
    return {"x": x.reshape(N, 128, 4 * C), "u": u.reshape(N, 128, 512), "v": d["v"], **weights(rng, w.reshape(N, 128, 2048))}
def some(rng, k):
    return np.bincount(rng.integers(0, A, k), minlength=A)
def setup_inputs_caps(rng):
    d = numbers_of(rng)
    x = d["x"].reshape(N, 8, 16, C, 4)
    u = d["u"].reshape(N, 128, 128, 4)
    z = rng.permutation(N) % 4
    size = np.exp2(np.array([-28.0, -12.0, 0.0, 28.0])[z])
    one = np.exp2(np.array([-30.0, 0.0, 0.0, 30.0])[z]).astype(np.float32)
    u[:, :, DECIDE] = 0
    u[:, DECIDE, DECIDE, 0] = one.astype(BF)[:, None]
    u[:, DECIDE, DECIDE, 1] = (-one).astype(BF)[:, None]
    lead = np.array([[[0, 0], [1, -1], [-2, 1]], [[1, 1], [2, -1], [-1, 2]]])
    o = rng.permutation(8)
    g1, g2 = int(o[6]), int(o[7])
    turn = int(rng.integers(4))
    few = (C - A) // 2
    come = np.bincount(rng.permutation(A)[np.arange(L) % A], minlength=A)
    own = (come + 1) % 2
    own = own + 2 * some(rng, (few - np.sum(own)) // 2)
    made = (come + 1) % 2
    made[rng.permutation(A)[:((few + L) // 2 - np.sum(made)) // 2]] += 2
    early = np.bincount(rng.permutation(np.repeat(np.flatnonzero(made), 2))[:L], minlength=A)
    none, half = 0 * come, come // 2
    plan = {g1: [(own, none), (come + some(rng, P - L), come)] * 2,
            g2: [(2 * made - early, none), (early + some(rng, P - L), early), (come + 2 * some(rng, (few - L) // 2), none), (half + some(rng, P - np.sum(half)), half)]}
    for r in range(N):
        a, b = np.zeros(8, int), np.zeros(8, int)
        a[o[:6]] = rng.permutation(6) % 5
        b[o[:6]] = rng.permutation(6) % 5
        part = (r ^ turn) & 3
        for g in range(8):
            if g in plan:
                i = np.repeat(np.arange(A), plan[g][part][0])
                i = i // 2 + i % 2 * (A // 2)
                odd = C - 2 * len(i)
            else:
                odd = [C - 2 * P, C - 2 * P - 2, C - 2 * P + 2, 0, A][a[g]]
                i = rng.integers(0, A, (C - odd) // 2)
            e = rng.permutation(np.concatenate([rng.permutation(A)[:odd], i, i]))
            pair, wait = match(e)
            pair = pair[:, pair[0] >= 0]
            n = pair.shape[1]
            if g in plan:
                to = 2 * e[pair[0]] % A + 2 * e[pair[0]] // A
                j = rng.permutation(n)
                j = j[np.argsort(to[j], kind="stable")]
                go = np.zeros(n, bool)
                go[j] = np.arange(n) - np.searchsorted(to[j], to[j]) < plan[g][part][1][to[j]]
            else:
                go = rng.permutation(n) < [L, L + 1, L - 1, 0, n][b[g]]
            h = lead[go.astype(int), rng.integers(0, 3, n)]
            mark = np.zeros((8, C))
            mark[:K] = ((e >> np.arange(K)[:, None]) & 1) * 2 - 1
            if z[r] == 0 and g != g2: mark[:K] *= 0.25
            mark[7, pair[0]] = h[:, 0]
            mark[7, pair[1]] = h[:, 1]
            if g == g2:
                mark[7] = -8 if part == 0 else -1
                mark[7, pair[:, go]] = 4
                if part == 2: mark[7, wait[come > 0]] = 4
            m = np.stack([np.maximum(mark, 0), np.maximum(-mark, 0) + 0.0, 0 * mark + 0.0, 0 * mark + 0.0], axis=2)
            x[r, g, :8] = (np.abs(m) * (1.0 if g == g2 else size[r])).astype(np.float32).astype(BF)
    w = big(f(rng, N, 128, 2048)).reshape(N, 128, 4, 128, 4)
    w[:, DECIDE] = 0
    w[:, :, :, DECIDE] = 0
    to = DECIDE - DECIDE % 16 + np.where(DECIDE % 16 < K, (DECIDE % 16 + 1) % K, DECIDE % 16)
    less = (z == 0)[:, None] & ((DECIDE % 16 == 7) & (DECIDE // 16 != g2))[None, :]
    for b in range(4): w[:, DECIDE, b, to, b] = np.where(less, 0.0625, 32.0).astype(np.float32).astype(BF)
    return {"x": x.reshape(N, 128, 4 * C), "u": u.reshape(N, 128, 512), "v": d["v"], **weights(rng, w.reshape(N, 128, 2048))}
def setup_inputs_huge(rng):
    d = numbers_of(rng)
    o = rng.permutation(N)
    x = 2.0 ** 30 * (0.5 + 0.5 * rng.random((N, 128, 4 * C))) * (rng.random((N, 128, 4 * C)) < 0.5)
    q = int(rng.integers(8))
    x[o % 2 == 1, 16 * q:16 * q + 16] = 0
    c = np.argsort(rng.random((N, 512, 64)), axis=1) % 2 * 2.0 - 1.0
    c = c.reshape(N, 128, 4, 64).transpose(0, 1, 3, 2).copy()
    for r in range(N):
        s = rng.permutation(8) % 2 * 2.0 - 1.0
        if o[r] < 2: s = np.full(8, 2.0 * o[r] - 1.0)
        c[r][:, 7::8] = s[None, :, None]
        k = 8 * np.arange(8) + rng.integers(0, K, 8)
        c[r][:, k] = (rng.permutation(8) % 2 * 2.0 - 1.0)[None, :, None]
    u = d["u"].reshape(N, 128, 128, 4)
    u[:, :, DECIDE] = (2.0 ** 30 * (0.75 + 0.25 * rng.random((N, 128, 64, 4))) * c).astype(np.float32).astype(BF)
    w = np.zeros((N, 128, 4, 128, 4), np.float32)
    i = np.arange(128)
    for b in range(4): w[:, i, b, i, b] = 32
    return {"x": x.astype(np.float32).astype(BF), "u": u.reshape(N, 128, 512), "v": d["v"], **weights(rng, w.reshape(N, 128, 2048).astype(BF))}
def setup_inputs_spread(rng):
    d = setup_inputs(rng)
    d["x"] = big(wide(rng, N, 128, 4 * C, cols=6))
    return d
def check_inputs(d):
    b = []
    for k in ("x", "u", "v"):
        a = np.abs(d[k].astype(np.float32))
        if not (np.isfinite(a).all() and ((a == 0) | (a >= 2.0 ** -30) & (a <= 2.0 ** 30)).all()): b.append("a value of " + k)
    return b
def reference(x, u, v, wc, ws):
    qu = [mx_ref.quantize(u[r]) for r in range(N)]
    lay = [pk(wc[r], ws[r]) for r in range(N)]
    pool = [np.concatenate([np.zeros((128, 4 * A), BF), x[r]], axis=1) for r in range(N)]
    ad = [np.concatenate([np.full((8, A), -1), address(mx_ref.matmul(qu[r], mx_ref.quantize(x[r])))], axis=1) for r in range(N)]
    y, occ = np.zeros((N, 128, A + P), np.float32), np.zeros((N, 8, A + P), np.float32)
    oc, osc = np.zeros((N, 128, 4 * (A + P)), np.uint8), np.zeros((N, 16, A + P), np.uint8)
    for t in range(R):
        kept, slots, sent, dest = [], [], [], []
        for r in range(N):
            found = [match(a) for a in ad[r]]
            pair, wait = np.stack([e[0] for e in found]), np.stack([e[1] for e in found])
            have = pair[:, 0] >= 0
            one, two = gcols(pool[r], pair[:, 0]), gcols(pool[r], pair[:, 1])
            q = mx_ref.quantize(((one.astype(np.float32) + two.astype(np.float32)) * np.float32(0.5)).astype(BF))
            h = tile([np.maximum(mx_ref.matmul(pick(lay[r], np.arange(128 * b, 128 * b + 128)), q), np.float32(0.0)) * np.float32(0.03125) for b in range(4)])
            store = gcols(pool[r], wait)
            if t == R - 1:
                q = mx_ref.quantize(np.concatenate([store, gcols(h, np.where(have, np.arange(P), -1))], axis=1))
                y[r] = mx_ref.matmul(mx_ref.quantize(v[r]), q)
                occ[r] = np.concatenate([wait >= 0, have], axis=1)
                oc[r], osc[r] = emit(q)
                continue
            s = mx_ref.matmul(qu[r], mx_ref.quantize(h))
            to = np.where(have, address(s), -1)
            go, at = np.full((8, L), -1), np.full((8, L), -1)
            for g in range(8):
                i = np.flatnonzero(have[g] & (s[16 * g + 7] > 0))[:L]
                go[g, :len(i)] = i
                at[g, :len(i)] = to[g, i]
                to[g, i] = -1
            sent.append(mx_ref.quantize(gcols(h, go)))
            dest.append(at)
            kept.append(np.concatenate([store, h], axis=1))
            slots.append(np.concatenate([np.where(wait >= 0, np.arange(A), -1), to], axis=1))
        if t < R - 1:
            came = decode(join(*sent)).astype(BF)
            for r in range(N):
                e = r ^ (1 << t)
                pool[r] = np.concatenate([kept[r], cut(came, e, 4 * L)], axis=1)
                ad[r] = np.concatenate([slots[r], dest[e]], axis=1)
    return {"y": y, "occ": occ, "oc": oc, "osc": osc}

@@ -1,0 +1,555 @@
+import math
+from concourse.mybir import dt, AluOpType, ActivationFunctionType
+
+ALU = AluOpType
+ACT = ActivationFunctionType
+F32, BF, F16, I32, U16, U8, Q4 = "float32", "bfloat16", "float16", "int32", "uint16", "uint8", "float8_e4m3fn_x4"
+
+C, NA, L = 480, 64, 96
+PR = [224, 192, 160]
+BASE = [128, 608, 928]
+OFF = 124
+NID = 1216
+B = 2048.0
+FILL = -1024.0
+
+
+def sb(n, d):
+    return ("sbuf", [128, n], d)
+
+
+SCRATCH = {
+    "xt": sb(1920, BF), "ut": sb(512, BF), "vt": sb(512, BF),
+    "qx": sb(480, Q4), "sx": sb(480, U8), "qu": sb(128, Q4), "su": sb(128, U8), "qu7": sb(128, Q4), "su7": sb(128, U8),
+    "qv": sb(128, Q4), "sv": sb(128, U8), "wq": sb(512, Q4), "wp": sb(512, U8),
+    "pool": sb(4 * (NID - OFF), BF), "bt0": sb(512, BF), "bt": sb(896, BF), "sg": sb(224, BF), "qb": sb(256, Q4), "sbb": sb(256, U8),
+    "ii": sb(32, I32), "ij": sb(32, I32), "col": sb(32, F32), "iof": sb(NID, F32), "ids": sb(NID, F16), "kfr": sb(224, F32),
+    "jg": sb(128, F32), "jh": sb(140, F32), "tm1": sb(24, F32), "tm2": sb(24, F32), "pat": sb(24, F32),
+    "c16": sb(496, BF), "c4": sb(224, BF), "c2": sb(64, BF), "r16": sb(992, BF), "r4": sb(640, BF),
+    "one": sb(512, BF), "tab": sb(768, BF), "uc": sb(32, F32), "o7": sb(8, U16),
+    "wc0": sb(512, BF), "wb0": sb(512, BF), "et": sb(2048, BF),
+    "qwc": sb(128, Q4), "swc": sb(128, U8), "qwb": sb(128, Q4), "swb": sb(128, U8), "qe": sb(512, Q4), "se": sb(512, U8),
+    "oe": sb(120, U16), "e": sb(1920, BF), "d0": sb(1920, BF), "yy": sb(1924, F16), "ys": sb(4, F32), "vv": sb(1920, F16),
+    "q4": sb(64 + 1984, F16), "tt": sb(992, F16), "rr": sb(992, F16), "sel": sb(64, F32), "pw": sb(32, U16),
+    "fb": sb(496, BF), "cum": sb(496, F16), "cs": sb(2, F32), "cw": sb(496, F16), "nf": sb(32, F32), "zz": sb(32, F32), "ds": sb(32, F32),
+    "od": sb(32, U16), "win": sb(1152, F32), "ptab": sb(504, F32),
+    "w4": sb(224, F32), "w16": sb(224, F32), "o2": sb(56, U16), "o16": sb(14, U16), "g1": sb(224, F16), "w1": sb(224, F16), "o1": sb(56, U16),
+    "two": sb(896, BF), "bb": sb(896, BF), "qbb": sb(256, Q4), "sbq": sb(256, U8), "hh": sb(896, BF),
+    "qh0": sb(224, Q4), "sh0": sb(224, U8), "qh1": sb(192, Q4), "sh1": sb(192, U8),
+    "thr": sb(224, F32), "nh": sb(224, BF), "nc": sb(448, F16), "ncw": sb(448, F16), "la": sb(48, F32),
+    "ol": sb(14, U16), "val": sb(224, F32), "lwin": sb(832, F32), "lw": sb(96, F32), "li": sb(48, I32),
+    "ls0": sb(48, U16), "ls1": sb(48, U16), "t1": sb(224, F16), "reg": sb(224, F16), "idx": sb(224, F16), "iw": sb(224, F16),
+    "rq0": sb(224, Q4), "rs0": sb(224, U8), "rl0": sb(48, U16), "rq1": sb(192, Q4), "rs1": sb(192, U8), "rl1": sb(48, U16),
+    "mq": sb(192, Q4), "ms": sb(192, U8), "ml": sb(48, U16), "dst": sb(896, BF),
+    "tl": sb(1152, BF), "qt": sb(288, Q4), "st": sb(288, U8), "ot": sb(20, U16), "hm": sb(640, F32), "occb": sb(288, F32), "yb": sb(288, F32),
+    "pr": ("psum", [128, 2048], F32), "ps": ("psum", [128, 2048], F32),
+}
+SEMAPHORES = ["sv_", "sa_", "sp_", "sg_", "lu", "lx0", "lx1", "lw_", "lp_", "lv", "out",
+              "aq0", "as0", "al0", "aq1", "as1", "al1", "mq_", "ms_", "ml_", "loc"]
+(PI, PQ, G4, H4, GM, QOFF, FIX16, FIX4, NFG, TCOL, C1, C20, C21, C22, O16, DFX, WT, WT0, G1, AOF, KOF, IFX, F256, TMP, POW, TM2) = range(26)
+
+
+def relay_of(src, dst, k, topo):
+    ok = [c for c in topo.cores_of(src) if c != src and topo.may_write(c, dst)]
+    near = [c for c in ok if topo.die(c) == topo.die(src)] or ok
+    return near[0] if k == "q" else near[-1]
+
+
+def relay_program(g, core, T, topo, src, dst):
+    rid, pid = topo.addr(dst, core)
+    n = 0
+    for k in "qsl":
+        if relay_of(src, dst, k, topo) == core:
+            g.wait_ge(T.sem["m%s_" % k], len(topo.engines(src, core)))
+            a, b = T["r%s1" % k][:], T["m" + k][:]
+            if k == "q":
+                a, b = a.bitcast(dt.uint8), b.bitcast(dt.uint8)
+            g.remote_dma(a, b, T.sem["a%s1" % k], T.sem["loc"], pid, rid, topo.mask(core, dst))
+            n += len(topo.engines(core, dst))
+    if n:
+        g.wait_ge(T.sem["loc"], n)
+
+
+def rank_program(g, core, T, topo):
+    rank = T.rank_of(core)
+    if rank is None:
+        for r, c in enumerate(T.cores):
+            d = T.cores[r ^ 2]
+            if core in topo.cores_of(c) and not topo.may_write(c, d):
+                relay_program(g, core, T, topo, c, d)
+        return
+    Q = {"v": g.vector, "a": g.scalar, "p": g.tensor, "g": g, "s": g.sync}
+    SEM = {"v": "sv_", "a": "sa_", "p": "sp_", "g": "sg_"}
+    count = {}
+    waited = {k: {} for k in Q}
+    log = {}
+
+    def R(name, lo=0, hi=None, step=1):
+        n = SCRATCH[name][1][1]
+        hi = n if hi is None else hi
+        ap = T[name][:, lo:hi] if step == 1 else T[name][:, lo:hi:step]
+        if SCRATCH[name][0] == "psum":
+            return (ap, [(name, lo // 512 * 512, lo // 512 * 512 + 512, 1, True)])
+        return (ap, [(name, lo, hi, step, False)])
+
+    def col(c):
+        return R("col", c, c + 1)
+
+    def ind(w, o):
+        return (w[0].indirect(o[0]), w[1] + o[1])
+
+    def wait(q, tok):
+        if waited[q].get(tok[0], 0) < tok[1]:
+            Q[q].wait_ge(T.sem[tok[0]], tok[1])
+            waited[q][tok[0]] = tok[1]
+
+    def meet(a, b):
+        if a[1] >= b[2] or b[1] >= a[2]:
+            return False
+        return not (a[3] == b[3] and a[3] > 1 and (a[1] - b[1]) % a[3] != 0)
+
+    def deps(q, outs, ins):
+        need = {}
+        for acc, wr in [(a, True) for a in outs] + [(a, False) for a in ins]:
+            for old, owr, tok, oq in log.get(acc[0], []):
+                if (wr or owr or (acc[4] and oq != q)) and meet(acc, old):
+                    need[tok[0]] = max(need.get(tok[0], 0), tok[1])
+        for s in need:
+            wait(q, (s, need[s]))
+
+    def note(q, outs, ins, tok):
+        for acc, wr in [(a, True) for a in outs] + [(a, False) for a in ins]:
+            log.setdefault(acc[0], []).append((acc, wr, tok, q))
+
+    def emit(q, make, outs, ins, sem=None):
+        outs = [a for o in outs for a in o[1]]
+        ins = [a for o in ins if isinstance(o, tuple) for a in o[1]]
+        deps(q, outs, ins)
+        s, n = (SEM[q], 1) if sem is None else (sem, 16)
+        make().then_inc(T.sem[s], n)
+        count[s] = count.get(s, 0) + n
+        note(q, outs, ins, (s, count[s]))
+
+    def ap(x):
+        return x[0] if isinstance(x, tuple) else x
+
+    def ts(o, i, s1, op0, s2=None, op1=None):
+        if op1 is None:
+            emit("v", lambda: g.vector.tensor_scalar(o[0], i[0], ap(s1), None, op0), [o], [i, s1])
+        else:
+            emit("v", lambda: g.vector.tensor_scalar(o[0], i[0], ap(s1), ap(s2), op0, op1), [o], [i, s1, s2])
+
+    def tt(o, a, b, op):
+        emit("v", lambda: g.vector.tensor_tensor(o[0], a[0], b[0], op), [o], [a, b])
+
+    def cp(o, i):
+        emit("v", lambda: g.vector.tensor_copy(o[0], i[0]), [o], [i])
+
+    def scat(w, offs, i):
+        emit("v", lambda: g.vector.tensor_copy(w[0].indirect(offs[0]), i[0]), [w], [i, offs])
+
+    def scan(o, a, b, init, op0, op1):
+        emit("v", lambda: g.vector.tensor_tensor_scan(o[0], a[0], b[0], ap(init), op0, op1), [o], [a, b, init])
+
+    def ms(o, c):
+        emit("v", lambda: g.vector.memset(o[0], c), [o], [])
+
+    def tr(o, i):
+        emit("v", lambda: g.vector.transpose(o[0], i[0]), [o], [i])
+
+    def quant(qn, sn, lo, hi, i):
+        a, b = R(qn, lo, hi), R(sn, lo, hi)
+        emit("v", lambda: g.vector.quantize_mx(a[0], b[0], i[0]), [a, b], [i])
+
+    def mm(o, wq, ws, w0, xq, xs, lo, hi):
+        a, b, c, d = R(wq, w0, w0 + 128), R(ws, w0, w0 + 128), R(xq, lo, hi), R(xs, lo, hi)
+        emit("p", lambda: g.tensor.matmul_mx(o[0], a[0], b[0], c[0], d[0], True, True), [o], [a, b, c, d])
+
+    def act(o, i, f, scale=1.0, bias=None):
+        if bias is None:
+            emit("a", lambda: g.scalar.activation(o[0], i[0], f, scale=ap(scale)), [o], [i, scale])
+        else:
+            emit("a", lambda: g.scalar.activation(o[0], i[0], f, bias=ap(bias), scale=ap(scale)), [o], [i, scale, bias])
+
+    def lin(c, a, scale, bias):
+        act(col(c), col(a), ACT.Identity, scale, bias)
+
+    def iota(o, pat, base, cm, small=True):
+        if small:
+            emit("g", lambda: g.iota(o[0], pat, base, cm, allow_small_or_imprecise_dtypes=True), [o], [])
+        else:
+            emit("g", lambda: g.iota(o[0], pat, base, cm), [o], [])
+
+    def keep(o, pat, op, base, cm):
+        i = R("one", 0, pat[0][1] * pat[1][1])
+        emit("g", lambda: g.affine_select(o[0], i[0], pat, op, 0.0, base, cm), [o], [i])
+
+    def load(q, o, src, sem, codes=False):
+        emit(q, lambda: Q[q].dma_start(o[0].bitcast(dt.uint8) if codes else o[0], src), [o], [], sem)
+
+    peer = [T.cores[rank ^ 1], T.cores[rank ^ 2]]
+
+    def send(src, k, t):
+        i = R(src)
+        deps("g", [], i[1])
+        if topo.may_write(core, peer[t]):
+            dst, land, far = peer[t], "r%s%d" % (k, t), "a%s%d" % (k, t)
+        else:
+            dst, land, far = relay_of(core, peer[t], k, topo), "m" + k, "m%s_" % k
+        rid, pid = topo.addr(dst, core)
+        a, b = T[land][:], i[0]
+        if k == "q":
+            a, b = a.bitcast(dt.uint8), b.bitcast(dt.uint8)
+        g.remote_dma(a, b, T.sem[far], T.sem["loc"], pid, rid, topo.mask(core, dst))
+        count["loc"] = count.get("loc", 0) + len(topo.engines(core, dst))
+
+    def store(q, o, i, src):
+        deps(q, [], src[1])
+        Q[q].dma_start(o, i).then_inc(T.sem["out"], 16)
+        count["out"] = count.get("out", 0) + 16
+
+    def pick(o, c, x, n):
+        scan(R(o[0], o[1], o[1] + n), R(c, 0, n), x, -B, ALU.add, ALU.min)
+
+    load("s", R("ut"), T.u[:], "lu")
+    load("a", R("xt", 0, 640), T.x[:, 0:640], "lx0")
+    load("s", R("xt", 640, 1920), T.x[:, 640:1920], "lx1")
+    load("s", R("wq"), T.wc[:], "lw_", True)
+    load("s", R("wp"), T.ws[:], "lp_")
+    load("s", R("vt"), T.v[:], "lv")
+    for t in range(2):
+        for k in "qsl":
+            last = peer[t] if topo.may_write(peer[t], core) else relay_of(peer[t], core, k, topo)
+            sem = "a%s%d" % (k, t)
+            count[sem] = len(topo.engines(last, core))
+            note("x", R("r%s%d" % (k, t))[1], [], (sem, count[sem]))
+
+    iota(R("ii", 16, 17), [[0, 1]], 0, 1, False)
+    iota(R("jh"), [[1, 35], [0, 4]], -3, 0)
+    iota(R("iof", 0, 128), [[1, 128]], 0, 0)
+    iota(R("ii", 0, 16), [[1, 16]], 128, -1, False)
+    iota(R("iof", 128, 608), [[1, 480]], 128, 0)
+    ms(R("one"), 1.0)
+    for k in range(2):
+        keep(R("r4", 320 * k, 320 * k + 320), [[0, 80], [1, 4]], ALU.not_equal, 0, 0)
+    iota(R("iof", 608, NID), [[1, NID - 608]], 608, 0)
+    for k in range(2):
+        keep(R("r16", 496 * k, 496 * k + 496), [[0, 31], [1, 16]], ALU.not_equal, 0, 0)
+    iota(R("uc"), [[16, 32]], 256, 1)
+    iota(R("ii", 24, 32), [[16, 8]], 7, 0, False)
+    iota(R("jg"), [[4, 8], [0, 16]], 0, 0)
+    iota(R("wb0"), [[0, 512]], 0, 0)
+    iota(R("bt"), [[0, 896]], 0, 0)
+    for b in range(4):
+        keep(R("et", 512 * b, 512 * b + 512), [[0, 1], [1, 512]], ALU.is_equal, -b, -4)
+    p_ = R("ii", 16, 17)
+    ts(R("ij", 24, 25), p_, 15, ALU.bitwise_and)
+    ts(R("ij", 25, 26), p_, 3, ALU.bitwise_and)
+    ts(R("ij", 26, 27), p_, 2, ALU.logical_shift_right, 28, ALU.bitwise_and)
+    ts(R("ij", 27, 28), p_, 2, ALU.logical_shift_right, 3, ALU.bitwise_and)
+    ts(R("ij", 28, 29), p_, 4, ALU.logical_shift_right, 1, ALU.bitwise_and)
+    cp(R("col", PI, GM + 1), R("ij", 24, 29))
+    act(col(POW), col(PI), ACT.Exp, math.log(2.0))
+    lin(QOFF, PQ, -16.0, 48.0)
+    ms(R("bt0", 160, 512), 0.0)
+    ms(R("tab", 128, 256), 0.0)
+    ms(R("tab", 512, 768), 0.0)
+    ms(R("ys"), -512.0)
+    ts(col(TCOL), col(PI), 48.0, ALU.add)
+    ts(col(FIX16), col(PI), 14.5, ALU.is_lt, B, ALU.mult)
+    ts(col(FIX4), col(H4), 2.5, ALU.is_lt, B, ALU.mult)
+    cp(R("yy", 0, 4), R("ys"))
+    ts(R("tab", 0, 128), R("iof", 0, 128), col(TCOL), ALU.is_equal, -1.0, ALU.mult)
+    ts(R("ij", 0, 16), R("ii", 0, 16), 15, ALU.bitwise_and)
+    ts(R("ii", 18, 22), R("iof", 4, 8), col(H4), ALU.subtract)
+    ts(R("ii", 22, 24), R("iof", 2, 4), col(GM), ALU.subtract)
+    ts(col(TMP), col(PI), 7.0, ALU.is_equal, 128.0, ALU.mult)
+    ts(R("ij", 16, 20), R("ii", 18, 22), 3, ALU.bitwise_and)
+    ts(R("ij", 20, 22), R("ii", 22, 24), 1, ALU.bitwise_and)
+    ts(col(WT0), col(PI), 5.5, ALU.is_lt, col(POW), ALU.mult)
+    for t in range(4):
+        ts(R("wc0", t, 512, 4), R("jh", 12 - 4 * t, 140 - 4 * t), col(G4), ALU.is_equal, col(WT0), ALU.mult)
+    for r in (2, 3):
+        act(R("tab", 128 * r, 128 * r + 128), R("tab", 0, 128), ACT.Copy)
+    act(R("ids", 128, 608), R("iof", 128, 608), ACT.Copy)
+    act(R("kfr"), R("iof", 0, 224), ACT.Copy, 1.0 / 256)
+    lin(NFG, GM, B, -B)
+    lin(DFX, FIX16, 1.0, -1.0)
+    lin(TM2, FIX4, 4.0, col(PQ))
+    lin(O16, FIX16, 1.0, 8.0)
+    lin(IFX, FIX4, 1.0, col(QOFF))
+    lin(C1, TM2, 1.0, -4.0 * OFF)
+    lin(F256, FIX4, 256.0, 0.0)
+    lin(KOF, PQ, 224.0, 0.0)
+    S7, CD = 512, 1024
+    quant("qu", "su", 0, 128, R("ut"))
+    quant("qx", "sx", 0, 160, R("xt", 0, 640))
+    mm(R("ps", 0, 160), "qu", "su", 0, "qx", "sx", 0, 160)
+    quant("qwc", "swc", 0, 128, R("wc0"))
+    ts(R("tm1", 0, 22), R("ij", 0, 22), 0.0, ALU.is_equal, 4 * B, ALU.mult)
+    ts(R("bt0", 0, 160), R("ps", 0, 160), 0.0, ALU.is_gt)
+    quant("qb", "sbb", 0, 128, R("bt0"))
+    mm(R("ps", CD, CD + 128), "qwc", "swc", 0, "qb", "sbb", 0, 128)
+    ts(R("tm2", 0, 22), R("ij", 0, 22), 1.0, ALU.is_equal, -B, ALU.mult)
+    tt(col(WT), col(WT0), col(TMP), ALU.add)
+    ms(R("ptab", 0, 8), 0.0)
+    ts(R("oe", 0, 40), R("ps", CD, CD + 40), col(QOFF), ALU.add)
+
+    def marks(offs, s0, s1, both=False):
+        act(R("e", 4 * s0, 4 * s1), ind(R("tab"), offs), ACT.Copy)
+        if both:
+            act(R("d0", 4 * s0, 4 * s1), R("e", 4 * s0, 4 * s1), ACT.Identity, 5.0, 1.0)
+
+    def shared_marks(offs, s0):
+        a = 4 * s0
+        ts(R("d0", a, a + 192), ind(R("tab"), R(offs, 0, 12)), 5.0, ALU.mult, 1.0, ALU.add)
+        act(R("e", a + 192, a + 384), ind(R("tab"), R(offs, 12, 24)), ACT.Copy)
+        ts(R("d0", a + 192, a + 384), R("e", a + 192, a + 384), 5.0, ALU.mult, 1.0, ALU.add)
+        act(R("e", a, a + 192), R("d0", a, a + 192), ACT.Identity, 0.2, -0.2)
+
+    marks(R("oe", 0, 40), 0, 160)
+    quant("qx", "sx", 160, 480, R("xt", 640, 1920))
+    mm(R("ps", 512, 832), "qu", "su", 0, "qx", "sx", 160, 480)
+    tt(R("pat", 0, 22), R("tm1", 0, 22), R("tm2", 0, 22), ALU.add)
+    ms(R("pool", 0, 16), 0.0)
+    ts(R("q4", 0, 64), R("one", 0, 64), 0.0, ALU.mult)
+    ts(R("q4", 64 + 1920, 64 + 1984), R("one", 0, 64), 0.0, ALU.mult)
+    ts(R("bt0", 160, 480), R("ps", 512, 832), 0.0, ALU.is_gt)
+    quant("qb", "sbb", 128, 256, R("bt0"))
+    mm(R("ps", 1536, 1664), "qwc", "swc", 0, "qb", "sbb", 128, 256)
+    ts(R("d0", 0, 640), R("e", 0, 640), 5.0, ALU.mult, 1.0, ALU.add)
+    ts(R("oe", 40, 120), R("ps", 1576, 1656), col(QOFF), ALU.add)
+    for k in range(2):
+        act(R("c2", k, 64, 2), R("one", 0, 32), ACT.Copy, R("pat", 20 + k, 21 + k))
+    for k in range(4):
+        act(R("c4", k, 224, 4), R("one", 0, 56), ACT.Copy, R("pat", 16 + k, 17 + k))
+    marks(R("oe", 40, 80), 160, 320)
+    marks(R("oe", 80, 120), 320, 480)
+    act(R("win", 0, 256), R("one", 0, 256), ACT.Copy, FILL)
+    for k in range(16):
+        act(R("c16", k, 496, 16), R("one", 0, 31), ACT.Copy, R("pat", k, k + 1))
+    act(R("pool", 16, 16 + 960), R("xt", 0, 960), ACT.Copy, 0.5)
+    lin(G1, GM, 64.0, col(C1))
+    lin(AOF, IFX, 1.0, 128.0 - 0.44)
+    for t in range(3):
+        lin(C20 + t, G1, 1.0, 4.0 * (BASE[t] - 16))
+
+    def more_constants():
+        act(R("pool", 16 + 960, 16 + 1920), R("xt", 960, 1920), ACT.Copy, 0.5)
+        act(R("ids", 608, NID), R("iof", 608, NID), ACT.Copy)
+
+    def rows(t, s0, s1, made=False):
+        a, b = 4 * s0, 4 * s1
+        if not made:
+            ts(R("d0", a, b), R("e", a, b), 5.0, ALU.mult, 1.0, ALU.add)
+        for q in range(4):
+            scan(R("yy", 4 + a + q, 4 + b, 4), R("d0", a + q, b, 4), R("ids", BASE[t] + s0, BASE[t] + s1), R("ys", q, q + 1), ALU.mult, ALU.min)
+        scan(R("vv", a, b), R("yy", a, b), R("e", a, b), 0.0, ALU.max, ALU.mult)
+        cp(R("ys"), R("yy", b, b + 4))
+        scan(R("q4", 64 + a, 64 + b), R("r4", 0, b - a), R("vv", a, b), 0.0, ALU.mult, ALU.min)
+
+    def number(s0, s1, last, then=None):
+        n1 = (s1 - s0) // 32
+        n2 = n1 + (1 if last else 0)
+        m0, m = s0 // 16, n1 + n2
+        tr(R("tt", 0, 32 * n2), R("q4", 3 + 4 * s0, 4 * s0 + 128 * n2, 4))
+        tr(R("tt", 32 * n2, 32 * m), R("q4", 67 + 4 * s0, 64 + 4 * s1, 4))
+        scan(R("rr", 0, 32 * m), R("r16", 0, 32 * m), R("tt", 0, 32 * m), 0.0, ALU.mult, ALU.min)
+        pick(("sel", 0), "c2", R("rr", 15, 32 * m, 16), 2 * m)
+        ts(R("pw", m0, m0 + m, 2), R("sel", 1, 2 * n2, 2), -1.0, ALU.mult, col(NFG), ALU.add)
+        ts(R("pw", m0 + 1, m0 + m, 2), R("sel", 2 * n2 + 1, 2 * m, 2), -1.0, ALU.mult, col(NFG), ALU.add)
+        o, a, b = R("pw", m0, m0 + m), 16 * m0, 16 * (m0 + m)
+        h = m0 + (m + 2) // 4 * 2
+        act(R("fb", 16 * h, b), ind(R("iof"), R("pw", h, m0 + m)), ACT.Sign)
+        act(R("ptab", 8 + a, 8 + b), ind(R("iof"), o), ACT.Copy)
+        if then is not None:
+            then()
+        ts(R("fb", a, 16 * h), ind(R("iof"), R("pw", m0, h)), 0.0, ALU.is_gt)
+        ts(R("nf", m0, m0 + m), o, 0.0, ALU.is_equal)
+        scan(R("cum", a, b), R("one", 0, b - a), R("fb", a, b), R("cs", 0, 1) if s0 else 0.0, ALU.mult, ALU.add)
+        tt(R("zz", m0, m0 + m), R("nf", m0, m0 + m), R("uc", m0, m0 + m), ALU.mult)
+        pick(("cw", a), "c16", R("cum", a, b), b - a)
+        if not last:
+            cp(R("cs", 0, 1), R("cum", b - 1, b))
+        tt(R("ds", m0, m0 + m), R("cw", a + 15, b, 16), R("zz", m0, m0 + m), ALU.add)
+        ts(R("od", m0, m0 + m), R("ds", m0, m0 + m), col(DFX), ALU.add)
+        scat(R("win"), R("od", m0, m0 + m), R("iof", a, b))
+
+    def fire(t, n, cut, during):
+        P = PR[t]
+        top = 4 * (BASE[t] + n - OFF)
+        w = R("win", 0, P)
+        pick(("w4", 0), "c4", w, P)
+        ts(R("o2", 0, P // 4), R("w4", 3, P, 4), 4.0, ALU.mult, col(C20 + t), ALU.add)
+        h = 32 if cut else P // 8
+        for a, b in ((0, h), (h, P // 4)):
+            act(R("two", 16 * a, 16 * b), ind(R("pool", 0, top), R("o2", a, b)), ACT.Copy)
+        during()
+        pick(("w16", 0), "c16", w, P)
+        ts(R("o16", 0, P // 16), R("w16", 15, P, 16), col(O16), ALU.add)
+        cp(R("g1", 0, P), ind(R("ptab", 0, 8 + n + 16), R("o16", 0, P // 16)))
+        pick(("w1", 0), "c4", R("g1", 0, P), P)
+        ts(R("o1", 0, P // 4), R("w1", 3, P, 4), 4.0, ALU.mult, col(C1), ALU.add)
+        for a, b in ((0, h), (h, P // 4)):
+            tt(R("bb", 16 * a, 16 * b), ind(R("pool", 0, top), R("o1", a, b)), R("two", 16 * a, 16 * b), ALU.add)
+            if cut:
+                k = 128 if a else 0
+                quant("qbb", "sbq", k, k + 128, R("bb", 4 * (4 * b - 128), 16 * b))
+                for c in range(4):
+                    mm(R("ps" if a else "pr", 512 * c, 512 * c + 128), "wq", "wp", 128 * c, "qbb", "sbq", k, k + 128)
+                if not a:
+                    for c in range(4):
+                        act(R("hh", c, 512, 4), R("pr", 512 * c, 512 * c + 128), ACT.Relu, 0.03125)
+        if not cut:
+            quant("qbb", "sbq", 0, P, R("bb", 0, 4 * P))
+            for c in range(4):
+                mm(R("pr", 512 * c, 512 * c + P), "wq", "wp", 128 * c, "qbb", "sbq", 0, P)
+
+    rows(0, 0, 160, True)
+    rows(0, 160, 320)
+    rows(0, 320, 480)
+    cp(R("o7"), R("ii", 24, 32))
+    number(0, 480, True, more_constants)
+    n = C
+    for t in range(2):
+        P = PR[t]
+        qh, sh, ls, rl = "qh%d" % t, "sh%d" % t, "ls%d" % t, "rl%d" % t
+        w = R("win", 0, P)
+
+        def limits():
+            act(R("thr", 0, P), w, ACT.Relu, -1e26)
+            act(R("nh", 0, P), w, ACT.Relu, -0.5)
+            if t == 0:
+                a, b, o = R("su7"), R("su"), R("o7")
+                emit("a", lambda: g.scalar.activation(a[0], b[0].indirect(o[0]), ACT.Copy), [a], [b, o])
+
+        fire(t, n, True, limits)
+        n = P + L
+        if t == 0:
+            a, b, o = R("qu7"), R("qu"), R("o7")
+            emit("v", lambda: g.vector.tensor_copy(a[0].bitcast(dt.uint32), b[0].bitcast(dt.uint32).indirect(o[0])), [a], [b, o])
+        else:
+            quant("qv", "sv", 0, 128, R("vt"))
+            ms(R("tl", 256, 512), 0.0)
+        quant(qh, sh, 0, 128, R("hh", 0, 512))
+        lo = 256 - P
+        for b in (0, 2):
+            ts(R("hh", 512 + b, 4 * P, 4), R("ps", 512 * b + lo, 512 * b + 128), 0.0, ALU.max, 0.03125, ALU.mult)
+            act(R("hh", 513 + b, 4 * P, 4), R("ps", 512 * b + 512 + lo, 512 * b + 640), ACT.Relu, 0.03125)
+            if t == 0:
+                if b == 0:
+                    ts(R("wb0", 0, 512, 4), R("jg"), col(G4), ALU.is_equal, col(WT), ALU.mult)
+                else:
+                    quant("qwb", "swb", 0, 128, R("wb0"))
+        quant(qh, sh, P - 128, P, R("hh", 4 * (P - 128), 4 * P))
+        mm(R("ps", S7, S7 + P), "qu7", "su7", 0, qh, sh, 0, P)
+        mm(R("ps", 0, P), "qu", "su", 0, qh, sh, 0, P)
+        direct = topo.may_write(core, peer[t])
+        send(qh, "q", t)
+        send(sh, "s", t)
+        nb = BASE[t + 1]
+        act(R("lwin", 0, L), R("one", 0, L), ACT.Copy, 0.0)
+        act(R("yy", 0, 4), R("ys"), ACT.Copy)
+        act(R("q4", 64 + 4 * n, 128 + 4 * n), R("one", 0, 64), ACT.Copy, 0.0)
+        if t == 0:
+            quant("qe", "se", 0, 256, R("et", 0, 1024))
+        else:
+            ms(R("tl", 640, 1152), 0.0)
+            ms(R("occb", NA + PR[2], 288), 0.0)
+        act(R("sg", 0, P), R("ps", 0, P), ACT.Sign)
+        act(R("bt", 0, 4 * P, 4), R("sg", 0, P), ACT.Relu)
+        act(R("pool", 4 * (nb - OFF), 4 * (nb - OFF + P)), R("hh", 0, 4 * P), ACT.Copy, 0.5)
+        m = P // 16
+        tt(R("nc", 0, P), R("ps", S7, S7 + P), R("thr", 0, P), ALU.is_le)
+        scan(R("nc", P, 2 * P), R("one", 0, P), R("nc", 0, P), 0.0, ALU.add, ALU.subtract)
+        pick(("ncw", 0), "c16", R("nc", 0, 2 * P), 2 * P)
+        ts(R("t1", 0, P), R("nc", P, 2 * P), L + 0.5, ALU.is_gt, 256.0, ALU.mult)
+        ts(R("la", 0, m), R("ncw", 15, P, 16), col(FIX16), ALU.add)
+        quant("qb", "sbb", 0, P, R("bt", 0, 4 * P))
+        mm(R("ps", CD, CD + P), "qwb", "swb", 0, "qb", "sbb", 0, P)
+        tt(R("la", 16, 16 + m), R("la", 0, m), R("uc", 0, m), ALU.mult)
+        scan(R("reg", 0, P), R("t1", 0, P), R("nh", 0, P), 0.0, ALU.max, ALU.max)
+        tt(R("la", 32, 32 + m), R("ncw", P + 15, 2 * P, 16), R("la", 16, 16 + m), ALU.add)
+        ts(R("ol", 0, m), R("la", 32, 32 + m), col(DFX), ALU.add)
+
+        def staying():
+            tt(R("idx", 0, P), R("ps", CD, CD + P), R("reg", 0, P), ALU.add)
+            pick(("iw", 0), "c4", R("idx", 0, P), P)
+            if direct:
+                tt(R("val", 0, P), R("ps", CD, CD + P), R("kfr", 0, P), ALU.add)
+            ts(R("oe", 0, P // 4), R("iw", 3, P, 4), col(IFX), ALU.add)
+            if direct:
+                marks(R("oe", 0, 24), 0, 96, True)
+            else:
+                shared_marks("oe", 0)
+            marks(R("oe", 24, P // 4), 96, P, direct)
+
+        if direct:
+            staying()
+        else:
+            tt(R("val", 0, P), R("ps", CD, CD + P), R("kfr", 0, P), ALU.add)
+        scat(R("lwin"), R("ol", 0, m), R("val", 0, P))
+        pick(("lw", 0), "c4", R("lwin", 0, L), L)
+        ts(R("li", 0, 24), R("lw", 3, L, 4), 256.0, ALU.mult, col(F256), ALU.add)
+        ts(R(ls, 0, 24), R("lw", 3, L, 4), col(AOF), ALU.add)
+        ts(R("li", 24, 48), R("li", 0, 24), 255, ALU.bitwise_and)
+        ts(R(ls, 24, 48), R("li", 24, 48), col(KOF), ALU.add)
+        send(ls, "l", t)
+        if not direct:
+            staying()
+        act(R("win", 0, 256), R("one", 0, 256), ACT.Copy, FILL)
+        rows(t + 1, 0, 96, True)
+        if t == 0:
+            quant("qe", "se", 256, 512, R("et", 1024, 2048))
+        rows(t + 1, 96, P, direct)
+        if not direct:
+            number(0, P, False)
+
+        def unpacked():
+            for b in range(4):
+                mm(R("pr", 512 * b, 512 * b + P), "qe", "se", 128 * b, "rq%d" % t, "rs%d" % t, 0, P)
+                act(R("dst", 224 * b, 224 * b + P), R("pr", 512 * b, 512 * b + P), ACT.Copy, 0.5)
+            act(R("pool", 4 * (nb - OFF + P), 4 * (nb - OFF + n)), ind(R("dst"), R(rl, 24, 48)), ACT.Copy)
+
+        shared_marks(rl, P)
+        if direct:
+            unpacked()
+        rows(t + 1, P, n, True)
+        number(0 if direct else P, n, True, None if direct else unpacked)
+    P = PR[2]
+    w = R("win", 0, P)
+
+    def results():
+        for k in range(4):
+            ts(R("ot", 4 * k, 4 * k + 4), R("ys"), 4.0, ALU.mult, float(k - 4 * OFF), ALU.add)
+        cp(R("ot", 16, 20), R("ys"))
+        for k in range(4):
+            act(R("tl", k, 4 * NA, 4), ind(R("pool"), R("ot", 4 * k, 4 * k + 4)), ACT.Copy, 2.0)
+        act(R("thr", 0, P), w, ACT.Relu, 1e26, 5.12e28)
+        act(R("occb", 0, NA), ind(R("iof"), R("ot", 16, 20)), ACT.Sign)
+        act(R("occb", NA, NA + P), w, ACT.Sign, 1.0, -FILL)
+        store("s", T.occ[:], T.occb[0:128:16, :], R("occb"))
+
+    fire(2, n, False, results)
+    quant("qt", "st", 0, 128, R("tl", 0, 512))
+    quant("qt", "st", 160, 288, R("tl", 640, 1152))
+    mm(R("ps", 512, 640), "qv", "sv", 0, "qt", "st", 0, 128)
+    mm(R("ps", 1024, 1152), "qv", "sv", 0, "qt", "st", 160, 288)
+    for a in (0, NA + P):
+        store("s", T.oc[:, 4 * a:4 * a + 256], T.qt[:, a:a + 64].bitcast(dt.uint8), R("qt", a, a + 64))
+    for b in range(4):
+        tt(R("hm", P * b, P * b + P), R("pr", 512 * b, 512 * b + P), R("thr", 0, P), ALU.min)
+        act(R("tl", 4 * NA + b, 4 * (NA + P), 4), R("hm", P * b, P * b + P), ACT.Relu, 0.03125)
+    cp(R("yb", 0, NA), R("ps", 512, 512 + NA))
+    cp(R("yb", NA + P, 288), R("ps", 1088, 1152))
+    for a in (0, NA + P):
+        store("s", T.y[:, a:a + 64], T.yb[:, a:a + 64], R("yb", a, a + 64))
+    quant("qt", "st", NA, NA + P, R("tl", 4 * NA, 4 * (NA + P)))
+    mm(R("ps", 0, P), "qv", "sv", 0, "qt", "st", NA, NA + P)
+    store("s", T.oc[:, 4 * NA:4 * (NA + P)], T.qt[:, NA:NA + P].bitcast(dt.uint8), R("qt"))
+    for k in range(4):
+        store("a", T.osc[4 * k:4 * k + 4, :], T.st[32 * k:32 * k + 4, :], R("st"))
+    cp(R("yb", NA, NA + P), R("ps", 0, P))
+    store("s", T.y[:, NA:NA + P], T.yb[:, NA:NA + P], R("yb"))
+    for s in count:
+        wait("s", (s, count[s]))

@@ -11,7 +11,12 @@ BASE = [128, 608, 928]
 OFF = 124
 NID = 1216
 B = 2048.0
-FILL = -1024.0
+FILL = -4096.0
+HOP, DMA = 2800.0, 2000.0
+CASES = ((90.0, 0.8), (130.0, 1.0), (180.0, 1.3))
+TRIES = [2500, 20000]
+LOADS = 6
+ORDER = []
 
 
 def sb(n, d):
@@ -24,20 +29,21 @@ SCRATCH = {
     "qv": sb(128, Q4), "sv": sb(128, U8), "wq": sb(512, Q4), "wp": sb(512, U8),
     "pool": sb(4 * (NID - OFF), BF), "bt0": sb(512, BF), "bt": sb(896, BF), "sg": sb(224, BF), "qb": sb(256, Q4), "sbb": sb(256, U8),
     "ii": sb(32, I32), "ij": sb(32, I32), "col": sb(32, F32), "iof": sb(NID, F32), "ids": sb(NID, F16), "kfr": sb(224, F32),
+    "pfr": sb(NID, F32), "pos4": sb(496, F32),
     "jg": sb(128, F32), "jh": sb(140, F32), "tm1": sb(24, F32), "tm2": sb(24, F32), "pat": sb(24, F32),
-    "c16": sb(496, BF), "c4": sb(224, BF), "c2": sb(64, BF), "r16": sb(992, BF), "r4": sb(640, BF),
+    "c16": sb(496, BF), "c4": sb(224, BF), "c4x": sb(224, BF), "c2": sb(64, BF), "r16": sb(992, BF), "r4": sb(640, BF),
     "one": sb(512, BF), "tab": sb(768, BF), "uc": sb(32, F32), "o7": sb(8, U16),
     "wc0": sb(512, BF), "wb0": sb(512, BF), "et": sb(2048, BF),
     "qwc": sb(128, Q4), "swc": sb(128, U8), "qwb": sb(128, Q4), "swb": sb(128, U8), "qe": sb(512, Q4), "se": sb(512, U8),
-    "oe": sb(120, U16), "e": sb(1920, BF), "d0": sb(1920, BF), "yy": sb(1924, F16), "ys": sb(4, F32), "vv": sb(1920, F16),
+    "oe": sb(120, U16), "e": sb(1920, BF), "d0": sb(1920, BF), "yy": sb(1924, F16), "ys": sb(12, F32), "vv": sb(1920, F16),
     "q4": sb(64 + 1984, F16), "tt": sb(992, F16), "rr": sb(992, F16), "sel": sb(64, F32), "pw": sb(32, U16),
     "fb": sb(496, BF), "cum": sb(496, F16), "cs": sb(2, F32), "cw": sb(496, F16), "nf": sb(32, F32), "zz": sb(32, F32), "ds": sb(32, F32),
-    "od": sb(32, U16), "win": sb(1152, F32), "ptab": sb(504, F32),
-    "w4": sb(224, F32), "w16": sb(224, F32), "o2": sb(56, U16), "o16": sb(14, U16), "g1": sb(224, F16), "w1": sb(224, F16), "o1": sb(56, U16),
+    "od": sb(32, U16), "win": sb(1152, F32), "pk": sb(496, F32),
+    "w4": sb(224, F32), "wi": sb(112, I32), "o2": sb(56, U16), "o1": sb(56, U16),
     "two": sb(896, BF), "bb": sb(896, BF), "qbb": sb(256, Q4), "sbq": sb(256, U8), "hh": sb(896, BF),
     "qh0": sb(224, Q4), "sh0": sb(224, U8), "qh1": sb(192, Q4), "sh1": sb(192, U8),
     "thr": sb(224, F32), "nh": sb(224, BF), "nc": sb(448, F16), "ncw": sb(448, F16), "la": sb(48, F32),
-    "ol": sb(14, U16), "val": sb(224, F32), "lwin": sb(832, F32), "lw": sb(96, F32), "li": sb(48, I32),
+    "ol": sb(14, U16), "val": sb(224, F32), "lwin": sb(832, F32), "lw": sb(96, F32), "li": sb(48, I32), "ko": sb(24, U16),
     "ls0": sb(48, U16), "ls1": sb(48, U16), "t1": sb(224, F16), "reg": sb(224, F16), "idx": sb(224, F16), "iw": sb(224, F16),
     "rq0": sb(224, Q4), "rs0": sb(224, U8), "rl0": sb(48, U16), "rq1": sb(192, Q4), "rs1": sb(192, U8), "rl1": sb(48, U16),
     "mq": sb(192, Q4), "ms": sb(192, U8), "ml": sb(48, U16), "dst": sb(896, BF),
@@ -46,7 +52,7 @@ SCRATCH = {
 }
 SEMAPHORES = ["sv_", "sa_", "sp_", "sg_", "lu", "lx0", "lx1", "lw_", "lp_", "lv", "out",
               "aq0", "as0", "al0", "aq1", "as1", "al1", "mq_", "ms_", "ml_", "loc"]
-(PI, PQ, G4, H4, GM, QOFF, FIX16, FIX4, NFG, TCOL, C1, C20, C21, C22, O16, DFX, WT, WT0, G1, AOF, KOF, IFX, F256, TMP, POW, TM2) = range(26)
+(PI, PQ, G4, H4, GM, QOFF, FIX16, FIX4, NFG, TCOL, C1, C20, C21, C22, C1X, DFX, WT, WT0, G1, AOF, KOF, IFX, F256, TMP, POW, TM2, FXX) = range(27)
 
 
 def relay_of(src, dst, k, topo):
@@ -70,6 +76,117 @@ def relay_program(g, core, T, topo, src, dst):
         g.wait_ge(T.sem["loc"], n)
 
 
+def arrange(ops):
+    n = len(ops)
+    q, pre, cost, lat = ([o[k] for o in ops] for k in ("q", "pre", "cost", "lat"))
+    after = [[] for _ in ops]
+    for i in range(n):
+        for p in pre[i]:
+            after[p].append(i)
+
+    def span(order, gap, hop):
+        free, done = dict.fromkeys("vapgsx", 0.0), [0.0] * n
+        for i in order:
+            t = free[q[i]]
+            for p in pre[i]:
+                if done[p] + gap > t:
+                    t = done[p] + gap
+            if q[i] == "x":
+                done[i] = t + lat[i] * hop
+            else:
+                free[q[i]] = t + cost[i]
+                done[i] = t + cost[i] + lat[i]
+        return max(done)
+
+    def score(order):
+        return sum(span(order, gap, hop) for gap, hop in CASES)
+
+    def greedy(extra, gap=CASES[1][0]):
+        tail = [0.0] * n
+        for i in range(n - 1, -1, -1):
+            tail[i] = cost[i] + lat[i] + extra[i] + max([gap + tail[s] for s in after[i]] + [0.0])
+        left = [len(p) for p in pre]
+        ready = {i: 0.0 for i in range(n) if not left[i]}
+        free, done, order = dict.fromkeys("vapgsx", 0.0), [0.0] * n, []
+        while ready:
+            a = min(ready, key=lambda i: (max(ready[i], free[q[i]]), -tail[i]))
+            ta = max(ready[a], free[q[a]])
+            for b in ready:
+                if b != a and q[b] == q[a] != "x":
+                    tb = max(ready[b], free[q[b]])
+                    if max(tb + tail[b], max(tb + cost[b], ta) + tail[a]) < max(ta + tail[a], max(ta + cost[a], tb) + tail[b]):
+                        a, ta = b, tb
+            del ready[a]
+            order.append(a)
+            if q[a] != "x":
+                free[q[a]] = ta + cost[a]
+            done[a] = ta + cost[a] + lat[a]
+            for s in after[a]:
+                left[s] -= 1
+                if not left[s]:
+                    ready[s] = max(done[p] for p in pre[s]) + gap
+        return order
+
+    seed = [12345]
+
+    def draw(k):
+        seed[0] = (seed[0] * 6364136223846793005 + 1442695040888963407) % (1 << 64)
+        return (seed[0] >> 33) % k
+
+    extra = [0.0] * n
+    order = greedy(extra)
+    best = score(order)
+    for _ in range(TRIES[0]):
+        e = list(extra)
+        for _ in range(1 + draw(3)):
+            e[draw(n)] += draw(2801) - 1400.0
+        o = greedy(e)
+        s = score(o)
+        if s <= best:
+            best, extra, order = s, e, o
+    for _ in range(TRIES[1]):
+        k = draw(n)
+        i = order[k]
+        lo = max([order.index(p) for p in pre[i]] + [-1]) + 1
+        hi = min([order.index(s) for s in after[i]] + [n]) - 1
+        if hi > lo:
+            o = order[:k] + order[k + 1:]
+            o.insert(lo + draw(hi - lo + 1), i)
+            s = score(o)
+            if s <= best:
+                best, order = s, o
+    return list(range(LOADS)) + [i for i in order if i >= LOADS]
+
+
+def issue(ops, Q, T):
+    if not ORDER:
+        ORDER.extend(arrange(ops))
+    count, tok = {}, {}
+    waited = {k: {} for k in Q}
+
+    def wait(q, s, v):
+        if waited[q].get(s, 0) < v:
+            Q[q].wait_ge(T.sem[s], v)
+            waited[q][s] = v
+
+    for a in ORDER:
+        o = ops[a]
+        if o["q"] != "x":
+            need = {}
+            for p in o["pre"]:
+                if tok[p] is not None:
+                    need[tok[p][0]] = max(need.get(tok[p][0], 0), tok[p][1])
+            for s in need:
+                wait(o["q"], s, need[s])
+            call = o["make"]()
+            if o["sem"] != "loc":
+                call.then_inc(T.sem[o["sem"]], o["n"])
+        count[o["sem"]] = count.get(o["sem"], 0) + o["n"]
+        tok[a] = None if o["sem"] in ("loc", "out") else (o["sem"], count[o["sem"]])
+    for s in count:
+        wait("s", s, count[s])
+
+
 def rank_program(g, core, T, topo):
     rank = T.rank_of(core)
     if rank is None:
@@ -80,119 +197,118 @@ def rank_program(g, core, T, topo):
         return
     Q = {"v": g.vector, "a": g.scalar, "p": g.tensor, "g": g, "s": g.sync}
     SEM = {"v": "sv_", "a": "sa_", "p": "sp_", "g": "sg_"}
-    count = {}
-    waited = {k: {} for k in Q}
+    ops = []
     log = {}
+    own = []
 
     def R(name, lo=0, hi=None, step=1):
         n = SCRATCH[name][1][1]
         hi = n if hi is None else hi
         ap = T[name][:, lo:hi] if step == 1 else T[name][:, lo:hi:step]
         if SCRATCH[name][0] == "psum":
-            return (ap, [(name, lo // 512 * 512, lo // 512 * 512 + 512, 1, True)])
-        return (ap, [(name, lo, hi, step, False)])
+            return (ap, [(name, lo // 512 * 512, lo // 512 * 512 + 512, 1, True)], hi - lo)
+        return (ap, [(name, lo, hi, step, False)], len(range(lo, hi, step)))
 
     def col(c):
         return R("col", c, c + 1)
 
     def ind(w, o):
-        return (w[0].indirect(o[0]), w[1] + o[1])
-
-    def wait(q, tok):
-        if waited[q].get(tok[0], 0) < tok[1]:
-            Q[q].wait_ge(T.sem[tok[0]], tok[1])
-            waited[q][tok[0]] = tok[1]
+        return (w[0].indirect(o[0]), w[1] + o[1], 16 * o[2])
 
     def meet(a, b):
         if a[1] >= b[2] or b[1] >= a[2]:
             return False
         return not (a[3] == b[3] and a[3] > 1 and (a[1] - b[1]) % a[3] != 0)
 
-    def deps(q, outs, ins):
-        need = {}
-        for acc, wr in [(a, True) for a in outs] + [(a, False) for a in ins]:
-            for old, owr, tok, oq in log.get(acc[0], []):
-                if (wr or owr or (acc[4] and oq != q)) and meet(acc, old):
-                    need[tok[0]] = max(need.get(tok[0], 0), tok[1])
-        for s in need:
-            wait(q, (s, need[s]))
+    def emit(q, make, outs, ins, cost, sem=None, n=1, lat=0.0, pre=()):
+        acc = [(a, True) for o in outs for a in o[1]] + [(a, False) for o in ins if isinstance(o, tuple) for a in o[1]]
+        pre = set(pre)
+        for a, wr in acc:
+            for old, owr, i, oq in log.get(a[0], []):
+                if (wr or owr or (a[4] and oq != q)) and meet(a, old):
+                    pre.add(i)
+        for a, wr in acc:
+            log.setdefault(a[0], []).append((a, wr, len(ops), q))
+        ops.append({"q": q, "make": make, "pre": sorted(pre), "cost": cost, "lat": lat, "sem": sem or SEM[q], "n": n})
+        return len(ops) - 1
 
-    def note(q, outs, ins, tok):
-        for acc, wr in [(a, True) for a in outs] + [(a, False) for a in ins]:
-            log.setdefault(acc[0], []).append((acc, wr, tok, q))
-
-    def emit(q, make, outs, ins, sem=None):
-        outs = [a for o in outs for a in o[1]]
-        ins = [a for o in ins if isinstance(o, tuple) for a in o[1]]
-        deps(q, outs, ins)
-        s, n = (SEM[q], 1) if sem is None else (sem, 16)
-        make().then_inc(T.sem[s], n)
-        count[s] = count.get(s, 0) + n
-        note(q, outs, ins, (s, count[s]))
+    def length(o, ins, rate=None):
+        if any(len(i[1]) > 1 for i in ins):
+            return 50 + 1.6 * o[2]
+        if rate is None:
+            rate = 0.5 if all(SCRATCH[x[1][0][0]][2] in (BF, F16, U16) for x in [o] + ins) else 1.0
+        return max(64.0, rate * o[2])
 
     def ap(x):
         return x[0] if isinstance(x, tuple) else x
 
     def ts(o, i, s1, op0, s2=None, op1=None):
         if op1 is None:
-            emit("v", lambda: g.vector.tensor_scalar(o[0], i[0], ap(s1), None, op0), [o], [i, s1])
+            emit("v", lambda: g.vector.tensor_scalar(o[0], i[0], ap(s1), None, op0), [o], [i, s1], length(o, [i]))
         else:
-            emit("v", lambda: g.vector.tensor_scalar(o[0], i[0], ap(s1), ap(s2), op0, op1), [o], [i, s1, s2])
+            emit("v", lambda: g.vector.tensor_scalar(o[0], i[0], ap(s1), ap(s2), op0, op1), [o], [i, s1, s2], length(o, [i]))
 
     def tt(o, a, b, op):
-        emit("v", lambda: g.vector.tensor_tensor(o[0], a[0], b[0], op), [o], [a, b])
+        emit("v", lambda: g.vector.tensor_tensor(o[0], a[0], b[0], op), [o], [a, b], length(o, [a, b], 1.0 if a[1][0][4] else 2.0))
 
     def cp(o, i):
-        emit("v", lambda: g.vector.tensor_copy(o[0], i[0]), [o], [i])
+        emit("v", lambda: g.vector.tensor_copy(o[0], i[0]), [o], [i], length(o, [i]))
 
     def scat(w, offs, i):
-        emit("v", lambda: g.vector.tensor_copy(w[0].indirect(offs[0]), i[0]), [w], [i, offs])
+        emit("v", lambda: g.vector.tensor_copy(w[0].indirect(offs[0]), i[0]), [w], [i, offs], 50 + 3.8 * i[2])
 
     def scan(o, a, b, init, op0, op1):
-        emit("v", lambda: g.vector.tensor_tensor_scan(o[0], a[0], b[0], ap(init), op0, op1), [o], [a, b, init])
+        emit("v", lambda: g.vector.tensor_tensor_scan(o[0], a[0], b[0], ap(init), op0, op1), [o], [a, b, init], length(o, [a, b]))
 
     def ms(o, c):
-        emit("v", lambda: g.vector.memset(o[0], c), [o], [])
+        emit("v", lambda: g.vector.memset(o[0], c), [o], [], length(o, []))
 
     def tr(o, i):
-        emit("v", lambda: g.vector.transpose(o[0], i[0]), [o], [i])
+        emit("v", lambda: g.vector.transpose(o[0], i[0]), [o], [i], length(o, [i]))
 
     def quant(qn, sn, lo, hi, i):
         a, b = R(qn, lo, hi), R(sn, lo, hi)
-        emit("v", lambda: g.vector.quantize_mx(a[0], b[0], i[0]), [a, b], [i])
+        emit("v", lambda: g.vector.quantize_mx(a[0], b[0], i[0]), [a, b], [i], 15 + 0.27 * i[2])
 
     def mm(o, wq, ws, w0, xq, xs, lo, hi):
         a, b, c, d = R(wq, w0, w0 + 128), R(ws, w0, w0 + 128), R(xq, lo, hi), R(xs, lo, hi)
-        emit("p", lambda: g.tensor.matmul_mx(o[0], a[0], b[0], c[0], d[0], True, True), [o], [a, b, c, d])
+        emit("p", lambda: g.tensor.matmul_mx(o[0], a[0], b[0], c[0], d[0], True, True), [o], [a, b, c, d], 1.2 * (hi - lo + 16))
 
     def act(o, i, f, scale=1.0, bias=None):
+        c = 15 + length(o, [i], 1.0) + (1300 if f == ACT.Exp else 0)
         if bias is None:
-            emit("a", lambda: g.scalar.activation(o[0], i[0], f, scale=ap(scale)), [o], [i, scale])
+            emit("a", lambda: g.scalar.activation(o[0], i[0], f, scale=ap(scale)), [o], [i, scale], c)
         else:
-            emit("a", lambda: g.scalar.activation(o[0], i[0], f, bias=ap(bias), scale=ap(scale)), [o], [i, scale, bias])
+            emit("a", lambda: g.scalar.activation(o[0], i[0], f, bias=ap(bias), scale=ap(scale)), [o], [i, scale, bias], c)
 
     def lin(c, a, scale, bias):
         act(col(c), col(a), ACT.Identity, scale, bias)
 
     def iota(o, pat, base, cm, small=True):
         if small:
-            emit("g", lambda: g.iota(o[0], pat, base, cm, allow_small_or_imprecise_dtypes=True), [o], [])
+            own.append(emit("g", lambda: g.iota(o[0], pat, base, cm, allow_small_or_imprecise_dtypes=True), [o], [], 130 + 2.2 * o[2]))
         else:
-            emit("g", lambda: g.iota(o[0], pat, base, cm), [o], [])
+            own.append(emit("g", lambda: g.iota(o[0], pat, base, cm), [o], [], 130 + 2.2 * o[2]))
 
     def keep(o, pat, op, base, cm):
-        i = R("one", 0, pat[0][1] * pat[1][1])
-        emit("g", lambda: g.affine_select(o[0], i[0], pat, op, 0.0, base, cm), [o], [i])
+        i = R("one", 0, o[2])
+        own.append(emit("g", lambda: g.affine_select(o[0], i[0], pat, op, 0.0, base, cm), [o], [i], 170 + 2.2 * o[2]))
 
-    def load(q, o, src, sem, codes=False):
-        emit(q, lambda: Q[q].dma_start(o[0].bitcast(dt.uint8) if codes else o[0], src), [o], [], sem)
+    def load(q, o, src, sem, late, codes=False):
+        emit(q, lambda: Q[q].dma_start(o[0].bitcast(dt.uint8) if codes else o[0], src), [o], [], 100, sem, 16, DMA + late)
+
+    def picked(a, b, o, codes):
+        if codes:
+            emit("v", lambda: g.vector.tensor_copy(a[0].bitcast(dt.uint32), b[0].bitcast(dt.uint32).indirect(o[0])), [a], [b, o], 250)
+        else:
+            emit("a", lambda: g.scalar.activation(a[0], b[0].indirect(o[0]), ACT.Copy), [a], [b, o], 270)
 
     peer = [T.cores[rank ^ 1], T.cores[rank ^ 2]]
 
-    def send(src, k, t):
+    def send(src, k, t, pre):
         i = R(src)
-        deps("g", [], i[1])
-        if topo.may_write(core, peer[t]):
+        direct = topo.may_write(core, peer[t])
+        if direct:
             dst, land, far = peer[t], "r%s%d" % (k, t), "a%s%d" % (k, t)
         else:
             dst, land, far = relay_of(core, peer[t], k, topo), "m" + k, "m%s_" % k
@@ -200,48 +316,45 @@ def rank_program(g, core, T, topo):
         a, b = T[land][:], i[0]
         if k == "q":
             a, b = a.bitcast(dt.uint8), b.bitcast(dt.uint8)
-        g.remote_dma(a, b, T.sem[far], T.sem["loc"], pid, rid, topo.mask(core, dst))
-        count["loc"] = count.get("loc", 0) + len(topo.engines(core, dst))
+        s = emit("g", lambda: g.remote_dma(a, b, T.sem[far], T.sem["loc"], pid, rid, topo.mask(core, dst)), [], [i], 1000, "loc",
+                 len(topo.engines(core, dst)), 0.0, pre)
+        last = peer[t] if direct else relay_of(peer[t], core, k, topo)
+        emit("x", None, [R("r%s%d" % (k, t))], [], 0.0, "a%s%d" % (k, t), len(topo.engines(last, core)),
+             (HOP if direct else 2 * HOP + 1000) + (3000 if k == "q" else 0), [s])
+        return s
 
     def store(q, o, i, src):
-        deps(q, [], src[1])
-        Q[q].dma_start(o, i).then_inc(T.sem["out"], 16)
-        count["out"] = count.get("out", 0) + 16
+        emit(q, lambda: Q[q].dma_start(o, i), [], [src], 100, "out", 16, DMA + src[2])
 
-    def pick(o, c, x, n):
-        scan(R(o[0], o[1], o[1] + n), R(c, 0, n), x, -B, ALU.add, ALU.min)
+    def pick(o, c, x, n, b=B):
+        scan(R(o[0], o[1], o[1] + n), R(c, 0, n), x, -b, ALU.add, ALU.min)
 
-    load("s", R("ut"), T.u[:], "lu")
-    load("a", R("xt", 0, 640), T.x[:, 0:640], "lx0")
-    load("s", R("xt", 640, 1920), T.x[:, 640:1920], "lx1")
-    load("s", R("wq"), T.wc[:], "lw_", True)
-    load("s", R("wp"), T.ws[:], "lp_")
-    load("s", R("vt"), T.v[:], "lv")
-    for t in range(2):
-        for k in "qsl":
-            last = peer[t] if topo.may_write(peer[t], core) else relay_of(peer[t], core, k, topo)
-            sem = "a%s%d" % (k, t)
-            count[sem] = len(topo.engines(last, core))
-            note("x", R("r%s%d" % (k, t))[1], [], (sem, count[sem]))
+    load("s", R("ut"), T.u[:], "lu", 1000)
+    load("a", R("xt", 0, 640), T.x[:, 0:640], "lx0", 1300)
+    load("s", R("xt", 640, 1920), T.x[:, 640:1920], "lx1", 2600)
+    load("s", R("wq"), T.wc[:], "lw_", 4000, True)
+    load("s", R("wp"), T.ws[:], "lp_", 4500)
+    load("s", R("vt"), T.v[:], "lv", 5000)
 
     iota(R("ii", 16, 17), [[0, 1]], 0, 1, False)
     iota(R("jh"), [[1, 35], [0, 4]], -3, 0)
     iota(R("iof", 0, 128), [[1, 128]], 0, 0)
     iota(R("ii", 0, 16), [[1, 16]], 128, -1, False)
-    iota(R("iof", 128, 608), [[1, 480]], 128, 0)
+    for k in range(128, NID, 272):
+        iota(R("iof", k, k + 272), [[1, 272]], k, 0)
     ms(R("one"), 1.0)
     for k in range(2):
         keep(R("r4", 320 * k, 320 * k + 320), [[0, 80], [1, 4]], ALU.not_equal, 0, 0)
-    iota(R("iof", 608, NID), [[1, NID - 608]], 608, 0)
-    for k in range(2):
         keep(R("r16", 496 * k, 496 * k + 496), [[0, 31], [1, 16]], ALU.not_equal, 0, 0)
     iota(R("uc"), [[16, 32]], 256, 1)
+    iota(R("pos4"), [[4, 496]], 0, 0)
     iota(R("ii", 24, 32), [[16, 8]], 7, 0, False)
     iota(R("jg"), [[4, 8], [0, 16]], 0, 0)
     iota(R("wb0"), [[0, 512]], 0, 0)
     iota(R("bt"), [[0, 896]], 0, 0)
     for b in range(4):
         keep(R("et", 512 * b, 512 * b + 512), [[0, 1], [1, 512]], ALU.is_equal, -b, -4)
+        quant("qe", "se", 128 * b, 128 * b + 128, R("et", 512 * b, 512 * b + 512))
     p_ = R("ii", 16, 17)
     ts(R("ij", 24, 25), p_, 15, ALU.bitwise_and)
     ts(R("ij", 25, 26), p_, 3, ALU.bitwise_and)
@@ -250,15 +363,15 @@ def rank_program(g, core, T, topo):
     ts(R("ij", 28, 29), p_, 4, ALU.logical_shift_right, 1, ALU.bitwise_and)
     cp(R("col", PI, GM + 1), R("ij", 24, 29))
     act(col(POW), col(PI), ACT.Exp, math.log(2.0))
-    lin(QOFF, PQ, -16.0, 48.0)
+    ts(col(QOFF), col(PQ), -16.0, ALU.mult, 48.0, ALU.add)
     ms(R("bt0", 160, 512), 0.0)
     ms(R("tab", 128, 256), 0.0)
     ms(R("tab", 512, 768), 0.0)
-    ms(R("ys"), -512.0)
+    ms(R("ys", 0, 4), -512.0)
     ts(col(TCOL), col(PI), 48.0, ALU.add)
     ts(col(FIX16), col(PI), 14.5, ALU.is_lt, B, ALU.mult)
     ts(col(FIX4), col(H4), 2.5, ALU.is_lt, B, ALU.mult)
-    cp(R("yy", 0, 4), R("ys"))
+    cp(R("yy", 0, 4), R("ys", 0, 4))
     ts(R("tab", 0, 128), R("iof", 0, 128), col(TCOL), ALU.is_equal, -1.0, ALU.mult)
     ts(R("ij", 0, 16), R("ii", 0, 16), 15, ALU.bitwise_and)
     ts(R("ii", 18, 22), R("iof", 4, 8), col(H4), ALU.subtract)
@@ -267,104 +380,91 @@ def rank_program(g, core, T, topo):
     ts(R("ij", 16, 20), R("ii", 18, 22), 3, ALU.bitwise_and)
     ts(R("ij", 20, 22), R("ii", 22, 24), 1, ALU.bitwise_and)
     ts(col(WT0), col(PI), 5.5, ALU.is_lt, col(POW), ALU.mult)
+    tt(col(WT), col(WT0), col(TMP), ALU.add)
     for t in range(4):
         ts(R("wc0", t, 512, 4), R("jh", 12 - 4 * t, 140 - 4 * t), col(G4), ALU.is_equal, col(WT0), ALU.mult)
+    quant("qwc", "swc", 0, 128, R("wc0"))
+    ts(R("wb0", 0, 512, 4), R("jg"), col(G4), ALU.is_equal, col(WT), ALU.mult)
+    quant("qwb", "swb", 0, 128, R("wb0"))
     for r in (2, 3):
         act(R("tab", 128 * r, 128 * r + 128), R("tab", 0, 128), ACT.Copy)
-    act(R("ids", 128, 608), R("iof", 128, 608), ACT.Copy)
+    for k in range(128, NID, 272):
+        act(R("ids", k, k + 272), R("iof", k, k + 272), ACT.Copy)
+    for k in range(0, NID, 304):
+        act(R("pfr", k, k + 304), R("iof", k, k + 304), ACT.Copy, 1.0 / 2048)
     act(R("kfr"), R("iof", 0, 224), ACT.Copy, 1.0 / 256)
     lin(NFG, GM, B, -B)
     lin(DFX, FIX16, 1.0, -1.0)
     lin(TM2, FIX4, 4.0, col(PQ))
-    lin(O16, FIX16, 1.0, 8.0)
+    lin(C1X, PQ, 1.0, -4.0 * OFF)
     lin(IFX, FIX4, 1.0, col(QOFF))
     lin(C1, TM2, 1.0, -4.0 * OFF)
     lin(F256, FIX4, 256.0, 0.0)
+    lin(FXX, FIX4, 4.0, 0.0)
     lin(KOF, PQ, 224.0, 0.0)
-    S7, CD = 512, 1024
-    quant("qu", "su", 0, 128, R("ut"))
-    quant("qx", "sx", 0, 160, R("xt", 0, 640))
-    mm(R("ps", 0, 160), "qu", "su", 0, "qx", "sx", 0, 160)
-    quant("qwc", "swc", 0, 128, R("wc0"))
+    lin(G1, GM, 64.0, col(C1))
+    lin(AOF, IFX, 1.0, 128.0 - 0.44)
+    for t in range(3):
+        lin(C20 + t, G1, 1.0, 4.0 * (BASE[t] - 16) - 0.33)
     ts(R("tm1", 0, 22), R("ij", 0, 22), 0.0, ALU.is_equal, 4 * B, ALU.mult)
-    ts(R("bt0", 0, 160), R("ps", 0, 160), 0.0, ALU.is_gt)
-    quant("qb", "sbb", 0, 128, R("bt0"))
-    mm(R("ps", CD, CD + 128), "qwc", "swc", 0, "qb", "sbb", 0, 128)
     ts(R("tm2", 0, 22), R("ij", 0, 22), 1.0, ALU.is_equal, -B, ALU.mult)
-    tt(col(WT), col(WT0), col(TMP), ALU.add)
-    ms(R("ptab", 0, 8), 0.0)
-    ts(R("oe", 0, 40), R("ps", CD, CD + 40), col(QOFF), ALU.add)
+    tt(R("pat", 0, 22), R("tm1", 0, 22), R("tm2", 0, 22), ALU.add)
+    for name, n, k0, per in (("c2", 64, 20, 2), ("c4", 224, 16, 4), ("c16", 496, 0, 16)):
+        for k in range(per):
+            act(R(name, k, n, per), R("one", 0, n // per), ACT.Copy, R("pat", k0 + k, k0 + k + 1))
+    act(R("c4x"), R("c4"), ACT.Copy, 4.0)
+    ms(R("pool", 0, 16), 0.0)
+    ms(R("tl", 256, 512), 0.0)
+    ms(R("tl", 640, 1152), 0.0)
+    ms(R("occb", NA + PR[2], 288), 0.0)
+    ts(R("q4", 0, 64), R("one", 0, 64), 0.0, ALU.mult)
+    ts(R("q4", 64 + 1920, 64 + 1984), R("one", 0, 64), 0.0, ALU.mult)
+    act(R("win", 0, 256), R("one", 0, 256), ACT.Copy, FILL)
+    for k in range(0, 1920, 480):
+        act(R("pool", 16 + k, 496 + k), R("xt", k, k + 480), ACT.Copy, 0.5)
+    quant("qu", "su", 0, 128, R("ut"))
+    quant("qv", "sv", 0, 128, R("vt"))
+    cp(R("o7"), R("ii", 24, 32))
+    picked(R("qu7"), R("qu"), R("o7"), True)
+    picked(R("su7"), R("su"), R("o7"), False)
+    S7, CD = 512, 1024
 
-    def marks(offs, s0, s1, both=False):
+    def marks(offs, s0, s1):
         act(R("e", 4 * s0, 4 * s1), ind(R("tab"), offs), ACT.Copy)
-        if both:
-            act(R("d0", 4 * s0, 4 * s1), R("e", 4 * s0, 4 * s1), ACT.Identity, 5.0, 1.0)
+        ts(R("d0", 4 * s0, 4 * s1), R("e", 4 * s0, 4 * s1), 5.0, ALU.mult, 1.0, ALU.add)
 
     def shared_marks(offs, s0):
         a = 4 * s0
         ts(R("d0", a, a + 192), ind(R("tab"), R(offs, 0, 12)), 5.0, ALU.mult, 1.0, ALU.add)
-        act(R("e", a + 192, a + 384), ind(R("tab"), R(offs, 12, 24)), ACT.Copy)
-        ts(R("d0", a + 192, a + 384), R("e", a + 192, a + 384), 5.0, ALU.mult, 1.0, ALU.add)
+        marks(R(offs, 12, 24), s0 + 48, s0 + 96)
         act(R("e", a, a + 192), R("d0", a, a + 192), ACT.Identity, 0.2, -0.2)
 
-    marks(R("oe", 0, 40), 0, 160)
-    quant("qx", "sx", 160, 480, R("xt", 640, 1920))
-    mm(R("ps", 512, 832), "qu", "su", 0, "qx", "sx", 160, 480)
-    tt(R("pat", 0, 22), R("tm1", 0, 22), R("tm2", 0, 22), ALU.add)
-    ms(R("pool", 0, 16), 0.0)
-    ts(R("q4", 0, 64), R("one", 0, 64), 0.0, ALU.mult)
-    ts(R("q4", 64 + 1920, 64 + 1984), R("one", 0, 64), 0.0, ALU.mult)
-    ts(R("bt0", 160, 480), R("ps", 512, 832), 0.0, ALU.is_gt)
-    quant("qb", "sbb", 128, 256, R("bt0"))
-    mm(R("ps", 1536, 1664), "qwc", "swc", 0, "qb", "sbb", 128, 256)
-    ts(R("d0", 0, 640), R("e", 0, 640), 5.0, ALU.mult, 1.0, ALU.add)
-    ts(R("oe", 40, 120), R("ps", 1576, 1656), col(QOFF), ALU.add)
-    for k in range(2):
-        act(R("c2", k, 64, 2), R("one", 0, 32), ACT.Copy, R("pat", 20 + k, 21 + k))
-    for k in range(4):
-        act(R("c4", k, 224, 4), R("one", 0, 56), ACT.Copy, R("pat", 16 + k, 17 + k))
-    marks(R("oe", 40, 80), 160, 320)
-    marks(R("oe", 80, 120), 320, 480)
-    act(R("win", 0, 256), R("one", 0, 256), ACT.Copy, FILL)
-    for k in range(16):
-        act(R("c16", k, 496, 16), R("one", 0, 31), ACT.Copy, R("pat", k, k + 1))
-    act(R("pool", 16, 16 + 960), R("xt", 0, 960), ACT.Copy, 0.5)
-    lin(G1, GM, 64.0, col(C1))
-    lin(AOF, IFX, 1.0, 128.0 - 0.44)
-    for t in range(3):
-        lin(C20 + t, G1, 1.0, 4.0 * (BASE[t] - 16))
+    state = [0]
 
-    def more_constants():
-        act(R("pool", 16 + 960, 16 + 1920), R("xt", 960, 1920), ACT.Copy, 0.5)
-        act(R("ids", 608, NID), R("iof", 608, NID), ACT.Copy)
-
-    def rows(t, s0, s1, made=False):
-        a, b = 4 * s0, 4 * s1
-        if not made:
-            ts(R("d0", a, b), R("e", a, b), 5.0, ALU.mult, 1.0, ALU.add)
+    def rows(t, s0, s1):
+        a, b, k = 4 * s0, 4 * s1, state[0]
         for q in range(4):
-            scan(R("yy", 4 + a + q, 4 + b, 4), R("d0", a + q, b, 4), R("ids", BASE[t] + s0, BASE[t] + s1), R("ys", q, q + 1), ALU.mult, ALU.min)
+            scan(R("yy", 4 + a + q, 4 + b, 4), R("d0", a + q, b, 4), R("ids", BASE[t] + s0, BASE[t] + s1), R("ys", k + q, k + q + 1), ALU.mult, ALU.min)
+        state[0] = (k + 4) % 12
+        cp(R("ys", state[0], state[0] + 4), R("yy", b, b + 4))
         scan(R("vv", a, b), R("yy", a, b), R("e", a, b), 0.0, ALU.max, ALU.mult)
-        cp(R("ys"), R("yy", b, b + 4))
         scan(R("q4", 64 + a, 64 + b), R("r4", 0, b - a), R("vv", a, b), 0.0, ALU.mult, ALU.min)
 
-    def number(s0, s1, last, then=None):
+    def number(s0, s1, last):
         n1 = (s1 - s0) // 32
         n2 = n1 + (1 if last else 0)
         m0, m = s0 // 16, n1 + n2
-        tr(R("tt", 0, 32 * n2), R("q4", 3 + 4 * s0, 4 * s0 + 128 * n2, 4))
-        tr(R("tt", 32 * n2, 32 * m), R("q4", 67 + 4 * s0, 64 + 4 * s1, 4))
-        scan(R("rr", 0, 32 * m), R("r16", 0, 32 * m), R("tt", 0, 32 * m), 0.0, ALU.mult, ALU.min)
-        pick(("sel", 0), "c2", R("rr", 15, 32 * m, 16), 2 * m)
-        ts(R("pw", m0, m0 + m, 2), R("sel", 1, 2 * n2, 2), -1.0, ALU.mult, col(NFG), ALU.add)
-        ts(R("pw", m0 + 1, m0 + m, 2), R("sel", 2 * n2 + 1, 2 * m, 2), -1.0, ALU.mult, col(NFG), ALU.add)
+        z = 32 * m0
+        tr(R("tt", z, z + 32 * n2), R("q4", 3 + 4 * s0, 4 * s0 + 128 * n2, 4))
+        tr(R("tt", z + 32 * n2, z + 32 * m), R("q4", 67 + 4 * s0, 64 + 4 * s1, 4))
+        scan(R("rr", z, z + 32 * m), R("r16", 0, 32 * m), R("tt", z, z + 32 * m), 0.0, ALU.mult, ALU.min)
+        y = 2 * m0
+        pick(("sel", y), "c2", R("rr", z + 15, z + 32 * m, 16), 2 * m)
+        ts(R("pw", m0, m0 + m, 2), R("sel", y + 1, y + 2 * n2, 2), -1.0, ALU.mult, col(NFG), ALU.add)
+        ts(R("pw", m0 + 1, m0 + m, 2), R("sel", y + 2 * n2 + 1, y + 2 * m, 2), -1.0, ALU.mult, col(NFG), ALU.add)
         o, a, b = R("pw", m0, m0 + m), 16 * m0, 16 * (m0 + m)
-        h = m0 + (m + 2) // 4 * 2
-        act(R("fb", 16 * h, b), ind(R("iof"), R("pw", h, m0 + m)), ACT.Sign)
-        act(R("ptab", 8 + a, 8 + b), ind(R("iof"), o), ACT.Copy)
-        if then is not None:
-            then()
-        ts(R("fb", a, 16 * h), ind(R("iof"), R("pw", m0, h)), 0.0, ALU.is_gt)
+        act(R("fb", a, b), ind(R("iof"), o), ACT.Sign)
+        tt(R("pk", a, b), ind(R("pfr"), o), R("pos4", a, b), ALU.add)
         ts(R("nf", m0, m0 + m), o, 0.0, ALU.is_equal)
         scan(R("cum", a, b), R("one", 0, b - a), R("fb", a, b), R("cs", 0, 1) if s0 else 0.0, ALU.mult, ALU.add)
         tt(R("zz", m0, m0 + m), R("nf", m0, m0 + m), R("uc", m0, m0 + m), ALU.mult)
@@ -373,183 +473,147 @@ def rank_program(g, core, T, topo):
             cp(R("cs", 0, 1), R("cum", b - 1, b))
         tt(R("ds", m0, m0 + m), R("cw", a + 15, b, 16), R("zz", m0, m0 + m), ALU.add)
         ts(R("od", m0, m0 + m), R("ds", m0, m0 + m), col(DFX), ALU.add)
-        scat(R("win"), R("od", m0, m0 + m), R("iof", a, b))
+        scat(R("win"), R("od", m0, m0 + m), R("pk", a, b))
 
-    def fire(t, n, cut, during):
+    def fire(t, n, cut):
         P = PR[t]
         top = 4 * (BASE[t] + n - OFF)
-        w = R("win", 0, P)
-        pick(("w4", 0), "c4", w, P)
-        ts(R("o2", 0, P // 4), R("w4", 3, P, 4), 4.0, ALU.mult, col(C20 + t), ALU.add)
-        h = 32 if cut else P // 8
-        for a, b in ((0, h), (h, P // 4)):
+        m = P // 4
+        pick(("w4", 0), "c4x", R("win", 0, P), P, 4 * B)
+        ts(R("o2", 0, m), R("w4", 3, P, 4), col(C20 + t), ALU.add)
+        ts(R("wi", 0, m), R("w4", 3, P, 4), col(FXX), ALU.add, 2048.0, ALU.mult)
+        ts(R("wi", 56, 56 + m), R("wi", 0, m), 2047, ALU.bitwise_and)
+        ts(R("o1", 0, m), R("wi", 56, 56 + m), 4.0, ALU.mult, col(C1X), ALU.add)
+        for a, b in ((0, 12), (12, 32), (32, m)) if cut else ((0, 10), (10, 24), (24, m)):
             act(R("two", 16 * a, 16 * b), ind(R("pool", 0, top), R("o2", a, b)), ACT.Copy)
-        during()
-        pick(("w16", 0), "c16", w, P)
-        ts(R("o16", 0, P // 16), R("w16", 15, P, 16), col(O16), ALU.add)
-        cp(R("g1", 0, P), ind(R("ptab", 0, 8 + n + 16), R("o16", 0, P // 16)))
-        pick(("w1", 0), "c4", R("g1", 0, P), P)
-        ts(R("o1", 0, P // 4), R("w1", 3, P, 4), 4.0, ALU.mult, col(C1), ALU.add)
-        for a, b in ((0, h), (h, P // 4)):
             tt(R("bb", 16 * a, 16 * b), ind(R("pool", 0, top), R("o1", a, b)), R("two", 16 * a, 16 * b), ALU.add)
-            if cut:
-                k = 128 if a else 0
+            if cut and a:
+                k = 0 if b == 32 else 128
                 quant("qbb", "sbq", k, k + 128, R("bb", 4 * (4 * b - 128), 16 * b))
                 for c in range(4):
-                    mm(R("ps" if a else "pr", 512 * c, 512 * c + 128), "wq", "wp", 128 * c, "qbb", "sbq", k, k + 128)
-                if not a:
-                    for c in range(4):
+                    mm(R("ps" if k else "pr", 512 * c, 512 * c + 128), "wq", "wp", 128 * c, "qbb", "sbq", k, k + 128)
+                    if not k:
                         act(R("hh", c, 512, 4), R("pr", 512 * c, 512 * c + 128), ACT.Relu, 0.03125)
         if not cut:
             quant("qbb", "sbq", 0, P, R("bb", 0, 4 * P))
             for c in range(4):
                 mm(R("pr", 512 * c, 512 * c + P), "wq", "wp", 128 * c, "qbb", "sbq", 0, P)
 
-    rows(0, 0, 160, True)
-    rows(0, 160, 320)
-    rows(0, 320, 480)
-    cp(R("o7"), R("ii", 24, 32))
-    number(0, 480, True, more_constants)
+    quant("qx", "sx", 0, 160, R("xt", 0, 640))
+    mm(R("ps", 0, 160), "qu", "su", 0, "qx", "sx", 0, 160)
+    ts(R("bt0", 0, 160), R("ps", 0, 160), 0.0, ALU.is_gt)
+    quant("qb", "sbb", 0, 128, R("bt0"))
+    mm(R("ps", CD, CD + 128), "qwc", "swc", 0, "qb", "sbb", 0, 128)
+    ts(R("oe", 0, 40), R("ps", CD, CD + 40), col(QOFF), ALU.add)
+    quant("qx", "sx", 160, 480, R("xt", 640, 1920))
+    mm(R("ps", 512, 832), "qu", "su", 0, "qx", "sx", 160, 480)
+    ts(R("bt0", 160, 480), R("ps", 512, 832), 0.0, ALU.is_gt)
+    quant("qb", "sbb", 128, 256, R("bt0"))
+    mm(R("ps", 1536, 1664), "qwc", "swc", 0, "qb", "sbb", 128, 256)
+    ts(R("oe", 40, 120), R("ps", 1576, 1656), col(QOFF), ALU.add)
+    for s0 in (0, 160, 320):
+        marks(R("oe", s0 // 4, s0 // 4 + 40), s0, s0 + 160)
+        rows(0, s0, s0 + 160)
+    number(0, 320, False)
+    number(320, 480, True)
     n = C
     for t in range(2):
         P = PR[t]
         qh, sh, ls, rl = "qh%d" % t, "sh%d" % t, "ls%d" % t, "rl%d" % t
         w = R("win", 0, P)
-
-        def limits():
-            act(R("thr", 0, P), w, ACT.Relu, -1e26)
-            act(R("nh", 0, P), w, ACT.Relu, -0.5)
-            if t == 0:
-                a, b, o = R("su7"), R("su"), R("o7")
-                emit("a", lambda: g.scalar.activation(a[0], b[0].indirect(o[0]), ACT.Copy), [a], [b, o])
-
-        fire(t, n, True, limits)
+        fire(t, n, True)
+        act(R("thr", 0, P), w, ACT.Relu, -1e26)
+        act(R("nh", 0, P), w, ACT.Relu, -0.125)
         n = P + L
-        if t == 0:
-            a, b, o = R("qu7"), R("qu"), R("o7")
-            emit("v", lambda: g.vector.tensor_copy(a[0].bitcast(dt.uint32), b[0].bitcast(dt.uint32).indirect(o[0])), [a], [b, o])
-        else:
-            quant("qv", "sv", 0, 128, R("vt"))
-            ms(R("tl", 256, 512), 0.0)
-        quant(qh, sh, 0, 128, R("hh", 0, 512))
         lo = 256 - P
+        quant(qh, sh, 0, 128, R("hh", 0, 512))
+        mm(R("pr", 0, 128), "qu7", "su7", 0, qh, sh, 0, 128)
+        mm(R("pr", 512, 640), "qu", "su", 0, qh, sh, 0, 128)
+        tt(R("nc", 0, 128), R("pr", 0, 128), R("thr", 0, 128), ALU.is_le)
+        act(R("sg", 0, 128), R("pr", 512, 640), ACT.Sign)
         for b in (0, 2):
             ts(R("hh", 512 + b, 4 * P, 4), R("ps", 512 * b + lo, 512 * b + 128), 0.0, ALU.max, 0.03125, ALU.mult)
             act(R("hh", 513 + b, 4 * P, 4), R("ps", 512 * b + 512 + lo, 512 * b + 640), ACT.Relu, 0.03125)
-            if t == 0:
-                if b == 0:
-                    ts(R("wb0", 0, 512, 4), R("jg"), col(G4), ALU.is_equal, col(WT), ALU.mult)
-                else:
-                    quant("qwb", "swb", 0, 128, R("wb0"))
         quant(qh, sh, P - 128, P, R("hh", 4 * (P - 128), 4 * P))
-        mm(R("ps", S7, S7 + P), "qu7", "su7", 0, qh, sh, 0, P)
-        mm(R("ps", 0, P), "qu", "su", 0, qh, sh, 0, P)
-        direct = topo.may_write(core, peer[t])
-        send(qh, "q", t)
-        send(sh, "s", t)
+        mm(R("ps", 0, 128), "qu", "su", 0, qh, sh, P - 128, P)
+        mm(R("ps", S7, S7 + 128), "qu7", "su7", 0, qh, sh, P - 128, P)
+        tt(R("nc", 128, P), R("ps", S7 + lo, S7 + 128), R("thr", 128, P), ALU.is_le)
+        act(R("sg", 128, P), R("ps", lo, 128), ACT.Sign)
+        act(R("bt", 0, 512, 4), R("sg", 0, 128), ACT.Relu)
+        act(R("bt", 512, 4 * P, 4), R("sg", 128, P), ACT.Relu)
+        s = send(sh, "s", t, [send(qh, "q", t, own)])
         nb = BASE[t + 1]
         act(R("lwin", 0, L), R("one", 0, L), ACT.Copy, 0.0)
-        act(R("yy", 0, 4), R("ys"), ACT.Copy)
+        act(R("yy", 0, 4), R("ys", state[0], state[0] + 4), ACT.Copy)
         act(R("q4", 64 + 4 * n, 128 + 4 * n), R("one", 0, 64), ACT.Copy, 0.0)
-        if t == 0:
-            quant("qe", "se", 0, 256, R("et", 0, 1024))
-        else:
-            ms(R("tl", 640, 1152), 0.0)
-            ms(R("occb", NA + PR[2], 288), 0.0)
-        act(R("sg", 0, P), R("ps", 0, P), ACT.Sign)
-        act(R("bt", 0, 4 * P, 4), R("sg", 0, P), ACT.Relu)
-        act(R("pool", 4 * (nb - OFF), 4 * (nb - OFF + P)), R("hh", 0, 4 * P), ACT.Copy, 0.5)
+        act(R("win", 0, 256), R("one", 0, 256), ACT.Copy, FILL)
+        for k in range(0, 4 * P, 2 * P):
+            act(R("pool", 4 * (nb - OFF) + k, 4 * (nb - OFF) + k + 2 * P), R("hh", k, k + 2 * P), ACT.Copy, 0.5)
         m = P // 16
-        tt(R("nc", 0, P), R("ps", S7, S7 + P), R("thr", 0, P), ALU.is_le)
         scan(R("nc", P, 2 * P), R("one", 0, P), R("nc", 0, P), 0.0, ALU.add, ALU.subtract)
-        pick(("ncw", 0), "c16", R("nc", 0, 2 * P), 2 * P)
-        ts(R("t1", 0, P), R("nc", P, 2 * P), L + 0.5, ALU.is_gt, 256.0, ALU.mult)
+        pick(("ncw", 0), "c16", R("nc", 0, P), P)
+        pick(("ncw", P), "c16", R("nc", P, 2 * P), P)
         ts(R("la", 0, m), R("ncw", 15, P, 16), col(FIX16), ALU.add)
         quant("qb", "sbb", 0, P, R("bt", 0, 4 * P))
         mm(R("ps", CD, CD + P), "qwb", "swb", 0, "qb", "sbb", 0, P)
         tt(R("la", 16, 16 + m), R("la", 0, m), R("uc", 0, m), ALU.mult)
-        scan(R("reg", 0, P), R("t1", 0, P), R("nh", 0, P), 0.0, ALU.max, ALU.max)
         tt(R("la", 32, 32 + m), R("ncw", P + 15, 2 * P, 16), R("la", 16, 16 + m), ALU.add)
         ts(R("ol", 0, m), R("la", 32, 32 + m), col(DFX), ALU.add)
-
-        def staying():
-            tt(R("idx", 0, P), R("ps", CD, CD + P), R("reg", 0, P), ALU.add)
-            pick(("iw", 0), "c4", R("idx", 0, P), P)
-            if direct:
-                tt(R("val", 0, P), R("ps", CD, CD + P), R("kfr", 0, P), ALU.add)
-            ts(R("oe", 0, P // 4), R("iw", 3, P, 4), col(IFX), ALU.add)
-            if direct:
-                marks(R("oe", 0, 24), 0, 96, True)
-            else:
-                shared_marks("oe", 0)
-            marks(R("oe", 24, P // 4), 96, P, direct)
-
-        if direct:
-            staying()
-        else:
-            tt(R("val", 0, P), R("ps", CD, CD + P), R("kfr", 0, P), ALU.add)
+        tt(R("val", 0, P), R("ps", CD, CD + P), R("kfr", 0, P), ALU.add)
         scat(R("lwin"), R("ol", 0, m), R("val", 0, P))
         pick(("lw", 0), "c4", R("lwin", 0, L), L)
-        ts(R("li", 0, 24), R("lw", 3, L, 4), 256.0, ALU.mult, col(F256), ALU.add)
         ts(R(ls, 0, 24), R("lw", 3, L, 4), col(AOF), ALU.add)
-        ts(R("li", 24, 48), R("li", 0, 24), 255, ALU.bitwise_and)
-        ts(R(ls, 24, 48), R("li", 24, 48), col(KOF), ALU.add)
-        send(ls, "l", t)
-        if not direct:
-            staying()
-        act(R("win", 0, 256), R("one", 0, 256), ACT.Copy, FILL)
-        rows(t + 1, 0, 96, True)
-        if t == 0:
-            quant("qe", "se", 256, 512, R("et", 1024, 2048))
-        rows(t + 1, 96, P, direct)
-        if not direct:
-            number(0, P, False)
-
-        def unpacked():
-            for b in range(4):
-                mm(R("pr", 512 * b, 512 * b + P), "qe", "se", 128 * b, "rq%d" % t, "rs%d" % t, 0, P)
-                act(R("dst", 224 * b, 224 * b + P), R("pr", 512 * b, 512 * b + P), ACT.Copy, 0.5)
-            act(R("pool", 4 * (nb - OFF + P), 4 * (nb - OFF + n)), ind(R("dst"), R(rl, 24, 48)), ACT.Copy)
-
+        ts(R(ls, 24, 48), R("lw", 3, L, 4), 256.0, ALU.mult, col(F256), ALU.add)
+        send(ls, "l", t, [s])
+        ts(R("t1", 0, P), R("nc", P, 2 * P), L + 0.5, ALU.is_gt, 256.0, ALU.mult)
+        scan(R("reg", 0, P), R("t1", 0, P), R("nh", 0, P), 0.0, ALU.max, ALU.max)
+        tt(R("idx", 0, P), R("ps", CD, CD + P), R("reg", 0, P), ALU.add)
+        pick(("iw", 0), "c4", R("idx", 0, P), P)
+        ts(R("oe", 0, P // 4), R("iw", 3, P, 4), col(IFX), ALU.add)
+        marks(R("oe", 0, 24), 0, 96)
+        marks(R("oe", 24, P // 4), 96, P)
+        rows(t + 1, 0, 96)
+        rows(t + 1, 96, P)
+        number(0, P, False)
         shared_marks(rl, P)
-        if direct:
-            unpacked()
-        rows(t + 1, P, n, True)
-        number(0 if direct else P, n, True, None if direct else unpacked)
+        rows(t + 1, P, n)
+        number(P, n, True)
+        cp(R("li", 0, 24), R(rl, 24, 48))
+        ts(R("li", 24, 48), R("li", 0, 24), 255, ALU.bitwise_and)
+        ts(R("ko"), R("li", 24, 48), col(KOF), ALU.add)
+        for b in range(4):
+            mm(R("pr", 512 * b, 512 * b + P), "qe", "se", 128 * b, "rq%d" % t, "rs%d" % t, 0, P)
+            act(R("dst", 224 * b, 224 * b + P), R("pr", 512 * b, 512 * b + P), ACT.Copy, 0.5)
+        act(R("pool", 4 * (nb - OFF + P), 4 * (nb - OFF + n)), ind(R("dst"), R("ko")), ACT.Copy)
     P = PR[2]
     w = R("win", 0, P)
-
-    def results():
-        for k in range(4):
-            ts(R("ot", 4 * k, 4 * k + 4), R("ys"), 4.0, ALU.mult, float(k - 4 * OFF), ALU.add)
-        cp(R("ot", 16, 20), R("ys"))
-        for k in range(4):
-            act(R("tl", k, 4 * NA, 4), ind(R("pool"), R("ot", 4 * k, 4 * k + 4)), ACT.Copy, 2.0)
-        act(R("thr", 0, P), w, ACT.Relu, 1e26, 5.12e28)
-        act(R("occb", 0, NA), ind(R("iof"), R("ot", 16, 20)), ACT.Sign)
-        act(R("occb", NA, NA + P), w, ACT.Sign, 1.0, -FILL)
-        store("s", T.occ[:], T.occb[0:128:16, :], R("occb"))
-
-    fire(2, n, False, results)
-    quant("qt", "st", 0, 128, R("tl", 0, 512))
+    fire(2, n, False)
+    ys = R("ys", state[0], state[0] + 4)
+    for k in range(4):
+        ts(R("ot", 4 * k, 4 * k + 4), ys, 4.0, ALU.mult, float(k - 4 * OFF), ALU.add)
+        act(R("tl", k, 4 * NA, 4), ind(R("pool"), R("ot", 4 * k, 4 * k + 4)), ACT.Copy, 2.0)
+    cp(R("ot", 16, 20), ys)
+    act(R("thr", 0, P), w, ACT.Relu, 1e26, 5.12e28)
+    act(R("occb", 0, NA), ind(R("iof"), R("ot", 16, 20)), ACT.Sign)
+    act(R("occb", NA, NA + P), w, ACT.Sign, 1.0, -FILL)
+    store("s", T.occ[:], T.occb[0:128:16, :], R("occb"))
     quant("qt", "st", 160, 288, R("tl", 640, 1152))
-    mm(R("ps", 512, 640), "qv", "sv", 0, "qt", "st", 0, 128)
+    quant("qt", "st", 0, 128, R("tl", 0, 512))
     mm(R("ps", 1024, 1152), "qv", "sv", 0, "qt", "st", 160, 288)
-    for a in (0, NA + P):
-        store("s", T.oc[:, 4 * a:4 * a + 256], T.qt[:, a:a + 64].bitcast(dt.uint8), R("qt", a, a + 64))
-    for b in range(4):
-        tt(R("hm", P * b, P * b + P), R("pr", 512 * b, 512 * b + P), R("thr", 0, P), ALU.min)
-        act(R("tl", 4 * NA + b, 4 * (NA + P), 4), R("hm", P * b, P * b + P), ACT.Relu, 0.03125)
+    mm(R("ps", 512, 640), "qv", "sv", 0, "qt", "st", 0, 128)
     cp(R("yb", 0, NA), R("ps", 512, 512 + NA))
     cp(R("yb", NA + P, 288), R("ps", 1088, 1152))
     for a in (0, NA + P):
+        store("s", T.oc[:, 4 * a:4 * a + 256], T.qt[:, a:a + 64].bitcast(dt.uint8), R("qt", a, a + 64))
         store("s", T.y[:, a:a + 64], T.yb[:, a:a + 64], R("yb", a, a + 64))
+    for b in range(4):
+        tt(R("hm", P * b, P * b + P), R("pr", 512 * b, 512 * b + P), R("thr", 0, P), ALU.min)
+        act(R("tl", 4 * NA + b, 4 * (NA + P), 4), R("hm", P * b, P * b + P), ACT.Relu, 0.03125)
     quant("qt", "st", NA, NA + P, R("tl", 4 * NA, 4 * (NA + P)))
     mm(R("ps", 0, P), "qv", "sv", 0, "qt", "st", NA, NA + P)
     store("s", T.oc[:, 4 * NA:4 * (NA + P)], T.qt[:, NA:NA + P].bitcast(dt.uint8), R("qt"))
     for k in range(4):
         store("a", T.osc[4 * k:4 * k + 4, :], T.st[32 * k:32 * k + 4, :], R("st"))
     cp(R("yb", NA, NA + P), R("ps", 0, P))
-    store("s", T.y[:, NA:NA + P], T.yb[:, NA:NA + P], R("yb"))
-    for s in count:
-        wait("s", (s, count[s]))
+    store("s", T.y[:, NA:NA + P], T.yb[:, NA:NA + P], R("yb", NA, NA + P))
+    issue(ops, Q, T)

@@ -7,11 +7,12 @@ F32, BF, F16, I32, U16, U8, Q4 = "float32", "bfloat16", "float16", "int32", "uin
 
 C, NA, L = 480, 64, 96
 PR = [224, 192, 160]
-BASE = [128, 608, 928]
-OFF = 124
-NID = 1216
+RUNS = ((0, 224, 32, 1), (224, 352, 256, 2), (352, 480, 512, 4))
+BASE = [0, 1024, 1344]
+NID = 1632
 B = 2048.0
-FILL = -4096.0
+BW = 7168.0
+B2 = 1024.0
 HOP, DMA = 2800.0, 2000.0
 CASES = ((90.0, 0.8), (130.0, 1.0), (180.0, 1.3))
 TRIES = [2500, 20000]
@@ -27,32 +28,44 @@ SCRATCH = {
     "xt": sb(1920, BF), "ut": sb(512, BF), "vt": sb(512, BF),
     "qx": sb(480, Q4), "sx": sb(480, U8), "qu": sb(128, Q4), "su": sb(128, U8), "qu7": sb(128, Q4), "su7": sb(128, U8),
     "qv": sb(128, Q4), "sv": sb(128, U8), "wq": sb(512, Q4), "wp": sb(512, U8),
-    "pool": sb(4 * (NID - OFF), BF), "bt0": sb(512, BF), "bt": sb(896, BF), "sg": sb(224, BF), "qb": sb(256, Q4), "sbb": sb(256, U8),
-    "ii": sb(32, I32), "ij": sb(32, I32), "col": sb(32, F32), "iof": sb(NID, F32), "ids": sb(NID, F16), "kfr": sb(224, F32),
-    "pfr": sb(NID, F32), "pos4": sb(496, F32),
-    "jg": sb(128, F32), "jh": sb(140, F32), "tm1": sb(24, F32), "tm2": sb(24, F32), "pat": sb(24, F32),
-    "c16": sb(496, BF), "c4": sb(224, BF), "c4x": sb(224, BF), "c2": sb(64, BF), "r16": sb(992, BF), "r4": sb(640, BF),
-    "one": sb(512, BF), "tab": sb(768, BF), "uc": sb(32, F32), "o7": sb(8, U16),
-    "wc0": sb(512, BF), "wb0": sb(512, BF), "et": sb(2048, BF),
-    "qwc": sb(128, Q4), "swc": sb(128, U8), "qwb": sb(128, Q4), "swb": sb(128, U8), "qe": sb(512, Q4), "se": sb(512, U8),
-    "oe": sb(120, U16), "e": sb(1920, BF), "d0": sb(1920, BF), "yy": sb(1924, F16), "ys": sb(12, F32), "vv": sb(1920, F16),
-    "q4": sb(64 + 1984, F16), "tt": sb(992, F16), "rr": sb(992, F16), "sel": sb(64, F32), "pw": sb(32, U16),
-    "fb": sb(496, BF), "cum": sb(496, F16), "cs": sb(2, F32), "cw": sb(496, F16), "nf": sb(32, F32), "zz": sb(32, F32), "ds": sb(32, F32),
-    "od": sb(32, U16), "win": sb(1152, F32), "pk": sb(496, F32),
-    "w4": sb(224, F32), "wi": sb(112, I32), "o2": sb(56, U16), "o1": sb(56, U16),
+    "pool": sb(4 * NID, BF), "sm": sb(16 + 4 * 288, BF), "tok": sb(4 * 288, BF), "bt0": sb(512, BF), "bt": sb(896, BF), "sg": sb(320, BF),
+    "qb": sb(256, Q4), "sbb": sb(256, U8),
+    "ii": sb(48, I32), "ij": sb(48, I32), "col": sb(40, F32), "iof": sb(224, F32), "ids": sb(608, F16), "kfr": sb(224, F32),
+    "idr": sb(480, BF), "idp0": sb(480, F32), "idp": sb(608, F32), "nj": sb(480, F16), "cq": sb(32, F32),
+    "jg": sb(128, BF), "jh": sb(140, BF), "jq": sb(128, BF), "tm1": sb(40, F32), "tm2": sb(40, F32), "pat": sb(4, F32),
+    "c32": sb(448, BF), "c4": sb(224, BF), "c4x": sb(224, BF), "r16": sb(224, BF), "r4": sb(512, BF),
+    "one": sb(512, BF), "tab": sb(768, BF), "o7": sb(8, U16),
+    "wc0": sb(512, BF), "wq0": sb(512, BF), "wb0": sb(512, BF), "et": sb(2048, BF),
+    "qwc": sb(128, Q4), "swc": sb(128, U8), "qwq": sb(128, Q4), "swq": sb(128, U8), "qwb": sb(128, Q4), "swb": sb(128, U8),
+    "qe": sb(512, Q4), "se": sb(512, U8),
+    "oe": sb(120, U16), "pq": sb(120, F32), "pq2": sb(32, F32), "ql": sb(32, U16), "mk": sb(480, BF),
+    "d0": sb(1920, BF), "y0": sb(1924, BF), "gq": sb(480, BF), "ta0": sb(480, BF), "fw0": sb(480, BF), "bw0": sb(480, BF), "vr0": sb(480, BF),
+    "e": sb(1280, BF), "yy": sb(1284, F16), "ys": sb(12, F32), "vv": sb(1280, F16), "q4": sb(1280, F16),
+    "ta": sb(320, F16), "fw": sb(320, F16), "bw": sb(320, F16), "vr": sb(320, F16),
+    "nf": sb(480, BF), "pz": sb(960, F16), "pw": sb(960, F16), "cs": sb(4, F32), "od": sb(32, U16), "pk": sb(480, F32),
+    "win0": sb(768, F32), "win1": sb(768, F32), "win2": sb(768, F32),
+    "w4": sb(224, F32), "wi": sb(112, I32), "o2": sb(56, U16), "o1": sb(56, U16), "p4": sb(288, F32), "l4": sb(72, U16),
     "two": sb(896, BF), "bb": sb(896, BF), "qbb": sb(256, Q4), "sbq": sb(256, U8), "hh": sb(896, BF),
     "qh0": sb(224, Q4), "sh0": sb(224, U8), "qh1": sb(192, Q4), "sh1": sb(192, U8),
-    "thr": sb(224, F32), "nh": sb(224, BF), "nc": sb(448, F16), "ncw": sb(448, F16), "la": sb(48, F32),
-    "ol": sb(14, U16), "val": sb(224, F32), "lwin": sb(832, F32), "lw": sb(96, F32), "li": sb(48, I32), "ko": sb(24, U16),
+    "thr": sb(224, F32), "nh": sb(224, BF), "nc": sb(224, BF), "nz": sb(448, F16), "nw": sb(448, F16),
+    "ol": sb(14, U16), "val": sb(224, F32), "lwin": sb(512, F32), "lw": sb(96, F32), "li": sb(48, I32), "ko": sb(24, U16),
     "ls0": sb(48, U16), "ls1": sb(48, U16), "t1": sb(224, F16), "reg": sb(224, F16), "idx": sb(224, F16), "iw": sb(224, F16),
     "rq0": sb(224, Q4), "rs0": sb(224, U8), "rl0": sb(48, U16), "rq1": sb(192, Q4), "rs1": sb(192, U8), "rl1": sb(48, U16),
     "mq": sb(192, Q4), "ms": sb(192, U8), "ml": sb(48, U16), "dst": sb(896, BF),
     "tl": sb(1152, BF), "qt": sb(288, Q4), "st": sb(288, U8), "ot": sb(20, U16), "hm": sb(640, F32), "occb": sb(288, F32), "yb": sb(288, F32),
     "pr": ("psum", [128, 2048], F32), "ps": ("psum", [128, 2048], F32),
 }
+SHARED = {}
+for whole, names in (("hf", "ta fw bw vr pz pw nz nw t1 reg idx iw"), ("win", "win0 win1 win2"), ("tm", "tm1 tm2 pat cs pq pq2")):
+    at = 0
+    for name in names.split():
+        SHARED[name] = (whole, at, SCRATCH[name][1][1])
+        at += (SCRATCH[name][1][1] + 31) // 32 * 32
+        kind = SCRATCH.pop(name)[2]
+    SCRATCH[whole] = sb(at, kind)
 SEMAPHORES = ["sv_", "sa_", "sp_", "sg_", "lu", "lx0", "lx1", "lw_", "lp_", "lv", "out",
               "aq0", "as0", "al0", "aq1", "as1", "al1", "mq_", "ms_", "ml_", "loc"]
-(PI, PQ, G4, H4, GM, QOFF, FIX16, FIX4, NFG, TCOL, C1, C20, C21, C22, C1X, DFX, WT, WT0, G1, AOF, KOF, IFX, F256, TMP, POW, TM2, FXX) = range(27)
+(PI, PQ, G4, H4, QOFF, FIX4, TCOL, ODX, FW, C1, C2, C3, C4, WT, WT0, WQ, AOF, KOF, IFX, F256, TMP, TM2, TM3, POW, G8, K0, K1, K2, K3) = range(29)
 
 
 def relay_of(src, dst, k, topo):
@@ -202,12 +215,17 @@ def rank_program(g, core, T, topo):
     own = []
 
     def R(name, lo=0, hi=None, step=1):
-        n = SCRATCH[name][1][1]
-        hi = n if hi is None else hi
+        name, at, n = SHARED.get(name) or (name, 0, SCRATCH[name][1][1])
+        lo, hi = at + lo, at + (n if hi is None else hi)
         ap = T[name][:, lo:hi] if step == 1 else T[name][:, lo:hi:step]
         if SCRATCH[name][0] == "psum":
             return (ap, [(name, lo // 512 * 512, lo // 512 * 512 + 512, 1, True)], hi - lo)
         return (ap, [(name, lo, hi, step, False)], len(range(lo, hi, step)))
+
+    def back(name, lo, hi):
+        name, at, n = SHARED.get(name) or (name, 0, 0)
+        lo, hi = at + lo, at + hi
+        return (T[name][:, hi - 1:(lo - 1 if lo else None):-1], [(name, lo, hi, 1, False)], hi - lo)
 
     def col(c):
         return R("col", c, c + 1)
@@ -336,266 +354,301 @@ def rank_program(g, core, T, topo):
     load("s", R("wp"), T.ws[:], "lp_", 4500)
     load("s", R("vt"), T.v[:], "lv", 5000)
 
-    iota(R("ii", 16, 17), [[0, 1]], 0, 1, False)
+    iota(R("ii", 40, 41), [[0, 1]], 0, 1, False)
     iota(R("jh"), [[1, 35], [0, 4]], -3, 0)
+    iota(R("jq"), [[8, 8], [0, 4], [-1, 4]], 0, 0)
     iota(R("iof", 0, 128), [[1, 128]], 0, 0)
-    iota(R("ii", 0, 16), [[1, 16]], 128, -1, False)
-    for k in range(128, NID, 272):
-        iota(R("iof", k, k + 272), [[1, 272]], k, 0)
+    iota(R("iof", 128, 224), [[1, 96]], 128, 0)
+    iota(R("ii", 0, 32), [[1, 32]], 256, -2, False)
+    iota(R("cq"), [[64, 32]], 0, 0)
+    for a, b, first, step in RUNS:
+        iota(R("idr", a, b), [[-step, b - a]], -first, 0)
+    for k in (0, 320):
+        iota(R("idp", k, min(k + 320, 608)), [[8192, min(320, 608 - k)]], 8192 * (BASE[1] + k), 0)
     ms(R("one"), 1.0)
-    for k in range(2):
-        keep(R("r4", 320 * k, 320 * k + 320), [[0, 80], [1, 4]], ALU.not_equal, 0, 0)
-        keep(R("r16", 496 * k, 496 * k + 496), [[0, 31], [1, 16]], ALU.not_equal, 0, 0)
-    iota(R("uc"), [[16, 32]], 256, 1)
-    iota(R("pos4"), [[4, 496]], 0, 0)
-    iota(R("ii", 24, 32), [[16, 8]], 7, 0, False)
+    keep(R("r16"), [[0, 14], [1, 16]], ALU.not_equal, 0, 0)
+    keep(R("r4"), [[0, 128], [1, 4]], ALU.not_equal, 0, 0)
+    iota(R("ii", 32, 40), [[16, 8]], 7, 0, False)
     iota(R("jg"), [[4, 8], [0, 16]], 0, 0)
     iota(R("wb0"), [[0, 512]], 0, 0)
     iota(R("bt"), [[0, 896]], 0, 0)
     for b in range(4):
         keep(R("et", 512 * b, 512 * b + 512), [[0, 1], [1, 512]], ALU.is_equal, -b, -4)
         quant("qe", "se", 128 * b, 128 * b + 128, R("et", 512 * b, 512 * b + 512))
-    p_ = R("ii", 16, 17)
-    ts(R("ij", 24, 25), p_, 15, ALU.bitwise_and)
-    ts(R("ij", 25, 26), p_, 3, ALU.bitwise_and)
-    ts(R("ij", 26, 27), p_, 2, ALU.logical_shift_right, 28, ALU.bitwise_and)
-    ts(R("ij", 27, 28), p_, 2, ALU.logical_shift_right, 3, ALU.bitwise_and)
-    ts(R("ij", 28, 29), p_, 4, ALU.logical_shift_right, 1, ALU.bitwise_and)
-    cp(R("col", PI, GM + 1), R("ij", 24, 29))
+    p_ = R("ii", 40, 41)
+    ts(R("ij", 40, 41), p_, 15, ALU.bitwise_and)
+    ts(R("ij", 41, 42), p_, 3, ALU.bitwise_and)
+    ts(R("ij", 42, 43), p_, 2, ALU.logical_shift_right, 28, ALU.bitwise_and)
+    ts(R("ij", 43, 44), p_, 2, ALU.logical_shift_right, 3, ALU.bitwise_and)
+    cp(R("col", PI, H4 + 1), R("ij", 40, 44))
     act(col(POW), col(PI), ACT.Exp, math.log(2.0))
     ts(col(QOFF), col(PQ), -16.0, ALU.mult, 48.0, ALU.add)
     ms(R("bt0", 160, 512), 0.0)
-    ms(R("tab", 128, 256), 0.0)
-    ms(R("tab", 512, 768), 0.0)
-    ms(R("ys", 0, 4), -512.0)
+    ms(R("y0", 0, 4), 256.0)
     ts(col(TCOL), col(PI), 48.0, ALU.add)
-    ts(col(FIX16), col(PI), 14.5, ALU.is_lt, B, ALU.mult)
     ts(col(FIX4), col(H4), 2.5, ALU.is_lt, B, ALU.mult)
-    cp(R("yy", 0, 4), R("ys", 0, 4))
-    ts(R("tab", 0, 128), R("iof", 0, 128), col(TCOL), ALU.is_equal, -1.0, ALU.mult)
-    ts(R("ij", 0, 16), R("ii", 0, 16), 15, ALU.bitwise_and)
-    ts(R("ii", 18, 22), R("iof", 4, 8), col(H4), ALU.subtract)
-    ts(R("ii", 22, 24), R("iof", 2, 4), col(GM), ALU.subtract)
+    ts(R("tm1", 36, 37), col(PI), 14.5, ALU.is_lt, -B2, ALU.mult)
+    ts(R("sg", 0, 128), R("iof", 0, 128), col(TCOL), ALU.is_equal, -9.0, ALU.mult)
+    ts(R("tab", 0, 128), R("sg", 0, 128), 1.0, ALU.add)
+    ts(R("ij", 0, 32), R("ii", 0, 32), 31, ALU.bitwise_and)
+    ts(R("ii", 42, 46), R("iof", 4, 8), col(H4), ALU.subtract)
+    ts(R("ij", 32, 36), R("ii", 42, 46), 3, ALU.bitwise_and)
     ts(col(TMP), col(PI), 7.0, ALU.is_equal, 128.0, ALU.mult)
-    ts(R("ij", 16, 20), R("ii", 18, 22), 3, ALU.bitwise_and)
-    ts(R("ij", 20, 22), R("ii", 22, 24), 1, ALU.bitwise_and)
     ts(col(WT0), col(PI), 5.5, ALU.is_lt, col(POW), ALU.mult)
-    tt(col(WT), col(WT0), col(TMP), ALU.add)
+    ts(col(TM3), col(PI), 3.5, ALU.is_gt, 0.0625, ALU.mult)
+    tt(col(WQ), col(WT0), col(TM3), ALU.mult)
+    lin(WT, WT0, 1.0, col(TMP))
+    lin(G8, G4, 2.0, 0.0)
+    ts(R("col", K0, K3 + 1), R("iof", 0, 4), -1.0, ALU.mult, col(G8), ALU.add)
     for t in range(4):
         ts(R("wc0", t, 512, 4), R("jh", 12 - 4 * t, 140 - 4 * t), col(G4), ALU.is_equal, col(WT0), ALU.mult)
+        ts(R("wq0", t, 512, 4), R("jq"), col(K0 + t), ALU.is_equal, col(WQ), ALU.mult)
     quant("qwc", "swc", 0, 128, R("wc0"))
+    quant("qwq", "swq", 0, 128, R("wq0"))
     ts(R("wb0", 0, 512, 4), R("jg"), col(G4), ALU.is_equal, col(WT), ALU.mult)
     quant("qwb", "swb", 0, 128, R("wb0"))
+    scan(R("nj"), R("one", 0, 480), R("one", 0, 480), -255.0, ALU.mult, ALU.subtract)
+    act(R("tab", 128, 256), R("one", 0, 128), ACT.Copy)
+    act(R("tab", 512, 768), R("one", 0, 256), ACT.Copy)
     for r in (2, 3):
         act(R("tab", 128 * r, 128 * r + 128), R("tab", 0, 128), ACT.Copy)
-    for k in range(128, NID, 272):
-        act(R("ids", k, k + 272), R("iof", k, k + 272), ACT.Copy)
-    for k in range(0, NID, 304):
-        act(R("pfr", k, k + 304), R("iof", k, k + 304), ACT.Copy, 1.0 / 2048)
-    act(R("kfr"), R("iof", 0, 224), ACT.Copy, 1.0 / 256)
-    lin(NFG, GM, B, -B)
-    lin(DFX, FIX16, 1.0, -1.0)
-    lin(TM2, FIX4, 4.0, col(PQ))
-    lin(C1X, PQ, 1.0, -4.0 * OFF)
+    for k in (0, 240):
+        act(R("idp0", k, k + 240), R("idr", k, k + 240), ACT.Copy, -8192.0)
+    for k in (0, 320):
+        act(R("ids", k, min(k + 320, 608)), R("idp", k, min(k + 320, 608)), ACT.Copy, 1.0 / 8192)
+    act(R("kfr"), R("iof"), ACT.Copy, 1.0 / 256)
+    act(col(ODX), R("tm1", 36, 37), ACT.Identity, 1.0, -1.0)
+    lin(TM2, PI, 4.0, col(FIX4))
+    act(R("cq"), R("cq"), ACT.Identity, 1.0, col(TM2))
+    lin(FW, FIX4, BW, 0.0)
+    lin(C1, PQ, 1.0, 8192.0)
+    lin(TM2, PQ, 2048.0, col(FW))
+    lin(C2, TM2, 1.0, 860.0)
+    lin(C3, TM2, 1.0, -8192.0 * (BASE[2] - 4))
+    lin(C4, FIX4, -4.0, col(PQ))
     lin(IFX, FIX4, 1.0, col(QOFF))
-    lin(C1, TM2, 1.0, -4.0 * OFF)
     lin(F256, FIX4, 256.0, 0.0)
-    lin(FXX, FIX4, 4.0, 0.0)
     lin(KOF, PQ, 224.0, 0.0)
-    lin(G1, GM, 64.0, col(C1))
     lin(AOF, IFX, 1.0, 128.0 - 0.44)
+    ts(R("tm1", 0, 32), R("ij", 0, 32), 0.0, ALU.is_equal, 4 * B2, ALU.mult)
+    ts(R("tm2", 0, 32), R("ij", 0, 32), 2.0, ALU.is_equal, -B2, ALU.mult)
+    tt(R("c32", 0, 32), R("tm1", 0, 32), R("tm2", 0, 32), ALU.add)
+    for a, b in ((32, 64), (64, 128), (128, 256), (256, 448)):
+        act(R("c32", a, b), R("c32", 0, b - a), ACT.Copy)
+    ts(R("tm1", 32, 36), R("ij", 32, 36), 0.0, ALU.is_equal, 4 * B, ALU.mult)
+    ts(R("tm2", 32, 36), R("ij", 32, 36), 1.0, ALU.is_equal, -B, ALU.mult)
+    tt(R("pat"), R("tm1", 32, 36), R("tm2", 32, 36), ALU.add)
+    for k in range(4):
+        act(R("c4", k, 224, 4), R("one", 0, 56), ACT.Copy, R("pat", k, k + 1))
+    act(R("c4x"), R("c4"), ACT.Copy, BW)
+    act(R("pool", 0, 16), R("one", 0, 16), ACT.Copy, 0.0)
+    act(R("sm", 0, 16), R("one", 0, 16), ACT.Copy, 0.0)
+    act(R("tl", 256, 512), R("one", 0, 256), ACT.Copy, 0.0)
+    act(R("tl", 640, 1152), R("one", 0, 512), ACT.Copy, 0.0)
+    act(R("occb", NA + PR[2], 288), R("one", 0, 64), ACT.Copy, 0.0)
     for t in range(3):
-        lin(C20 + t, G1, 1.0, 4.0 * (BASE[t] - 16) - 0.33)
-    ts(R("tm1", 0, 22), R("ij", 0, 22), 0.0, ALU.is_equal, 4 * B, ALU.mult)
-    ts(R("tm2", 0, 22), R("ij", 0, 22), 1.0, ALU.is_equal, -B, ALU.mult)
-    tt(R("pat", 0, 22), R("tm1", 0, 22), R("tm2", 0, 22), ALU.add)
-    for name, n, k0, per in (("c2", 64, 20, 2), ("c4", 224, 16, 4), ("c16", 496, 0, 16)):
-        for k in range(per):
-            act(R(name, k, n, per), R("one", 0, n // per), ACT.Copy, R("pat", k0 + k, k0 + k + 1))
-    act(R("c4x"), R("c4"), ACT.Copy, 4.0)
-    ms(R("pool", 0, 16), 0.0)
-    ms(R("tl", 256, 512), 0.0)
-    ms(R("tl", 640, 1152), 0.0)
-    ms(R("occb", NA + PR[2], 288), 0.0)
-    ts(R("q4", 0, 64), R("one", 0, 64), 0.0, ALU.mult)
-    ts(R("q4", 64 + 1920, 64 + 1984), R("one", 0, 64), 0.0, ALU.mult)
-    act(R("win", 0, 256), R("one", 0, 256), ACT.Copy, FILL)
-    for k in range(0, 1920, 480):
-        act(R("pool", 16 + k, 496 + k), R("xt", k, k + 480), ACT.Copy, 0.5)
+        act(R("win%d" % t, 0, PR[t]), R("one", 0, PR[t]), ACT.Copy, -1.0)
+    for a, b, first, step in RUNS:
+        if step == 1:
+            for k in range(a, b, 56):
+                act(R("pool", 4 * (first + k), 4 * (first + k + 56)), R("xt", 4 * k, 4 * (k + 56)), ACT.Copy, 0.5)
+        else:
+            for t in range(4):
+                act(R("pool", 4 * first + t, 4 * (first + step * (b - a)), 4 * step), R("xt", 4 * a + t, 4 * b, 4), ACT.Copy, 0.5)
     quant("qu", "su", 0, 128, R("ut"))
     quant("qv", "sv", 0, 128, R("vt"))
-    cp(R("o7"), R("ii", 24, 32))
+    cp(R("o7"), R("ii", 32, 40))
     picked(R("qu7"), R("qu"), R("o7"), True)
     picked(R("su7"), R("su"), R("o7"), False)
-    S7, CD = 512, 1024
-
-    def marks(offs, s0, s1):
-        act(R("e", 4 * s0, 4 * s1), ind(R("tab"), offs), ACT.Copy)
-        ts(R("d0", 4 * s0, 4 * s1), R("e", 4 * s0, 4 * s1), 5.0, ALU.mult, 1.0, ALU.add)
-
-    def shared_marks(offs, s0):
-        a = 4 * s0
-        ts(R("d0", a, a + 192), ind(R("tab"), R(offs, 0, 12)), 5.0, ALU.mult, 1.0, ALU.add)
-        marks(R(offs, 12, 24), s0 + 48, s0 + 96)
-        act(R("e", a, a + 192), R("d0", a, a + 192), ACT.Identity, 0.2, -0.2)
 
     state = [0]
 
     def rows(t, s0, s1):
         a, b, k = 4 * s0, 4 * s1, state[0]
+        z = BASE[t] - BASE[1]
         for q in range(4):
-            scan(R("yy", 4 + a + q, 4 + b, 4), R("d0", a + q, b, 4), R("ids", BASE[t] + s0, BASE[t] + s1), R("ys", k + q, k + q + 1), ALU.mult, ALU.min)
+            scan(R("yy", 4 + a + q, 4 + b, 4), R("d0", a + q, b, 4), R("ids", z + s0, z + s1), R("ys", k + q, k + q + 1), ALU.mult, ALU.min)
         state[0] = (k + 4) % 12
         cp(R("ys", state[0], state[0] + 4), R("yy", b, b + 4))
         scan(R("vv", a, b), R("yy", a, b), R("e", a, b), 0.0, ALU.max, ALU.mult)
-        scan(R("q4", 64 + a, 64 + b), R("r4", 0, b - a), R("vv", a, b), 0.0, ALU.mult, ALU.min)
+        scan(R("q4", a, b), R("r4", 0, b - a), R("vv", a, b), 0.0, ALU.mult, ALU.min)
 
-    def number(s0, s1, last):
-        n1 = (s1 - s0) // 32
-        n2 = n1 + (1 if last else 0)
-        m0, m = s0 // 16, n1 + n2
-        z = 32 * m0
-        tr(R("tt", z, z + 32 * n2), R("q4", 3 + 4 * s0, 4 * s0 + 128 * n2, 4))
-        tr(R("tt", z + 32 * n2, z + 32 * m), R("q4", 67 + 4 * s0, 64 + 4 * s1, 4))
-        scan(R("rr", z, z + 32 * m), R("r16", 0, 32 * m), R("tt", z, z + 32 * m), 0.0, ALU.mult, ALU.min)
-        y = 2 * m0
-        pick(("sel", y), "c2", R("rr", z + 15, z + 32 * m, 16), 2 * m)
-        ts(R("pw", m0, m0 + m, 2), R("sel", y + 1, y + 2 * n2, 2), -1.0, ALU.mult, col(NFG), ALU.add)
-        ts(R("pw", m0 + 1, m0 + m, 2), R("sel", y + 2 * n2 + 1, y + 2 * m, 2), -1.0, ALU.mult, col(NFG), ALU.add)
-        o, a, b = R("pw", m0, m0 + m), 16 * m0, 16 * (m0 + m)
-        act(R("fb", a, b), ind(R("iof"), o), ACT.Sign)
-        tt(R("pk", a, b), ind(R("pfr"), o), R("pos4", a, b), ALU.add)
-        ts(R("nf", m0, m0 + m), o, 0.0, ALU.is_equal)
-        scan(R("cum", a, b), R("one", 0, b - a), R("fb", a, b), R("cs", 0, 1) if s0 else 0.0, ALU.mult, ALU.add)
-        tt(R("zz", m0, m0 + m), R("nf", m0, m0 + m), R("uc", m0, m0 + m), ALU.mult)
-        pick(("cw", a), "c16", R("cum", a, b), b - a)
+    def places(z, w, o, nf, s0, s1, carry):
+        scan(R(z, 2 * s0, 2 * s1, 2), nf, R("one", 0, s1 - s0), carry, ALU.add, ALU.subtract)
+        scan(R(z, 2 * s0 + 1, 2 * s1, 2), nf, R("nj", s0, s1), 0.0, ALU.max, ALU.mult)
+        pick((w, 2 * s0), "c32", R(z, 2 * s0, 2 * s1), 2 * (s1 - s0), B2)
+        ts(R(o, s0 // 16, s1 // 16), R(w, 2 * s0 + 31, 2 * s1, 32), -1.0, ALU.mult, col(ODX), ALU.add)
+
+    def number(t, s0, s1, last):
+        x = "" if t else "0"
+        n = s1 - s0
+        tr(R("ta" + x, s0, s1), R("q4", 4 * s0 + 3, 4 * s1, 4) if t else R("gq", s0, s1))
+        scan(R("fw" + x, s0, s1), R("r16", 0, n), R("ta" + x, s0, s1), 0.0, ALU.mult, ALU.min)
+        scan(back("bw" + x, s0, s1), R("r16", 0, n), back("fw" + x, s0, s1), 0.0, ALU.mult, ALU.min)
+        v = R("vr" + x, s0, s1)
+        tr(v, R("bw" + x, s0, s1))
+        if t:
+            ts(R("nf", s0, s1), v, -0.5, ALU.is_gt)
+        else:
+            act(R("nf", s0, s1), v, ACT.Relu, 1.0, 1.0)
+        k = state[1]
+        places("pz", "pw", "od", R("nf", s0, s1), s0, s1, R("cs", k, k + 1) if s0 else 0.0)
         if not last:
-            cp(R("cs", 0, 1), R("cum", b - 1, b))
-        tt(R("ds", m0, m0 + m), R("cw", a + 15, b, 16), R("zz", m0, m0 + m), ALU.add)
-        ts(R("od", m0, m0 + m), R("ds", m0, m0 + m), col(DFX), ALU.add)
-        scat(R("win"), R("od", m0, m0 + m), R("pk", a, b))
+            state[1] = 1 - k
+            cp(R("cs", 1 - k, 2 - k), R("pz", 2 * s1 - 2, 2 * s1 - 1))
+        z = BASE[t] - BASE[1]
+        mine = R("idp", z + s0, z + s1) if t else R("idp0", s0, s1)
+        if t < 2:
+            scan(R("pk", s0, s1), v, mine, 0.0, ALU.min, ALU.add)
+            mine = R("pk", s0, s1)
+        else:
+            pick(("p4", s0), "c4", v, n)
+            ts(R("l4", s0 // 4, s1 // 4), R("p4", s0 + 3, s1, 4), -4.0, ALU.mult, col(C4), ALU.add)
+            for a in range(s0, s1, 48):
+                tt(R("sm", 16 + 4 * a, 208 + 4 * a), ind(R("pool", 0, 4 * (BASE[t] + s1)), R("l4", a // 4, a // 4 + 12)),
+                   R("tok", 4 * a, 4 * a + 192), ALU.add)
+        scat(R("win%d" % t), R("od", s0 // 16, s1 // 16), mine)
 
-    def fire(t, n, cut):
+    state.append(0)
+
+    def fire(t, n):
         P = PR[t]
-        top = 4 * (BASE[t] + n - OFF)
         m = P // 4
-        pick(("w4", 0), "c4x", R("win", 0, P), P, 4 * B)
-        ts(R("o2", 0, m), R("w4", 3, P, 4), col(C20 + t), ALU.add)
-        ts(R("wi", 0, m), R("w4", 3, P, 4), col(FXX), ALU.add, 2048.0, ALU.mult)
+        pick(("w4", 0), "c4x", R("win%d" % t, 0, P), P, BW * B)
+        if t == 2:
+            ts(R("o1", 0, m), R("w4", 3, P, 4), col(C3), ALU.add, 1.0 / 2048, ALU.mult)
+            act(R("bb", 0, 320), ind(R("sm"), R("o1", 0, 20)), ACT.Copy)
+            cp(R("bb", 320, 640), ind(R("sm"), R("o1", 20, 40)))
+            quant("qbb", "sbq", 0, P, R("bb", 0, 4 * P))
+            for c in range(4):
+                mm(R("pr", 512 * c, 512 * c + P), "wq", "wp", 128 * c, "qbb", "sbq", 0, P)
+            return
+        top = 4 * (BASE[1] + n if t else BASE[1])
+        ts(R("o2", 0, m), R("w4", 3, P, 4), col(C2), ALU.add, 1.0 / 2048, ALU.mult)
+        ts(R("wi", 0, m), R("w4", 3, P, 4), col(FW), ALU.add)
         ts(R("wi", 56, 56 + m), R("wi", 0, m), 2047, ALU.bitwise_and)
-        ts(R("o1", 0, m), R("wi", 56, 56 + m), 4.0, ALU.mult, col(C1X), ALU.add)
-        for a, b in ((0, 12), (12, 32), (32, m)) if cut else ((0, 10), (10, 24), (24, m)):
+        ts(R("o1", 0, m), R("wi", 56, 56 + m), -4.0, ALU.mult, col(C1), ALU.add)
+        for a, b in ((0, 12), (12, 32), (32, m)):
             act(R("two", 16 * a, 16 * b), ind(R("pool", 0, top), R("o2", a, b)), ACT.Copy)
             tt(R("bb", 16 * a, 16 * b), ind(R("pool", 0, top), R("o1", a, b)), R("two", 16 * a, 16 * b), ALU.add)
-            if cut and a:
+            if a:
                 k = 0 if b == 32 else 128
                 quant("qbb", "sbq", k, k + 128, R("bb", 4 * (4 * b - 128), 16 * b))
                 for c in range(4):
                     mm(R("ps" if k else "pr", 512 * c, 512 * c + 128), "wq", "wp", 128 * c, "qbb", "sbq", k, k + 128)
-                    if not k:
-                        act(R("hh", c, 512, 4), R("pr", 512 * c, 512 * c + 128), ACT.Relu, 0.03125)
-        if not cut:
-            quant("qbb", "sbq", 0, P, R("bb", 0, 4 * P))
-            for c in range(4):
-                mm(R("pr", 512 * c, 512 * c + P), "wq", "wp", 128 * c, "qbb", "sbq", 0, P)
 
-    quant("qx", "sx", 0, 160, R("xt", 0, 640))
-    mm(R("ps", 0, 160), "qu", "su", 0, "qx", "sx", 0, 160)
-    ts(R("bt0", 0, 160), R("ps", 0, 160), 0.0, ALU.is_gt)
-    quant("qb", "sbb", 0, 128, R("bt0"))
-    mm(R("ps", CD, CD + 128), "qwc", "swc", 0, "qb", "sbb", 0, 128)
-    ts(R("oe", 0, 40), R("ps", CD, CD + 40), col(QOFF), ALU.add)
-    quant("qx", "sx", 160, 480, R("xt", 640, 1920))
-    mm(R("ps", 512, 832), "qu", "su", 0, "qx", "sx", 160, 480)
-    ts(R("bt0", 160, 480), R("ps", 512, 832), 0.0, ALU.is_gt)
-    quant("qb", "sbb", 128, 256, R("bt0"))
-    mm(R("ps", 1536, 1664), "qwc", "swc", 0, "qb", "sbb", 128, 256)
-    ts(R("oe", 40, 120), R("ps", 1576, 1656), col(QOFF), ALU.add)
+    for h, (a, b) in enumerate(((0, 160), (160, 480))):
+        quant("qx", "sx", a, b, R("xt", 4 * a, 4 * b))
+        s = R("ps", 512 * h, 512 * h + b - a)
+        mm(s, "qu", "su", 0, "qx", "sx", a, b)
+        if h:
+            act(R("sg"), s, ACT.Sign)
+            act(R("bt0", a, b), R("sg"), ACT.Relu)
+        else:
+            ts(R("bt0", a, b), s, 0.0, ALU.is_gt)
+        quant("qb", "sbb", 128 * h, 128 * h + 128, R("bt0"))
+        z = 1024 + 512 * h
+        mm(R("ps", z, z + 128), "qwc", "swc", 0, "qb", "sbb", 128 * h, 128 * h + 128)
+        mm(R("pr", 512 * h, 512 * h + 128), "qwq", "swq", 0, "qb", "sbb", 128 * h, 128 * h + 128)
+        ts(R("oe", a // 4, b // 4), R("ps", z + a // 4, z + b // 4), col(QOFF), ALU.add)
+        pick(("pq", a // 4), "c4", R("pr", 512 * h + a // 4, 512 * h + b // 4), (b - a) // 4)
+        tt(R("pq2", a // 16, b // 16), R("pq", a // 4 + 3, b // 4, 4), R("cq", a // 16, b // 16), ALU.add)
+        cp(R("ql", a // 16, b // 16), R("pq2", a // 16, b // 16))
     for s0 in (0, 160, 320):
-        marks(R("oe", s0 // 4, s0 // 4 + 40), s0, s0 + 160)
-        rows(0, s0, s0 + 160)
-    number(0, 320, False)
-    number(320, 480, True)
+        s1 = s0 + 160
+        a, b = 4 * s0, 4 * s1
+        act(R("d0", a, b), ind(R("tab", 0, 128), R("oe", s0 // 4, s1 // 4)), ACT.Copy)
+        for q in range(4):
+            scan(R("y0", 4 + a + q, 4 + b, 4), R("d0", a + q, b, 4), R("idr", s0, s1), R("y0", a + q, a + q + 1), ALU.mult, ALU.max)
+        o = R("ql", s0 // 16, s1 // 16)
+        act(R("mk", s0, s1), ind(R("d0", 0, b), o), ACT.Relu, -0.125)
+        tt(R("gq", s0, s1), ind(R("y0", 0, b), o), R("mk", s0, s1), ALU.mult)
+        number(0, s0, s1, s1 == C)
+    act(R("ys", 0, 4), R("y0", 4 * C, 4 * C + 4), ACT.Copy, -1.0)
     n = C
     for t in range(2):
         P = PR[t]
         qh, sh, ls, rl = "qh%d" % t, "sh%d" % t, "ls%d" % t, "rl%d" % t
-        w = R("win", 0, P)
-        fire(t, n, True)
+        w = R("win%d" % t, 0, P)
+        act(R("lwin", 0, L), R("one", 0, L), ACT.Copy, 0.0)
+        fire(t, n)
         act(R("thr", 0, P), w, ACT.Relu, -1e26)
-        act(R("nh", 0, P), w, ACT.Relu, -0.125)
+        act(R("nh", 0, P), w, ACT.Relu, -512.0)
         n = P + L
-        lo = 256 - P
-        quant(qh, sh, 0, 128, R("hh", 0, 512))
-        mm(R("pr", 0, 128), "qu7", "su7", 0, qh, sh, 0, 128)
-        mm(R("pr", 512, 640), "qu", "su", 0, qh, sh, 0, 128)
-        tt(R("nc", 0, 128), R("pr", 0, 128), R("thr", 0, 128), ALU.is_le)
-        act(R("sg", 0, 128), R("pr", 512, 640), ACT.Sign)
-        for b in (0, 2):
-            ts(R("hh", 512 + b, 4 * P, 4), R("ps", 512 * b + lo, 512 * b + 128), 0.0, ALU.max, 0.03125, ALU.mult)
-            act(R("hh", 513 + b, 4 * P, 4), R("ps", 512 * b + 512 + lo, 512 * b + 640), ACT.Relu, 0.03125)
-        quant(qh, sh, P - 128, P, R("hh", 4 * (P - 128), 4 * P))
-        mm(R("ps", 0, 128), "qu", "su", 0, qh, sh, P - 128, P)
-        mm(R("ps", S7, S7 + 128), "qu7", "su7", 0, qh, sh, P - 128, P)
-        tt(R("nc", 128, P), R("ps", S7 + lo, S7 + 128), R("thr", 128, P), ALU.is_le)
-        act(R("sg", 128, P), R("ps", lo, 128), ACT.Sign)
-        act(R("bt", 0, 512, 4), R("sg", 0, 128), ACT.Relu)
-        act(R("bt", 512, 4 * P, 4), R("sg", 128, P), ACT.Relu)
+        ad = []
+        for a, b, y in ((0, 128, "pr"), (128, P, "ps")):
+            lo = 128 - (b - a)
+            for c in range(4):
+                o, i = R("hh", 4 * a + c, 4 * b, 4), R(y, 512 * c + lo, 512 * c + 128)
+                if a and c % 2 == 0:
+                    ts(o, i, 0.0, ALU.max, 0.03125, ALU.mult)
+                else:
+                    act(o, i, ACT.Relu, 0.03125)
+            quant(qh, sh, b - 128, b, R("hh", 4 * (b - 128), 4 * b))
+            mm(R(y, 0, 128), "qu", "su", 0, qh, sh, b - 128, b)
+            mm(R(y, 512, 640), "qu7", "su7", 0, qh, sh, b - 128, b)
+            if a:
+                ts(R("bt", 4 * a, 4 * b, 4), R(y, lo, 128), 0.0, ALU.is_gt)
+            else:
+                act(R("sg", a, b), R(y, lo, 128), ACT.Sign)
+                act(R("bt", 4 * a, 4 * b, 4), R("sg", a, b), ACT.Relu)
+            tt(R("nc", a, b), R(y, 512 + lo, 640), R("thr", a, b), ALU.is_le)
+            quant("qb", "sbb", a, a + 128, R("bt", 4 * (b - 128), 4 * b))
+            mm(R(y, 1024, 1152), "qwb", "swb", 0, "qb", "sbb", a, a + 128)
+            ad.append(R(y, 1024 + lo, 1152))
+            places("nz", "nw", "ol", R("nc", a, b), a, b, R("cs", 2, 3) if a else 0.0)
+            if not a:
+                cp(R("cs", 2, 3), R("nz", 2 * b - 2, 2 * b - 1))
+            tt(R("val", a, b), ad[-1], R("kfr", a, b), ALU.add)
+            scat(R("lwin"), R("ol", a // 16, b // 16), R("val", a, b))
         s = send(sh, "s", t, [send(qh, "q", t, own)])
         nb = BASE[t + 1]
-        act(R("lwin", 0, L), R("one", 0, L), ACT.Copy, 0.0)
         act(R("yy", 0, 4), R("ys", state[0], state[0] + 4), ACT.Copy)
-        act(R("q4", 64 + 4 * n, 128 + 4 * n), R("one", 0, 64), ACT.Copy, 0.0)
-        act(R("win", 0, 256), R("one", 0, 256), ACT.Copy, FILL)
         for k in range(0, 4 * P, 2 * P):
-            act(R("pool", 4 * (nb - OFF) + k, 4 * (nb - OFF) + k + 2 * P), R("hh", k, k + 2 * P), ACT.Copy, 0.5)
-        m = P // 16
-        scan(R("nc", P, 2 * P), R("one", 0, P), R("nc", 0, P), 0.0, ALU.add, ALU.subtract)
-        pick(("ncw", 0), "c16", R("nc", 0, P), P)
-        pick(("ncw", P), "c16", R("nc", P, 2 * P), P)
-        ts(R("la", 0, m), R("ncw", 15, P, 16), col(FIX16), ALU.add)
-        quant("qb", "sbb", 0, P, R("bt", 0, 4 * P))
-        mm(R("ps", CD, CD + P), "qwb", "swb", 0, "qb", "sbb", 0, P)
-        tt(R("la", 16, 16 + m), R("la", 0, m), R("uc", 0, m), ALU.mult)
-        tt(R("la", 32, 32 + m), R("ncw", P + 15, 2 * P, 16), R("la", 16, 16 + m), ALU.add)
-        ts(R("ol", 0, m), R("la", 32, 32 + m), col(DFX), ALU.add)
-        tt(R("val", 0, P), R("ps", CD, CD + P), R("kfr", 0, P), ALU.add)
-        scat(R("lwin"), R("ol", 0, m), R("val", 0, P))
+            act(R("pool", 4 * nb + k, 4 * nb + k + 2 * P), R("hh", k, k + 2 * P), ACT.Copy, 0.5)
+            if t:
+                act(R("tok", k, k + 2 * P), R("hh", k, k + 2 * P), ACT.Copy, 0.5)
         pick(("lw", 0), "c4", R("lwin", 0, L), L)
         ts(R(ls, 0, 24), R("lw", 3, L, 4), col(AOF), ALU.add)
         ts(R(ls, 24, 48), R("lw", 3, L, 4), 256.0, ALU.mult, col(F256), ALU.add)
         send(ls, "l", t, [s])
-        ts(R("t1", 0, P), R("nc", P, 2 * P), L + 0.5, ALU.is_gt, 256.0, ALU.mult)
+        ts(R("t1", 0, P), R("nz", 0, 2 * P, 2), -L - 0.5, ALU.is_lt, 256.0, ALU.mult)
         scan(R("reg", 0, P), R("t1", 0, P), R("nh", 0, P), 0.0, ALU.max, ALU.max)
-        tt(R("idx", 0, P), R("ps", CD, CD + P), R("reg", 0, P), ALU.add)
+        tt(R("idx", 0, 128), ad[0], R("reg", 0, 128), ALU.add)
+        tt(R("idx", 128, P), ad[1], R("reg", 128, P), ALU.add)
         pick(("iw", 0), "c4", R("idx", 0, P), P)
         ts(R("oe", 0, P // 4), R("iw", 3, P, 4), col(IFX), ALU.add)
-        marks(R("oe", 0, 24), 0, 96)
-        marks(R("oe", 24, P // 4), 96, P)
-        rows(t + 1, 0, 96)
-        rows(t + 1, 96, P)
-        number(0, P, False)
-        shared_marks(rl, P)
-        rows(t + 1, P, n)
-        number(P, n, True)
+        for s0, s1 in ((0, 96), (96, P)):
+            act(R("d0", 4 * s0, 4 * s1), ind(R("tab"), R("oe", s0 // 4, s1 // 4)), ACT.Copy)
+            act(R("e", 4 * s0, 4 * s1), R("d0", 4 * s0, 4 * s1), ACT.Identity, 1.0 / 9, -1.0 / 9)
+            rows(t + 1, s0, s1)
         cp(R("li", 0, 24), R(rl, 24, 48))
         ts(R("li", 24, 48), R("li", 0, 24), 255, ALU.bitwise_and)
         ts(R("ko"), R("li", 24, 48), col(KOF), ALU.add)
         for b in range(4):
             mm(R("pr", 512 * b, 512 * b + P), "qe", "se", 128 * b, "rq%d" % t, "rs%d" % t, 0, P)
             act(R("dst", 224 * b, 224 * b + P), R("pr", 512 * b, 512 * b + P), ACT.Copy, 0.5)
-        act(R("pool", 4 * (nb - OFF + P), 4 * (nb - OFF + n)), ind(R("dst"), R("ko")), ACT.Copy)
+        number(t + 1, 0, P, False)
+        a = 4 * P
+        cp(R("d0", a, a + 192), ind(R("tab"), R(rl, 0, 12)))
+        act(R("d0", a + 192, a + 384), ind(R("tab"), R(rl, 12, 24)), ACT.Copy)
+        act(R("e", a, a + 384), R("d0", a, a + 384), ACT.Identity, 1.0 / 9, -1.0 / 9)
+        act(R("pool", 4 * (nb + P), 4 * (nb + n)), ind(R("dst"), R("ko")), ACT.Copy)
+        if t:
+            act(R("tok", 4 * P, 4 * n), R("pool", 4 * (nb + P), 4 * (nb + n)), ACT.Copy)
+        rows(t + 1, P, n)
+        number(t + 1, P, n, True)
     P = PR[2]
-    w = R("win", 0, P)
-    fire(2, n, False)
+    w = R("win2", 0, P)
+    fire(2, n)
     ys = R("ys", state[0], state[0] + 4)
     for k in range(4):
-        ts(R("ot", 4 * k, 4 * k + 4), ys, 4.0, ALU.mult, float(k - 4 * OFF), ALU.add)
+        ts(R("ot", 4 * k, 4 * k + 4), ys, 4.0, ALU.mult, float(k), ALU.add)
         act(R("tl", k, 4 * NA, 4), ind(R("pool"), R("ot", 4 * k, 4 * k + 4)), ACT.Copy, 2.0)
-    cp(R("ot", 16, 20), ys)
-    act(R("thr", 0, P), w, ACT.Relu, 1e26, 5.12e28)
-    act(R("occb", 0, NA), ind(R("iof"), R("ot", 16, 20)), ACT.Sign)
-    act(R("occb", NA, NA + P), w, ACT.Sign, 1.0, -FILL)
+    ts(R("ot", 16, 20), ys, 1.0, ALU.min)
+    act(R("thr", 0, P), w, ACT.Relu, 1e22)
+    act(R("occb", 0, NA), ind(R("iof"), R("ot", 16, 20)), ACT.Copy)
+    act(R("occb", NA, NA + P), w, ACT.Sign, 1.0, 1.0)
     store("s", T.occ[:], T.occb[0:128:16, :], R("occb"))
     quant("qt", "st", 160, 288, R("tl", 640, 1152))
     quant("qt", "st", 0, 128, R("tl", 0, 512))

@@ -1,4 +1,3 @@
-import math
 from concourse.mybir import dt, AluOpType, ActivationFunctionType
 
 ALU = AluOpType
@@ -15,8 +14,13 @@ BW = 7168.0
 B2 = 1024.0
 HOP, DMA = 2800.0, 2000.0
 CASES = ((90.0, 0.8), (130.0, 1.0), (180.0, 1.3))
-TRIES = [2500, 20000]
-LOADS = 6
+TRIES = [200, 90000]
+SLACK = 500.0
+PIECES = ((0, 128), (128, 288), (288, 480))
+SHARE = (64, 32, 0)
+CUTS = ((0, 6, 18, 32, 44), (0, 6, 18, 32))
+OWN, CAME = (64, 0), 48
+LOADS = 7
 ORDER = []
 
 
@@ -29,7 +33,7 @@ SCRATCH = {
     "qx": sb(480, Q4), "sx": sb(480, U8), "qu": sb(128, Q4), "su": sb(128, U8), "qu7": sb(128, Q4), "su7": sb(128, U8),
     "qv": sb(128, Q4), "sv": sb(128, U8), "wq": sb(512, Q4), "wp": sb(512, U8),
     "pool": sb(4 * NID, BF), "sm": sb(16 + 4 * 288, BF), "tok": sb(4 * 288, BF), "bt0": sb(512, BF), "bt": sb(896, BF), "sg": sb(320, BF),
-    "qb": sb(256, Q4), "sbb": sb(256, U8),
+    "qb": sb(384, Q4), "sbb": sb(384, U8),
     "ii": sb(48, I32), "ij": sb(48, I32), "col": sb(40, F32), "iof": sb(224, F32), "ids": sb(608, F16), "kfr": sb(224, F32),
     "idr": sb(480, BF), "idp0": sb(480, F32), "idp": sb(608, F32), "nj": sb(480, F16), "cq": sb(32, F32),
     "jg": sb(128, BF), "jh": sb(140, BF), "jq": sb(128, BF), "tm1": sb(40, F32), "tm2": sb(40, F32), "pat": sb(4, F32),
@@ -40,9 +44,9 @@ SCRATCH = {
     "qe": sb(512, Q4), "se": sb(512, U8),
     "oe": sb(120, U16), "pq": sb(120, F32), "pq2": sb(32, F32), "ql": sb(32, U16), "mk": sb(480, BF),
     "d0": sb(1920, BF), "y0": sb(1924, BF), "gq": sb(480, BF), "ta0": sb(480, BF), "fw0": sb(480, BF), "bw0": sb(480, BF), "vr0": sb(480, BF),
-    "e": sb(1280, BF), "yy": sb(1284, F16), "ys": sb(12, F32), "vv": sb(1280, F16), "q4": sb(1280, F16),
+    "e": sb(1280, BF), "yy": sb(1284, F16), "vv": sb(1280, F16), "q4": sb(1280, F16),
     "ta": sb(320, F16), "fw": sb(320, F16), "bw": sb(320, F16), "vr": sb(320, F16),
-    "nf": sb(480, BF), "pz": sb(960, F16), "pw": sb(960, F16), "cs": sb(4, F32), "od": sb(32, U16), "pk": sb(480, F32),
+    "nf": sb(480, BF), "pz": sb(960, F16), "pw": sb(960, F16), "od": sb(32, U16), "pk": sb(480, F32),
     "win0": sb(768, F32), "win1": sb(768, F32), "win2": sb(768, F32),
     "w4": sb(224, F32), "wi": sb(112, I32), "o2": sb(56, U16), "o1": sb(56, U16), "p4": sb(288, F32), "l4": sb(72, U16),
     "two": sb(896, BF), "bb": sb(896, BF), "qbb": sb(256, Q4), "sbq": sb(256, U8), "hh": sb(896, BF),
@@ -56,14 +60,14 @@ SCRATCH = {
     "pr": ("psum", [128, 2048], F32), "ps": ("psum", [128, 2048], F32),
 }
 SHARED = {}
-for whole, names in (("hf", "ta fw bw vr pz pw nz nw t1 reg idx iw"), ("win", "win0 win1 win2"), ("tm", "tm1 tm2 pat cs pq pq2")):
+for whole, names in (("hf", "ta fw bw vr pz pw nz nw t1 reg idx iw"), ("win", "win0 win1 win2"), ("tm", "tm1 tm2 pat pq pq2")):
     at = 0
     for name in names.split():
         SHARED[name] = (whole, at, SCRATCH[name][1][1])
         at += (SCRATCH[name][1][1] + 31) // 32 * 32
         kind = SCRATCH.pop(name)[2]
     SCRATCH[whole] = sb(at, kind)
-SEMAPHORES = ["sv_", "sa_", "sp_", "sg_", "lu", "lx0", "lx1", "lw_", "lp_", "lv", "out",
+SEMAPHORES = ["sv_", "sa_", "sp_", "sg_", "lu", "lx0", "lx1", "lx2", "lw_", "lp_", "lv", "out",
               "aq0", "as0", "al0", "aq1", "as1", "al1", "mq_", "ms_", "ml_", "loc"]
 (PI, PQ, G4, H4, QOFF, FIX4, TCOL, ODX, FW, C1, C2, C3, C4, WT, WT0, WQ, AOF, KOF, IFX, F256, TMP, TM2, TM3, POW, G8, K0, K1, K2, K3) = range(29)
 
@@ -97,22 +101,31 @@ def arrange(ops):
         for p in pre[i]:
             after[p].append(i)
 
-    def span(order, gap, hop):
-        free, done = dict.fromkeys("vapgsx", 0.0), [0.0] * n
-        for i in order:
-            t = free[q[i]]
+    def span(order, gap, hop, first, done, free):
+        for i in order[first:]:
+            k = q[i]
+            t = free[k]
             for p in pre[i]:
-                if done[p] + gap > t:
-                    t = done[p] + gap
-            if q[i] == "x":
-                done[i] = t + lat[i] * hop
+                if done[p] > t:
+                    t = done[p]
+            if k == "x":
+                done[i] = t + lat[i] * hop + gap
             else:
-                free[q[i]] = t + cost[i]
-                done[i] = t + cost[i] + lat[i]
+                free[k] = t = t + cost[i]
+                done[i] = t + lat[i] + gap
         return max(done)
 
-    def score(order):
-        return sum(span(order, gap, hop) for gap, hop in CASES)
+    def score(order, first=0, known=None):
+        last = {}
+        for i in reversed(order[:first]):
+            last.setdefault(q[i], i)
+        total, times = 0.0, []
+        for c, (gap, hop) in enumerate(CASES):
+            done = list(known[c]) if known else [0.0] * n
+            free = {k: done[last[k]] - lat[last[k]] - gap if k in last and k != "x" else 0.0 for k in "vapgsx"}
+            total += span(order, gap, hop, first, done, free)
+            times.append(done)
+        return total, times
 
     def greedy(extra, gap=CASES[1][0]):
         tail = [0.0] * n
@@ -146,28 +159,66 @@ def arrange(ops):
         seed[0] = (seed[0] * 6364136223846793005 + 1442695040888963407) % (1 << 64)
         return (seed[0] >> 33) % k
 
+    def waits(order, gap, hop):
+        free, last, done, why = dict.fromkeys("vapgsx", 0.0), {}, [0.0] * n, [None] * n
+        for i in order:
+            t = free[q[i]]
+            if q[i] in last:
+                why[i] = (last[q[i]], True)
+            for p in pre[i]:
+                if done[p] + gap > t:
+                    t, why[i] = done[p] + gap, (p, False)
+            if q[i] == "x":
+                done[i] = t + lat[i] * hop
+            else:
+                free[q[i]], last[q[i]] = t + cost[i], i
+                done[i] = t + cost[i] + lat[i]
+        i, pairs = done.index(max(done)), []
+        while why[i]:
+            if why[i][1]:
+                pairs.append((why[i][0], i))
+            i = why[i][0]
+        return pairs
+
+    def swapped(order, a, b, ahead):
+        i, j = order.index(a), order.index(b)
+        part = order[i:j + 1]
+        move = {b if ahead else a}
+        for k in (reversed(part) if ahead else part):
+            if k in move:
+                move.update(pre[k] if ahead else after[k])
+        if (a if ahead else b) in move:
+            return None
+        one, two = [k for k in part if k in move], [k for k in part if k not in move]
+        return order[:i] + (one + two if ahead else two + one) + order[j + 1:]
+
     extra = [0.0] * n
     order = greedy(extra)
-    best = score(order)
+    best = score(order)[0]
     for _ in range(TRIES[0]):
         e = list(extra)
         for _ in range(1 + draw(3)):
             e[draw(n)] += draw(2801) - 1400.0
         o = greedy(e)
-        s = score(o)
+        s = score(o)[0]
         if s <= best:
             best, extra, order = s, e, o
-    for _ in range(TRIES[1]):
-        k = draw(n)
-        i = order[k]
-        lo = max([order.index(p) for p in pre[i]] + [-1]) + 1
-        hi = min([order.index(s) for s in after[i]] + [n]) - 1
-        if hi > lo:
-            o = order[:k] + order[k + 1:]
-            o.insert(lo + draw(hi - lo + 1), i)
-            s = score(o)
-            if s <= best:
-                best, order = s, o
+    now, cur, pairs, known = best, order, None, score(order)[1]
+    for k in range(TRIES[1]):
+        if not pairs:
+            pairs = waits(cur, *CASES[draw(len(CASES))])
+        a, b = pairs.pop(draw(len(pairs)))
+        ahead = draw(2)
+        mates = [i for i in cur if q[i] == q[a]]
+        far = mates.index(a) + (-draw(3) if ahead else 1 + draw(3))
+        far = mates[min(max(far, 0), len(mates) - 1)]
+        o = swapped(cur, far, b, True) if ahead else swapped(cur, a, far, False)
+        if o:
+            s, times = score(o, cur.index(far if ahead else a), known)
+            if s <= now + SLACK * (1 - k / TRIES[1]) * draw(1000) / 1000:
+                now, cur, pairs, known = s, o, None, times
+                if s < best:
+                    best, order = s, o
     return list(range(LOADS)) + [i for i in order if i >= LOADS]
 
 
@@ -348,8 +399,8 @@ def rank_program(g, core, T, topo):
         scan(R(o[0], o[1], o[1] + n), R(c, 0, n), x, -b, ALU.add, ALU.min)
 
     load("s", R("ut"), T.u[:], "lu", 1000)
-    load("a", R("xt", 0, 640), T.x[:, 0:640], "lx0", 1300)
-    load("s", R("xt", 640, 1920), T.x[:, 640:1920], "lx1", 2600)
+    for k, (a, b) in enumerate(PIECES):
+        load("as"[k % 2], R("xt", 4 * a, 4 * b), T.x[:, 4 * a:4 * b], "lx%d" % k, 800 + 4 * b)
     load("s", R("wq"), T.wc[:], "lw_", 4000, True)
     load("s", R("wp"), T.ws[:], "lp_", 4500)
     load("s", R("vt"), T.v[:], "lv", 5000)
@@ -381,9 +432,10 @@ def rank_program(g, core, T, topo):
     ts(R("ij", 42, 43), p_, 2, ALU.logical_shift_right, 28, ALU.bitwise_and)
     ts(R("ij", 43, 44), p_, 2, ALU.logical_shift_right, 3, ALU.bitwise_and)
     cp(R("col", PI, H4 + 1), R("ij", 40, 44))
-    act(col(POW), col(PI), ACT.Exp, math.log(2.0))
+    ts(R("tm2", 0, 8), R("iof", 0, 8), col(PI), ALU.is_lt, 1.0, ALU.add)
+    scan(R("tm1", 0, 8), R("tm2", 0, 8), R("one", 0, 8), 1.0, ALU.mult, ALU.mult)
     ts(col(QOFF), col(PQ), -16.0, ALU.mult, 48.0, ALU.add)
-    ms(R("bt0", 160, 512), 0.0)
+    ms(R("bt0", 128, 512), 0.0)
     ms(R("y0", 0, 4), 256.0)
     ts(col(TCOL), col(PI), 48.0, ALU.add)
     ts(col(FIX4), col(H4), 2.5, ALU.is_lt, B, ALU.mult)
@@ -394,7 +446,7 @@ def rank_program(g, core, T, topo):
     ts(R("ii", 42, 46), R("iof", 4, 8), col(H4), ALU.subtract)
     ts(R("ij", 32, 36), R("ii", 42, 46), 3, ALU.bitwise_and)
     ts(col(TMP), col(PI), 7.0, ALU.is_equal, 128.0, ALU.mult)
-    ts(col(WT0), col(PI), 5.5, ALU.is_lt, col(POW), ALU.mult)
+    ts(col(WT0), col(PI), 5.5, ALU.is_lt, R("tm1", 7, 8), ALU.mult)
     ts(col(TM3), col(PI), 3.5, ALU.is_gt, 0.0625, ALU.mult)
     tt(col(WQ), col(WT0), col(TM3), ALU.mult)
     lin(WT, WT0, 1.0, col(TMP))
@@ -461,20 +513,24 @@ def rank_program(g, core, T, topo):
     picked(R("qu7"), R("qu"), R("o7"), True)
     picked(R("su7"), R("su"), R("o7"), False)
 
-    state = [0]
+    def marks(offs, z, s0, s1, m):
+        m += s0
+        if m > s0:
+            cp(R("d0", 4 * s0, 4 * m), ind(R("tab"), R(offs, (s0 - z) // 4, (m - z) // 4)))
+            ts(R("e", 4 * s0, 4 * m), R("d0", 4 * s0, 4 * m), -1.0, ALU.add, 1.0 / 9, ALU.mult)
+        act(R("d0", 4 * m, 4 * s1), ind(R("tab"), R(offs, (m - z) // 4, (s1 - z) // 4)), ACT.Copy)
+        act(R("e", 4 * m, 4 * s1), R("d0", 4 * m, 4 * s1), ACT.Identity, 1.0 / 9, -1.0 / 9)
 
     def rows(t, s0, s1):
-        a, b, k = 4 * s0, 4 * s1, state[0]
+        a, b = 4 * s0, 4 * s1
         z = BASE[t] - BASE[1]
         for q in range(4):
-            scan(R("yy", 4 + a + q, 4 + b, 4), R("d0", a + q, b, 4), R("ids", z + s0, z + s1), R("ys", k + q, k + q + 1), ALU.mult, ALU.min)
-        state[0] = (k + 4) % 12
-        cp(R("ys", state[0], state[0] + 4), R("yy", b, b + 4))
+            scan(R("yy", 4 + a + q, 4 + b, 4), R("d0", a + q, b, 4), R("ids", z + s0, z + s1), R("yy", a + q, a + q + 1), ALU.mult, ALU.min)
         scan(R("vv", a, b), R("yy", a, b), R("e", a, b), 0.0, ALU.max, ALU.mult)
         scan(R("q4", a, b), R("r4", 0, b - a), R("vv", a, b), 0.0, ALU.mult, ALU.min)
 
-    def places(z, w, o, nf, s0, s1, carry):
-        scan(R(z, 2 * s0, 2 * s1, 2), nf, R("one", 0, s1 - s0), carry, ALU.add, ALU.subtract)
+    def places(z, w, o, nf, s0, s1):
+        scan(R(z, 2 * s0, 2 * s1, 2), nf, R("one", 0, s1 - s0), R(z, 2 * s0 - 2, 2 * s0 - 1) if s0 else 0.0, ALU.add, ALU.subtract)
         scan(R(z, 2 * s0 + 1, 2 * s1, 2), nf, R("nj", s0, s1), 0.0, ALU.max, ALU.mult)
         pick((w, 2 * s0), "c32", R(z, 2 * s0, 2 * s1), 2 * (s1 - s0), B2)
         ts(R(o, s0 // 16, s1 // 16), R(w, 2 * s0 + 31, 2 * s1, 32), -1.0, ALU.mult, col(ODX), ALU.add)
@@ -487,15 +543,11 @@ def rank_program(g, core, T, topo):
         scan(back("bw" + x, s0, s1), R("r16", 0, n), back("fw" + x, s0, s1), 0.0, ALU.mult, ALU.min)
         v = R("vr" + x, s0, s1)
         tr(v, R("bw" + x, s0, s1))
-        if t:
+        if t and last:
             ts(R("nf", s0, s1), v, -0.5, ALU.is_gt)
         else:
             act(R("nf", s0, s1), v, ACT.Relu, 1.0, 1.0)
-        k = state[1]
-        places("pz", "pw", "od", R("nf", s0, s1), s0, s1, R("cs", k, k + 1) if s0 else 0.0)
-        if not last:
-            state[1] = 1 - k
-            cp(R("cs", 1 - k, 2 - k), R("pz", 2 * s1 - 2, 2 * s1 - 1))
+        places("pz", "pw", "od", R("nf", s0, s1), s0, s1)
         z = BASE[t] - BASE[1]
         mine = R("idp", z + s0, z + s1) if t else R("idp0", s0, s1)
         if t < 2:
@@ -504,12 +556,11 @@ def rank_program(g, core, T, topo):
         else:
             pick(("p4", s0), "c4", v, n)
             ts(R("l4", s0 // 4, s1 // 4), R("p4", s0 + 3, s1, 4), -4.0, ALU.mult, col(C4), ALU.add)
-            for a in range(s0, s1, 48):
-                tt(R("sm", 16 + 4 * a, 208 + 4 * a), ind(R("pool", 0, 4 * (BASE[t] + s1)), R("l4", a // 4, a // 4 + 12)),
-                   R("tok", 4 * a, 4 * a + 192), ALU.add)
+            k = 48 if last else 64
+            for a in range(s0, s1, k):
+                tt(R("sm", 16 + 4 * a, 16 + 4 * (a + k)), ind(R("pool", 0, 4 * (BASE[t] + s1)), R("l4", a // 4, (a + k) // 4)),
+                   R("tok", 4 * a, 4 * (a + k)), ALU.add)
         scat(R("win%d" % t), R("od", s0 // 16, s1 // 16), mine)
-
-    state.append(0)
 
     def fire(t, n):
         P = PR[t]
@@ -528,43 +579,46 @@ def rank_program(g, core, T, topo):
         ts(R("wi", 0, m), R("w4", 3, P, 4), col(FW), ALU.add)
         ts(R("wi", 56, 56 + m), R("wi", 0, m), 2047, ALU.bitwise_and)
         ts(R("o1", 0, m), R("wi", 56, 56 + m), -4.0, ALU.mult, col(C1), ALU.add)
-        for a, b in ((0, 12), (12, 32), (32, m)):
-            act(R("two", 16 * a, 16 * b), ind(R("pool", 0, top), R("o2", a, b)), ACT.Copy)
-            tt(R("bb", 16 * a, 16 * b), ind(R("pool", 0, top), R("o1", a, b)), R("two", 16 * a, 16 * b), ALU.add)
+        for a, b in zip(CUTS[t], CUTS[t][1:] + (m,)):
             if a:
+                act(R("two", 16 * a, 16 * b), ind(R("pool", 0, top), R("o2", a, b)), ACT.Copy)
+            else:
+                cp(R("two", 16 * a, 16 * b), ind(R("pool", 0, top), R("o2", a, b)))
+            tt(R("bb", 16 * a, 16 * b), ind(R("pool", 0, top), R("o1", a, b)), R("two", 16 * a, 16 * b), ALU.add)
+            if b in (32, m):
                 k = 0 if b == 32 else 128
                 quant("qbb", "sbq", k, k + 128, R("bb", 4 * (4 * b - 128), 16 * b))
                 for c in range(4):
                     mm(R("ps" if k else "pr", 512 * c, 512 * c + 128), "wq", "wp", 128 * c, "qbb", "sbq", k, k + 128)
 
-    for h, (a, b) in enumerate(((0, 160), (160, 480))):
+    for h, (a, b) in enumerate(PIECES):
         quant("qx", "sx", a, b, R("xt", 4 * a, 4 * b))
-        s = R("ps", 512 * h, 512 * h + b - a)
+        y, z = ("pr", "ps")[h % 2], 1024 * (h // 2)
+        s = R(y, z, z + b - a)
         mm(s, "qu", "su", 0, "qx", "sx", a, b)
-        if h:
-            act(R("sg"), s, ACT.Sign)
-            act(R("bt0", a, b), R("sg"), ACT.Relu)
-        else:
-            ts(R("bt0", a, b), s, 0.0, ALU.is_gt)
+        ts(R("bt0", a, b), s, 0.0, ALU.is_gt)
         quant("qb", "sbb", 128 * h, 128 * h + 128, R("bt0"))
-        z = 1024 + 512 * h
-        mm(R("ps", z, z + 128), "qwc", "swc", 0, "qb", "sbb", 128 * h, 128 * h + 128)
-        mm(R("pr", 512 * h, 512 * h + 128), "qwq", "swq", 0, "qb", "sbb", 128 * h, 128 * h + 128)
-        ts(R("oe", a // 4, b // 4), R("ps", z + a // 4, z + b // 4), col(QOFF), ALU.add)
-        pick(("pq", a // 4), "c4", R("pr", 512 * h + a // 4, 512 * h + b // 4), (b - a) // 4)
+        mm(R(y, z, z + 128), "qwc", "swc", 0, "qb", "sbb", 128 * h, 128 * h + 128)
+        ts(R("oe", a // 4, b // 4), R(y, z + a // 4, z + b // 4), col(QOFF), ALU.add)
+        if h == 0:
+            continue
+        a = a if h > 1 else 0
+        mm(R(y, z + 512, z + 640), "qwq", "swq", 0, "qb", "sbb", 128 * h, 128 * h + 128)
+        pick(("pq", a // 4), "c4", R(y, z + 512 + a // 4, z + 512 + b // 4), (b - a) // 4)
         tt(R("pq2", a // 16, b // 16), R("pq", a // 4 + 3, b // 4, 4), R("cq", a // 16, b // 16), ALU.add)
         cp(R("ql", a // 16, b // 16), R("pq2", a // 16, b // 16))
-    for s0 in (0, 160, 320):
-        s1 = s0 + 160
-        a, b = 4 * s0, 4 * s1
-        act(R("d0", a, b), ind(R("tab", 0, 128), R("oe", s0 // 4, s1 // 4)), ACT.Copy)
+    for h, (s0, s1) in enumerate(PIECES):
+        a, b, m = 4 * s0, 4 * s1, s0 + SHARE[h]
+        if m > s0:
+            cp(R("d0", a, 4 * m), ind(R("tab", 0, 128), R("oe", s0 // 4, m // 4)))
+        act(R("d0", 4 * m, b), ind(R("tab", 0, 128), R("oe", m // 4, s1 // 4)), ACT.Copy)
         for q in range(4):
             scan(R("y0", 4 + a + q, 4 + b, 4), R("d0", a + q, b, 4), R("idr", s0, s1), R("y0", a + q, a + q + 1), ALU.mult, ALU.max)
         o = R("ql", s0 // 16, s1 // 16)
         act(R("mk", s0, s1), ind(R("d0", 0, b), o), ACT.Relu, -0.125)
         tt(R("gq", s0, s1), ind(R("y0", 0, b), o), R("mk", s0, s1), ALU.mult)
         number(0, s0, s1, s1 == C)
-    act(R("ys", 0, 4), R("y0", 4 * C, 4 * C + 4), ACT.Copy, -1.0)
+    act(R("yy", 0, 4), R("y0", 4 * C, 4 * C + 4), ACT.Copy, -1.0)
     n = C
     for t in range(2):
         P = PR[t]
@@ -574,16 +628,12 @@ def rank_program(g, core, T, topo):
         fire(t, n)
         act(R("thr", 0, P), w, ACT.Relu, -1e26)
         act(R("nh", 0, P), w, ACT.Relu, -512.0)
-        n = P + L
+        came, n = n, P + L
         ad = []
         for a, b, y in ((0, 128, "pr"), (128, P, "ps")):
             lo = 128 - (b - a)
             for c in range(4):
-                o, i = R("hh", 4 * a + c, 4 * b, 4), R(y, 512 * c + lo, 512 * c + 128)
-                if a and c % 2 == 0:
-                    ts(o, i, 0.0, ALU.max, 0.03125, ALU.mult)
-                else:
-                    act(o, i, ACT.Relu, 0.03125)
+                act(R("hh", 4 * a + c, 4 * b, 4), R(y, 512 * c + lo, 512 * c + 128), ACT.Relu, 0.03125)
             quant(qh, sh, b - 128, b, R("hh", 4 * (b - 128), 4 * b))
             mm(R(y, 0, 128), "qu", "su", 0, qh, sh, b - 128, b)
             mm(R(y, 512, 640), "qu7", "su7", 0, qh, sh, b - 128, b)
@@ -596,14 +646,13 @@ def rank_program(g, core, T, topo):
             quant("qb", "sbb", a, a + 128, R("bt", 4 * (b - 128), 4 * b))
             mm(R(y, 1024, 1152), "qwb", "swb", 0, "qb", "sbb", a, a + 128)
             ad.append(R(y, 1024 + lo, 1152))
-            places("nz", "nw", "ol", R("nc", a, b), a, b, R("cs", 2, 3) if a else 0.0)
-            if not a:
-                cp(R("cs", 2, 3), R("nz", 2 * b - 2, 2 * b - 1))
+            places("nz", "nw", "ol", R("nc", a, b), a, b)
             tt(R("val", a, b), ad[-1], R("kfr", a, b), ALU.add)
             scat(R("lwin"), R("ol", a // 16, b // 16), R("val", a, b))
         s = send(sh, "s", t, [send(qh, "q", t, own)])
         nb = BASE[t + 1]
-        act(R("yy", 0, 4), R("ys", state[0], state[0] + 4), ACT.Copy)
+        if t:
+            act(R("yy", 0, 4), R("yy", 4 * came, 4 * came + 4), ACT.Copy)
         for k in range(0, 4 * P, 2 * P):
             act(R("pool", 4 * nb + k, 4 * nb + k + 2 * P), R("hh", k, k + 2 * P), ACT.Copy, 0.5)
             if t:
@@ -612,27 +661,23 @@ def rank_program(g, core, T, topo):
         ts(R(ls, 0, 24), R("lw", 3, L, 4), col(AOF), ALU.add)
         ts(R(ls, 24, 48), R("lw", 3, L, 4), 256.0, ALU.mult, col(F256), ALU.add)
         send(ls, "l", t, [s])
-        ts(R("t1", 0, P), R("nz", 0, 2 * P, 2), -L - 0.5, ALU.is_lt, 256.0, ALU.mult)
-        scan(R("reg", 0, P), R("t1", 0, P), R("nh", 0, P), 0.0, ALU.max, ALU.max)
-        tt(R("idx", 0, 128), ad[0], R("reg", 0, 128), ALU.add)
-        tt(R("idx", 128, P), ad[1], R("reg", 128, P), ALU.add)
-        pick(("iw", 0), "c4", R("idx", 0, P), P)
-        ts(R("oe", 0, P // 4), R("iw", 3, P, 4), col(IFX), ALU.add)
-        for s0, s1 in ((0, 96), (96, P)):
-            act(R("d0", 4 * s0, 4 * s1), ind(R("tab"), R("oe", s0 // 4, s1 // 4)), ACT.Copy)
-            act(R("e", 4 * s0, 4 * s1), R("d0", 4 * s0, 4 * s1), ACT.Identity, 1.0 / 9, -1.0 / 9)
+        for (a, b), y in zip(((0, 128), (128, P)), ad):
+            ts(R("t1", a, b), R("nz", 2 * a, 2 * b, 2), -L - 0.5, ALU.is_lt, 256.0, ALU.mult)
+            scan(R("reg", a, b), R("t1", a, b), R("nh", a, b), 0.0, ALU.max, ALU.max)
+            tt(R("idx", a, b), y, R("reg", a, b), ALU.add)
+            pick(("iw", a), "c4", R("idx", a, b), b - a)
+            ts(R("oe", a // 4, b // 4), R("iw", a + 3, b, 4), col(IFX), ALU.add)
+        for (s0, s1), m in zip(((0, 128), (128, P)), OWN):
+            marks("oe", 0, s0, s1, m)
             rows(t + 1, s0, s1)
+            number(t + 1, s0, s1, False)
         cp(R("li", 0, 24), R(rl, 24, 48))
         ts(R("li", 24, 48), R("li", 0, 24), 255, ALU.bitwise_and)
         ts(R("ko"), R("li", 24, 48), col(KOF), ALU.add)
         for b in range(4):
             mm(R("pr", 512 * b, 512 * b + P), "qe", "se", 128 * b, "rq%d" % t, "rs%d" % t, 0, P)
             act(R("dst", 224 * b, 224 * b + P), R("pr", 512 * b, 512 * b + P), ACT.Copy, 0.5)
-        number(t + 1, 0, P, False)
-        a = 4 * P
-        cp(R("d0", a, a + 192), ind(R("tab"), R(rl, 0, 12)))
-        act(R("d0", a + 192, a + 384), ind(R("tab"), R(rl, 12, 24)), ACT.Copy)
-        act(R("e", a, a + 384), R("d0", a, a + 384), ACT.Identity, 1.0 / 9, -1.0 / 9)
+        marks(rl, P, P, n, CAME)
         act(R("pool", 4 * (nb + P), 4 * (nb + n)), ind(R("dst"), R("ko")), ACT.Copy)
         if t:
             act(R("tok", 4 * P, 4 * n), R("pool", 4 * (nb + P), 4 * (nb + n)), ACT.Copy)
@@ -641,7 +686,7 @@ def rank_program(g, core, T, topo):
     P = PR[2]
     w = R("win2", 0, P)
     fire(2, n)
-    ys = R("ys", state[0], state[0] + 4)
+    ys = R("yy", 4 * n, 4 * n + 4)
     for k in range(4):
         ts(R("ot", 4 * k, 4 * k + 4), ys, 4.0, ALU.mult, float(k), ALU.add)
         act(R("tl", k, 4 * NA, 4), ind(R("pool"), R("ot", 4 * k, 4 * k + 4)), ACT.Copy, 2.0)

@@ -1,3 +1,4 @@
+from concourse.bass import DstId, RemoteDMATransfer
 from concourse.mybir import dt, AluOpType, ActivationFunctionType
 
 ALU = AluOpType
@@ -13,14 +14,14 @@ B = 2048.0
 BW = 7168.0
 B2 = 1024.0
 HOP, DMA = 2800.0, 2000.0
-CASES = ((90.0, 0.8), (130.0, 1.0), (180.0, 1.3))
-TRIES = [200, 90000]
-SLACK = 500.0
-PIECES = ((0, 128), (128, 288), (288, 480))
+CASES = ((240.0, 1.25, 1.15), (190.0, 1.0, 0.85))
+TRIES = [6, 15000, 25000]
+SLACK = 350.0
+PIECES = ((0, 128), (128, 320), (320, 480))
 SHARE = (64, 32, 0)
-CUTS = ((0, 6, 18, 32, 44), (0, 6, 18, 32))
+CUTS = ((0, 6, 18), (32, 38, 46), (0, 6, 18, 32))
 OWN, CAME = (64, 0), 48
-LOADS = 7
+LOADS = 4
 ORDER = []
 
 
@@ -37,7 +38,7 @@ SCRATCH = {
     "ii": sb(48, I32), "ij": sb(48, I32), "col": sb(40, F32), "iof": sb(224, F32), "ids": sb(608, F16), "kfr": sb(224, F32),
     "idr": sb(480, BF), "idp0": sb(480, F32), "idp": sb(608, F32), "nj": sb(480, F16), "cq": sb(32, F32),
     "jg": sb(128, BF), "jh": sb(140, BF), "jq": sb(128, BF), "tm1": sb(40, F32), "tm2": sb(40, F32), "pat": sb(4, F32),
-    "c32": sb(448, BF), "c4": sb(224, BF), "c4x": sb(224, BF), "r16": sb(224, BF), "r4": sb(512, BF),
+    "c32": sb(448, BF), "c4": sb(224, BF), "c4x": sb(224, BF), "r16": sb(224, BF), "r4": sb(512, BF), "r64": sb(384, BF), "f4": sb(384, F16),
     "one": sb(512, BF), "tab": sb(768, BF), "o7": sb(8, U16),
     "wc0": sb(512, BF), "wq0": sb(512, BF), "wb0": sb(512, BF), "et": sb(2048, BF),
     "qwc": sb(128, Q4), "swc": sb(128, U8), "qwq": sb(128, Q4), "swq": sb(128, U8), "qwb": sb(128, Q4), "swb": sb(128, U8),
@@ -50,7 +51,7 @@ SCRATCH = {
     "win0": sb(768, F32), "win1": sb(768, F32), "win2": sb(768, F32),
     "w4": sb(224, F32), "wi": sb(112, I32), "o2": sb(56, U16), "o1": sb(56, U16), "p4": sb(288, F32), "l4": sb(72, U16),
     "two": sb(896, BF), "bb": sb(896, BF), "qbb": sb(256, Q4), "sbq": sb(256, U8), "hh": sb(896, BF),
-    "qh0": sb(224, Q4), "sh0": sb(224, U8), "qh1": sb(192, Q4), "sh1": sb(192, U8),
+    "qh0": sb(256, Q4), "sh0": sb(256, U8), "qh1": sb(256, Q4), "sh1": sb(256, U8),
     "thr": sb(224, F32), "nh": sb(224, BF), "nc": sb(224, BF), "nz": sb(448, F16), "nw": sb(448, F16),
     "ol": sb(14, U16), "val": sb(224, F32), "lwin": sb(512, F32), "lw": sb(96, F32), "li": sb(48, I32), "ko": sb(24, U16),
     "ls0": sb(48, U16), "ls1": sb(48, U16), "t1": sb(224, F16), "reg": sb(224, F16), "idx": sb(224, F16), "iw": sb(224, F16),
@@ -68,25 +69,27 @@ for whole, names in (("hf", "ta fw bw vr pz pw nz nw t1 reg idx iw"), ("win", "w
         kind = SCRATCH.pop(name)[2]
     SCRATCH[whole] = sb(at, kind)
 SEMAPHORES = ["sv_", "sa_", "sp_", "sg_", "lu", "lx0", "lx1", "lx2", "lw_", "lp_", "lv", "out",
-              "aq0", "as0", "al0", "aq1", "as1", "al1", "mq_", "ms_", "ml_", "loc"]
+              "aqa0", "aqb0", "as0", "al0", "aqa1", "aqb1", "as1", "al1", "mqa_", "mqb_", "ms_", "ml_", "loc"]
 (PI, PQ, G4, H4, QOFF, FIX4, TCOL, ODX, FW, C1, C2, C3, C4, WT, WT0, WQ, AOF, KOF, IFX, F256, TMP, TM2, TM3, POW, G8, K0, K1, K2, K3) = range(29)
 
 
 def relay_of(src, dst, k, topo):
     ok = [c for c in topo.cores_of(src) if c != src and topo.may_write(c, dst)]
     near = [c for c in ok if topo.die(c) == topo.die(src)] or ok
-    return near[0] if k == "q" else near[-1]
+    return near[0] if k[0] == "q" else near[-1]
 
 
 def relay_program(g, core, T, topo, src, dst):
     rid, pid = topo.addr(dst, core)
     n = 0
-    for k in "qsl":
+    h = PR[1] // 2
+    for k in ("qa", "qb", "s", "l"):
         if relay_of(src, dst, k, topo) == core:
             g.wait_ge(T.sem["m%s_" % k], len(topo.engines(src, core)))
-            a, b = T["r%s1" % k][:], T["m" + k][:]
-            if k == "q":
-                a, b = a.bitcast(dt.uint8), b.bitcast(dt.uint8)
+            a, b = T["r%s1" % k[0]][:], T["m" + k[0]][:]
+            if k[0] == "q":
+                at = 0 if k == "qa" else h
+                a, b = T.rq1[:, at:at + h].bitcast(dt.uint8), T.mq[:, at:at + h].bitcast(dt.uint8)
             g.remote_dma(a, b, T.sem["a%s1" % k], T.sem["loc"], pid, rid, topo.mask(core, dst))
             n += len(topo.engines(core, dst))
     if n:
@@ -96,12 +99,14 @@ def relay_program(g, core, T, topo, src, dst):
 def arrange(ops):
     n = len(ops)
     q, pre, cost, lat = ([o[k] for o in ops] for k in ("q", "pre", "cost", "lat"))
+    costs = {c[2]: [c[2] * x for x in cost] for c in CASES}
+    cost = costs[CASES[1][2]]
     after = [[] for _ in ops]
     for i in range(n):
         for p in pre[i]:
             after[p].append(i)
 
-    def span(order, gap, hop, first, done, free):
+    def span(order, gap, hop, cost, first, done, free):
         for i in order[first:]:
             k = q[i]
             t = free[k]
@@ -120,10 +125,10 @@ def arrange(ops):
         for i in reversed(order[:first]):
             last.setdefault(q[i], i)
         total, times = 0.0, []
-        for c, (gap, hop) in enumerate(CASES):
+        for c, (gap, hop, rate) in enumerate(CASES):
             done = list(known[c]) if known else [0.0] * n
             free = {k: done[last[k]] - lat[last[k]] - gap if k in last and k != "x" else 0.0 for k in "vapgsx"}
-            total += span(order, gap, hop, first, done, free)
+            total += span(order, gap, hop, costs[rate], first, done, free)
             times.append(done)
         return total, times
 
@@ -159,7 +164,8 @@ def arrange(ops):
         seed[0] = (seed[0] * 6364136223846793005 + 1442695040888963407) % (1 << 64)
         return (seed[0] >> 33) % k
 
-    def waits(order, gap, hop):
+    def waits(order, gap, hop, rate):
+        cost = costs[rate]
         free, last, done, why = dict.fromkeys("vapgsx", 0.0), {}, [0.0] * n, [None] * n
         for i in order:
             t = free[q[i]]
@@ -192,33 +198,35 @@ def arrange(ops):
         one, two = [k for k in part if k in move], [k for k in part if k not in move]
         return order[:i] + (one + two if ahead else two + one) + order[j + 1:]
 
-    extra = [0.0] * n
-    order = greedy(extra)
-    best = score(order)[0]
-    for _ in range(TRIES[0]):
-        e = list(extra)
-        for _ in range(1 + draw(3)):
-            e[draw(n)] += draw(2801) - 1400.0
-        o = greedy(e)
-        s = score(o)[0]
-        if s <= best:
-            best, extra, order = s, e, o
-    now, cur, pairs, known = best, order, None, score(order)[1]
-    for k in range(TRIES[1]):
-        if not pairs:
-            pairs = waits(cur, *CASES[draw(len(CASES))])
-        a, b = pairs.pop(draw(len(pairs)))
-        ahead = draw(2)
-        mates = [i for i in cur if q[i] == q[a]]
-        far = mates.index(a) + (-draw(3) if ahead else 1 + draw(3))
-        far = mates[min(max(far, 0), len(mates) - 1)]
-        o = swapped(cur, far, b, True) if ahead else swapped(cur, a, far, False)
-        if o:
-            s, times = score(o, cur.index(far if ahead else a), known)
-            if s <= now + SLACK * (1 - k / TRIES[1]) * draw(1000) / 1000:
-                now, cur, pairs, known = s, o, None, times
-                if s < best:
-                    best, order = s, o
+    def improved(order, tries):
+        best, known = score(order)
+        now, cur, pairs = best, order, None
+        for k in range(tries):
+            if not pairs:
+                pairs = waits(cur, *CASES[draw(len(CASES))])
+            a, b = pairs.pop(draw(len(pairs)))
+            ahead = draw(2)
+            mates = [i for i in cur if q[i] == q[a]]
+            far = mates.index(a) + (-draw(3) if ahead else 1 + draw(3))
+            far = mates[min(max(far, 0), len(mates) - 1)]
+            o = swapped(cur, far, b, True) if ahead else swapped(cur, a, far, False)
+            if o:
+                s, times = score(o, cur.index(far if ahead else a), known)
+                if s <= now + SLACK * (1 - k / tries) * draw(1000) / 1000:
+                    now, cur, pairs, known = s, o, None, times
+                    if s < best:
+                        best, order = s, o
+        return order
+
+    def joined(one, two, cut):
+        head = one[:one.index(cut) + 1]
+        done = set(head)
+        return head + [i for i in two if i not in done]
+
+    found = [improved(greedy([draw(200) for _ in ops]), TRIES[1]) for _ in range(TRIES[0])]
+    for cut in [i for i in range(n) if ops[i]["sem"] in ("al0", "al1")]:
+        found += sorted((joined(a, b, cut) for a in found for b in found if a is not b), key=lambda o: score(o)[0])[:TRIES[0]]
+    order = improved(min(found, key=lambda o: score(o)[0]), TRIES[2])
     return list(range(LOADS)) + [i for i in order if i >= LOADS]
 
 
@@ -323,8 +331,10 @@ def rank_program(g, core, T, topo):
     def cp(o, i):
         emit("v", lambda: g.vector.tensor_copy(o[0], i[0]), [o], [i], length(o, [i]))
 
-    def scat(w, offs, i):
-        emit("v", lambda: g.vector.tensor_copy(w[0].indirect(offs[0]), i[0]), [w], [i, offs], 50 + 3.8 * i[2])
+    def scat(w, offs, src, z, a, b, step=512):
+        for k in range(a, b, step):
+            o, i = R(offs, k // 16, min(k + step, b) // 16), R(src, z + k, z + min(k + step, b))
+            emit("v", lambda o=o, i=i: g.vector.tensor_copy(w[0].indirect(o[0]), i[0]), [w], [i, o], 50 + 3.8 * i[2])
 
     def scan(o, a, b, init, op0, op1):
         emit("v", lambda: g.vector.tensor_tensor_scan(o[0], a[0], b[0], ap(init), op0, op1), [o], [a, b, init], length(o, [a, b]))
@@ -363,8 +373,8 @@ def rank_program(g, core, T, topo):
         i = R("one", 0, o[2])
         own.append(emit("g", lambda: g.affine_select(o[0], i[0], pat, op, 0.0, base, cm), [o], [i], 170 + 2.2 * o[2]))
 
-    def load(q, o, src, sem, late, codes=False):
-        emit(q, lambda: Q[q].dma_start(o[0].bitcast(dt.uint8) if codes else o[0], src), [o], [], 100, sem, 16, DMA + late)
+    def load(q, o, src, sem, late, codes=False, pre=()):
+        emit(q, lambda: Q[q].dma_start(o[0].bitcast(dt.uint8) if codes else o[0], src), [o], [], 100, sem, 16, DMA + late, pre)
 
     def picked(a, b, o, codes):
         if codes:
@@ -374,22 +384,30 @@ def rank_program(g, core, T, topo):
 
     peer = [T.cores[rank ^ 1], T.cores[rank ^ 2]]
 
-    def send(src, k, t, pre):
-        i = R(src)
+    def send(k, t, parts, pre):
         direct = topo.may_write(core, peer[t])
         if direct:
-            dst, land, far = peer[t], "r%s%d" % (k, t), "a%s%d" % (k, t)
+            dst, land, far = peer[t], "r%s%d" % (k[0], t), "a%s%d" % (k, t)
         else:
-            dst, land, far = relay_of(core, peer[t], k, topo), "m" + k, "m%s_" % k
+            dst, land, far = relay_of(core, peer[t], k, topo), "m" + k[0], "m%s_" % k
         rid, pid = topo.addr(dst, core)
-        a, b = T[land][:], i[0]
-        if k == "q":
-            a, b = a.bitcast(dt.uint8), b.bitcast(dt.uint8)
-        s = emit("g", lambda: g.remote_dma(a, b, T.sem[far], T.sem["loc"], pid, rid, topo.mask(core, dst)), [], [i], 1000, "loc",
-                 len(topo.engines(core, dst)), 0.0, pre)
+        use = topo.engines(core, dst)
+        each = len(use) // len(parts)
+        sides = [(T[land][:, at:at + i[2]], i[0]) for i, at in parts]
+        if k[0] == "q":
+            sides = [(a.bitcast(dt.uint8), b.bitcast(dt.uint8)) for a, b in sides]
+
+        def make():
+            if len(parts) == 1:
+                return g.remote_dma(sides[0][0], sides[0][1], T.sem[far], T.sem["loc"], pid, rid, topo.mask(core, dst))
+            return g.remote_dma_fused([RemoteDMATransfer(
+                dst_ids=[DstId(rid=rid, pnc=pid)], dma_engine_mask=sum(1 << e for e in use[each * j:each * j + each]),
+                remote_sem=T.sem[far], src=b, dst=a) for j, (a, b) in enumerate(sides)], local_sem=T.sem["loc"])
+
+        s = emit("g", make, [], [i for i, at in parts], 1000, "loc", len(use), 0.0, pre)
         last = peer[t] if direct else relay_of(peer[t], core, k, topo)
-        emit("x", None, [R("r%s%d" % (k, t))], [], 0.0, "a%s%d" % (k, t), len(topo.engines(last, core)),
-             (HOP if direct else 2 * HOP + 1000) + (3000 if k == "q" else 0), [s])
+        emit("x", None, [R("r%s%d" % (k[0], t), at, at + i[2]) for i, at in parts], [], 0.0, "a%s%d" % (k, t), len(topo.engines(last, core)),
+             (HOP if direct else 2 * HOP + 1000) + (1500 if k[0] == "q" else 0), [s])
         return s
 
     def store(q, o, i, src):
@@ -401,9 +419,9 @@ def rank_program(g, core, T, topo):
     load("s", R("ut"), T.u[:], "lu", 1000)
     for k, (a, b) in enumerate(PIECES):
         load("as"[k % 2], R("xt", 4 * a, 4 * b), T.x[:, 4 * a:4 * b], "lx%d" % k, 800 + 4 * b)
-    load("s", R("wq"), T.wc[:], "lw_", 4000, True)
-    load("s", R("wp"), T.ws[:], "lp_", 4500)
-    load("s", R("vt"), T.v[:], "lv", 5000)
+    load("s", R("wq"), T.wc[:], "lw_", 1500, True, [LOADS - 1])
+    load("s", R("wp"), T.ws[:], "lp_", 2000, False, [LOADS - 1])
+    load("s", R("vt"), T.v[:], "lv", 2500, False, [LOADS - 1])
 
     iota(R("ii", 40, 41), [[0, 1]], 0, 1, False)
     iota(R("jh"), [[1, 35], [0, 4]], -3, 0)
@@ -418,6 +436,7 @@ def rank_program(g, core, T, topo):
         iota(R("idp", k, min(k + 320, 608)), [[8192, min(320, 608 - k)]], 8192 * (BASE[1] + k), 0)
     ms(R("one"), 1.0)
     keep(R("r16"), [[0, 14], [1, 16]], ALU.not_equal, 0, 0)
+    keep(R("r64"), [[0, 6], [1, 64]], ALU.not_equal, 0, 0)
     keep(R("r4"), [[0, 128], [1, 4]], ALU.not_equal, 0, 0)
     iota(R("ii", 32, 40), [[16, 8]], 7, 0, False)
     iota(R("jg"), [[4, 8], [0, 16]], 0, 0)
@@ -527,7 +546,6 @@ def rank_program(g, core, T, topo):
         for q in range(4):
             scan(R("yy", 4 + a + q, 4 + b, 4), R("d0", a + q, b, 4), R("ids", z + s0, z + s1), R("yy", a + q, a + q + 1), ALU.mult, ALU.min)
         scan(R("vv", a, b), R("yy", a, b), R("e", a, b), 0.0, ALU.max, ALU.mult)
-        scan(R("q4", a, b), R("r4", 0, b - a), R("vv", a, b), 0.0, ALU.mult, ALU.min)
 
     def places(z, w, o, nf, s0, s1):
         scan(R(z, 2 * s0, 2 * s1, 2), nf, R("one", 0, s1 - s0), R(z, 2 * s0 - 2, 2 * s0 - 1) if s0 else 0.0, ALU.add, ALU.subtract)
@@ -538,9 +556,18 @@ def rank_program(g, core, T, topo):
     def number(t, s0, s1, last):
         x = "" if t else "0"
         n = s1 - s0
-        tr(R("ta" + x, s0, s1), R("q4", 4 * s0 + 3, 4 * s1, 4) if t else R("gq", s0, s1))
-        scan(R("fw" + x, s0, s1), R("r16", 0, n), R("ta" + x, s0, s1), 0.0, ALU.mult, ALU.min)
-        scan(back("bw" + x, s0, s1), R("r16", 0, n), back("fw" + x, s0, s1), 0.0, ALU.mult, ALU.min)
+        if t and last:
+            for q in range(4):
+                tr(R("q4", 4 * s0 + q, 4 * s1, 4), R("vv", 4 * s0 + q, 4 * s1, 4))
+            scan(R("f4"), R("r64"), R("q4", 4 * s0, 4 * s1), 0.0, ALU.mult, ALU.min)
+            fw = (T.f4[:, 4 * n - 1:2:-4], R("f4")[1], n)
+        else:
+            if t:
+                scan(R("q4", 4 * s0, 4 * s1), R("r4", 0, 4 * n), R("vv", 4 * s0, 4 * s1), 0.0, ALU.mult, ALU.min)
+            tr(R("ta" + x, s0, s1), R("q4", 4 * s0 + 3, 4 * s1, 4) if t else R("gq", s0, s1))
+            scan(R("fw" + x, s0, s1), R("r16", 0, n), R("ta" + x, s0, s1), 0.0, ALU.mult, ALU.min)
+            fw = back("fw" + x, s0, s1)
+        scan(back("bw" + x, s0, s1), R("r16", 0, n), fw, 0.0, ALU.mult, ALU.min)
         v = R("vr" + x, s0, s1)
         tr(v, R("bw" + x, s0, s1))
         if t and last:
@@ -549,48 +576,55 @@ def rank_program(g, core, T, topo):
             act(R("nf", s0, s1), v, ACT.Relu, 1.0, 1.0)
         places("pz", "pw", "od", R("nf", s0, s1), s0, s1)
         z = BASE[t] - BASE[1]
-        mine = R("idp", z + s0, z + s1) if t else R("idp0", s0, s1)
         if t < 2:
-            scan(R("pk", s0, s1), v, mine, 0.0, ALU.min, ALU.add)
-            mine = R("pk", s0, s1)
+            scan(R("pk", s0, s1), v, R("idp", z + s0, z + s1) if t else R("idp0", s0, s1), 0.0, ALU.min, ALU.add)
+            scat(R("win%d" % t), "od", "pk", 0, s0, s1, 64 if t and not last else 512)
         else:
             pick(("p4", s0), "c4", v, n)
             ts(R("l4", s0 // 4, s1 // 4), R("p4", s0 + 3, s1, 4), -4.0, ALU.mult, col(C4), ALU.add)
-            k = 48 if last else 64
+            k = 24 if last else 32
             for a in range(s0, s1, k):
                 tt(R("sm", 16 + 4 * a, 16 + 4 * (a + k)), ind(R("pool", 0, 4 * (BASE[t] + s1)), R("l4", a // 4, (a + k) // 4)),
                    R("tok", 4 * a, 4 * (a + k)), ALU.add)
-        scat(R("win%d" % t), R("od", s0 // 16, s1 // 16), mine)
+            scat(R("win2"), "od", "idp", z, s0, s1)
 
-    def fire(t, n):
-        P = PR[t]
-        m = P // 4
-        pick(("w4", 0), "c4x", R("win%d" % t, 0, P), P, BW * B)
-        if t == 2:
-            ts(R("o1", 0, m), R("w4", 3, P, 4), col(C3), ALU.add, 1.0 / 2048, ALU.mult)
-            act(R("bb", 0, 320), ind(R("sm"), R("o1", 0, 20)), ACT.Copy)
-            cp(R("bb", 320, 640), ind(R("sm"), R("o1", 20, 40)))
-            quant("qbb", "sbq", 0, P, R("bb", 0, 4 * P))
-            for c in range(4):
-                mm(R("pr", 512 * c, 512 * c + P), "wq", "wp", 128 * c, "qbb", "sbq", 0, P)
-            return
-        top = 4 * (BASE[1] + n if t else BASE[1])
-        ts(R("o2", 0, m), R("w4", 3, P, 4), col(C2), ALU.add, 1.0 / 2048, ALU.mult)
-        ts(R("wi", 0, m), R("w4", 3, P, 4), col(FW), ALU.add)
-        ts(R("wi", 56, 56 + m), R("wi", 0, m), 2047, ALU.bitwise_and)
-        ts(R("o1", 0, m), R("wi", 56, 56 + m), -4.0, ALU.mult, col(C1), ALU.add)
-        for a, b in zip(CUTS[t], CUTS[t][1:] + (m,)):
-            if a:
+    def members(t, lo, hi, top, cuts):
+        m0, m = lo // 4, hi // 4
+        pick(("w4", lo), "c4x", R("win%d" % t, lo, hi), hi - lo, BW * B)
+        w = R("w4", lo + 3, hi, 4)
+        ts(R("o2", m0, m), w, col(C2), ALU.add, 1.0 / 2048, ALU.mult)
+        ts(R("wi", m0, m), w, col(FW), ALU.add)
+        ts(R("wi", 56 + m0, 56 + m), R("wi", m0, m), 2047, ALU.bitwise_and)
+        ts(R("o1", m0, m), R("wi", 56 + m0, 56 + m), -4.0, ALU.mult, col(C1), ALU.add)
+        for a, b in zip(cuts, cuts[1:] + (m,)):
+            if a > m0:
                 act(R("two", 16 * a, 16 * b), ind(R("pool", 0, top), R("o2", a, b)), ACT.Copy)
             else:
                 cp(R("two", 16 * a, 16 * b), ind(R("pool", 0, top), R("o2", a, b)))
             tt(R("bb", 16 * a, 16 * b), ind(R("pool", 0, top), R("o1", a, b)), R("two", 16 * a, 16 * b), ALU.add)
-            if b in (32, m):
-                k = 0 if b == 32 else 128
-                quant("qbb", "sbq", k, k + 128, R("bb", 4 * (4 * b - 128), 16 * b))
-                for c in range(4):
-                    mm(R("ps" if k else "pr", 512 * c, 512 * c + 128), "wq", "wp", 128 * c, "qbb", "sbq", k, k + 128)
 
+    def leave(t, a, b):
+        qh, sh, y, lo = "qh%d" % t, "sh%d" % t, "ps" if a else "pr", 128 - (b - a)
+        quant("qbb", "sbq", a, a + 128, R("bb", 4 * (b - 128), 4 * b))
+        for c in range(4):
+            mm(R(y, 512 * c, 512 * c + 128), "wq", "wp", 128 * c, "qbb", "sbq", a, a + 128)
+            act(R("hh", 4 * a + c, 4 * b, 4), R(y, 512 * c + lo, 512 * c + 128), ACT.Relu, 0.03125)
+        quant(qh, sh, a, a + 128, R("hh", 4 * (b - 128), 4 * b))
+        mm(R(y, 0, 128), "qu", "su", 0, qh, sh, a, a + 128)
+        mm(R(y, 512, 640), "qu7", "su7", 0, qh, sh, a, a + 128)
+        ts(R("bt", 4 * a, 4 * b, 4), R(y, lo, 128), 0.0, ALU.is_gt)
+        w = R("win%d" % t, a, b)
+        act(R("thr", a, b), w, ACT.Relu, -1e26)
+        act(R("nh", a, b), w, ACT.Relu, -512.0)
+        tt(R("nc", a, b), R(y, 512 + lo, 640), R("thr", a, b), ALU.is_le)
+        quant("qb", "sbb", a, a + 128, R("bt", 4 * (b - 128), 4 * b))
+        mm(R(y, 1024, 1152), "qwb", "swb", 0, "qb", "sbb", a, a + 128)
+        places("nz", "nw", "ol", R("nc", a, b), a, b)
+        tt(R("val", a, b), R(y, 1024 + lo, 1152), R("kfr", a, b), ALU.add)
+        scat(R("lwin"), "ol", "val", 0, a, b)
+        return R(y, 1024 + lo, 1152)
+
+    act(R("lwin", 0, L), R("one", 0, L), ACT.Copy, 0.0)
     for h, (a, b) in enumerate(PIECES):
         quant("qx", "sx", a, b, R("xt", 4 * a, 4 * b))
         y, z = ("pr", "ps")[h % 2], 1024 * (h // 2)
@@ -618,38 +652,26 @@ def rank_program(g, core, T, topo):
         act(R("mk", s0, s1), ind(R("d0", 0, b), o), ACT.Relu, -0.125)
         tt(R("gq", s0, s1), ind(R("y0", 0, b), o), R("mk", s0, s1), ALU.mult)
         number(0, s0, s1, s1 == C)
+        if s1 == NA + 2 * 128:
+            members(0, 0, 128, 4 * (RUNS[1][2] + RUNS[1][3] * (s1 - RUNS[1][0])), CUTS[0])
+            ad = [leave(0, 0, 128)]
     act(R("yy", 0, 4), R("y0", 4 * C, 4 * C + 4), ACT.Copy, -1.0)
     n = C
     for t in range(2):
         P = PR[t]
         qh, sh, ls, rl = "qh%d" % t, "sh%d" % t, "ls%d" % t, "rl%d" % t
-        w = R("win%d" % t, 0, P)
-        act(R("lwin", 0, L), R("one", 0, L), ACT.Copy, 0.0)
-        fire(t, n)
-        act(R("thr", 0, P), w, ACT.Relu, -1e26)
-        act(R("nh", 0, P), w, ACT.Relu, -512.0)
         came, n = n, P + L
-        ad = []
-        for a, b, y in ((0, 128, "pr"), (128, P, "ps")):
-            lo = 128 - (b - a)
-            for c in range(4):
-                act(R("hh", 4 * a + c, 4 * b, 4), R(y, 512 * c + lo, 512 * c + 128), ACT.Relu, 0.03125)
-            quant(qh, sh, b - 128, b, R("hh", 4 * (b - 128), 4 * b))
-            mm(R(y, 0, 128), "qu", "su", 0, qh, sh, b - 128, b)
-            mm(R(y, 512, 640), "qu7", "su7", 0, qh, sh, b - 128, b)
-            if a:
-                ts(R("bt", 4 * a, 4 * b, 4), R(y, lo, 128), 0.0, ALU.is_gt)
-            else:
-                act(R("sg", a, b), R(y, lo, 128), ACT.Sign)
-                act(R("bt", 4 * a, 4 * b, 4), R("sg", a, b), ACT.Relu)
-            tt(R("nc", a, b), R(y, 512 + lo, 640), R("thr", a, b), ALU.is_le)
-            quant("qb", "sbb", a, a + 128, R("bt", 4 * (b - 128), 4 * b))
-            mm(R(y, 1024, 1152), "qwb", "swb", 0, "qb", "sbb", a, a + 128)
-            ad.append(R(y, 1024 + lo, 1152))
-            places("nz", "nw", "ol", R("nc", a, b), a, b)
-            tt(R("val", a, b), ad[-1], R("kfr", a, b), ALU.add)
-            scat(R("lwin"), R("ol", a // 16, b // 16), R("val", a, b))
-        s = send(sh, "s", t, [send(qh, "q", t, own)])
+        if t:
+            act(R("lwin", 0, L), R("one", 0, L), ACT.Copy, 0.0)
+            members(1, 0, P, 4 * (BASE[1] + came), CUTS[2])
+            ad = [leave(1, 0, 128), leave(1, 128, P)]
+        else:
+            members(0, 128, P, 4 * BASE[1], CUTS[1])
+            ad.append(leave(0, 128, P))
+        h = P // 2
+        s = send("qa", t, [(R(qh, 0, h), 0)], own)
+        s = send("qb", t, [(R(qh, 256 - h, 256), h)], [s])
+        s = send("s", t, [(R(sh, 0, h), 0), (R(sh, 256 - h, 256), h)], [s])
         nb = BASE[t + 1]
         if t:
             act(R("yy", 0, 4), R("yy", 4 * came, 4 * came + 4), ACT.Copy)
@@ -660,7 +682,7 @@ def rank_program(g, core, T, topo):
         pick(("lw", 0), "c4", R("lwin", 0, L), L)
         ts(R(ls, 0, 24), R("lw", 3, L, 4), col(AOF), ALU.add)
         ts(R(ls, 24, 48), R("lw", 3, L, 4), 256.0, ALU.mult, col(F256), ALU.add)
-        send(ls, "l", t, [s])
+        send("l", t, [(R(ls), 0)], [s])
         for (a, b), y in zip(((0, 128), (128, P)), ad):
             ts(R("t1", a, b), R("nz", 2 * a, 2 * b, 2), -L - 0.5, ALU.is_lt, 256.0, ALU.mult)
             scan(R("reg", a, b), R("t1", a, b), R("nh", a, b), 0.0, ALU.max, ALU.max)
@@ -685,7 +707,13 @@ def rank_program(g, core, T, topo):
         number(t + 1, P, n, True)
     P = PR[2]
     w = R("win2", 0, P)
-    fire(2, n)
+    pick(("w4", 0), "c4x", w, P, BW * B)
+    ts(R("o1", 0, 40), R("w4", 3, P, 4), col(C3), ALU.add, 1.0 / 2048, ALU.mult)
+    act(R("bb", 0, 320), ind(R("sm"), R("o1", 0, 20)), ACT.Copy)
+    cp(R("bb", 320, 640), ind(R("sm"), R("o1", 20, 40)))
+    quant("qbb", "sbq", 0, P, R("bb", 0, 4 * P))
+    for c in range(4):
+        mm(R("pr", 512 * c, 512 * c + P), "wq", "wp", 128 * c, "qbb", "sbq", 0, P)
     ys = R("yy", 4 * n, 4 * n + 4)
     for k in range(4):
         ts(R("ot", 4 * k, 4 * k + 4), ys, 4.0, ALU.mult, float(k), ALU.add)
@@ -711,7 +739,7 @@ def rank_program(g, core, T, topo):
     mm(R("ps", 0, P), "qv", "sv", 0, "qt", "st", NA, NA + P)
     store("s", T.oc[:, 4 * NA:4 * (NA + P)], T.qt[:, NA:NA + P].bitcast(dt.uint8), R("qt"))
     for k in range(4):
-        store("a", T.osc[4 * k:4 * k + 4, :], T.st[32 * k:32 * k + 4, :], R("st"))
+        store("s", T.osc[4 * k:4 * k + 4, :], T.st[32 * k:32 * k + 4, :], R("st"))
     cp(R("yb", NA, NA + P), R("ps", 0, P))
-    store("s", T.y[:, NA:NA + P], T.yb[:, NA:NA + P], R("yb", NA, NA + P))
+    store("a", T.y[:, NA:NA + P], T.yb[:, NA:NA + P], R("yb", NA, NA + P))
     issue(ops, Q, T)

from concourse.bass import DstId, RemoteDMATransfer
from concourse.mybir import dt, AluOpType, ActivationFunctionType

ALU = AluOpType
ACT = ActivationFunctionType
F32, BF, F16, I32, U16, U8, Q4 = "float32", "bfloat16", "float16", "int32", "uint16", "uint8", "float8_e4m3fn_x4"

C, NA, L = 480, 64, 96
PR = [224, 192, 160]
RUNS = ((0, 224, 32, 1), (224, 352, 256, 2), (352, 480, 512, 4))
BASE = [0, 1024, 1344]
NID = 1632
B = 2048.0
BW = 7168.0
B2 = 1024.0
HOP, DMA = 2800.0, 2000.0
CASES = ((240.0, 1.25, 1.15), (190.0, 1.0, 0.85))
TRIES = [6, 15000, 25000]
SLACK = 350.0
PIECES = ((0, 128), (128, 320), (320, 480))
SHARE = (64, 32, 0)
CUTS = ((0, 6, 18), (32, 38, 46), (0, 6, 18, 32))
OWN, CAME = (64, 0), 48
LOADS = 4
ORDER = []


def sb(n, d):
    return ("sbuf", [128, n], d)


SCRATCH = {
    "xt": sb(1920, BF), "ut": sb(512, BF), "vt": sb(512, BF),
    "qx": sb(480, Q4), "sx": sb(480, U8), "qu": sb(128, Q4), "su": sb(128, U8), "qu7": sb(128, Q4), "su7": sb(128, U8),
    "qv": sb(128, Q4), "sv": sb(128, U8), "wq": sb(512, Q4), "wp": sb(512, U8),
    "pool": sb(4 * NID, BF), "sm": sb(16 + 4 * 288, BF), "tok": sb(4 * 288, BF), "bt0": sb(512, BF), "bt": sb(896, BF), "sg": sb(320, BF),
    "qb": sb(384, Q4), "sbb": sb(384, U8),
    "ii": sb(48, I32), "ij": sb(48, I32), "col": sb(40, F32), "iof": sb(224, F32), "ids": sb(608, F16), "kfr": sb(224, F32),
    "idr": sb(480, BF), "idp0": sb(480, F32), "idp": sb(608, F32), "nj": sb(480, F16), "cq": sb(32, F32),
    "jg": sb(128, BF), "jh": sb(140, BF), "jq": sb(128, BF), "tm1": sb(40, F32), "tm2": sb(40, F32), "pat": sb(4, F32),
    "c32": sb(448, BF), "c4": sb(224, BF), "c4x": sb(224, BF), "r16": sb(224, BF), "r4": sb(512, BF), "r64": sb(384, BF), "f4": sb(384, F16),
    "one": sb(512, BF), "tab": sb(768, BF), "o7": sb(8, U16),
    "wc0": sb(512, BF), "wq0": sb(512, BF), "wb0": sb(512, BF), "et": sb(2048, BF),
    "qwc": sb(128, Q4), "swc": sb(128, U8), "qwq": sb(128, Q4), "swq": sb(128, U8), "qwb": sb(128, Q4), "swb": sb(128, U8),
    "qe": sb(512, Q4), "se": sb(512, U8),
    "oe": sb(120, U16), "pq": sb(120, F32), "pq2": sb(32, F32), "ql": sb(32, U16), "mk": sb(480, BF),
    "d0": sb(1920, BF), "y0": sb(1924, BF), "gq": sb(480, BF), "ta0": sb(480, BF), "fw0": sb(480, BF), "bw0": sb(480, BF), "vr0": sb(480, BF),
    "e": sb(1280, BF), "yy": sb(1284, F16), "vv": sb(1280, F16), "q4": sb(1280, F16),
    "ta": sb(320, F16), "fw": sb(320, F16), "bw": sb(320, F16), "vr": sb(320, F16),
    "nf": sb(480, BF), "pz": sb(960, F16), "pw": sb(960, F16), "od": sb(32, U16), "pk": sb(480, F32),
    "win0": sb(768, F32), "win1": sb(768, F32), "win2": sb(768, F32),
    "w4": sb(224, F32), "wi": sb(112, I32), "o2": sb(56, U16), "o1": sb(56, U16), "p4": sb(288, F32), "l4": sb(72, U16),
    "two": sb(896, BF), "bb": sb(896, BF), "qbb": sb(256, Q4), "sbq": sb(256, U8), "hh": sb(896, BF),
    "qh0": sb(256, Q4), "sh0": sb(256, U8), "qh1": sb(256, Q4), "sh1": sb(256, U8),
    "thr": sb(224, F32), "nh": sb(224, BF), "nc": sb(224, BF), "nz": sb(448, F16), "nw": sb(448, F16),
    "ol": sb(14, U16), "val": sb(224, F32), "lwin": sb(512, F32), "lw": sb(96, F32), "li": sb(48, I32), "ko": sb(24, U16),
    "ls0": sb(48, U16), "ls1": sb(48, U16), "t1": sb(224, F16), "reg": sb(224, F16), "idx": sb(224, F16), "iw": sb(224, F16),
    "rq0": sb(224, Q4), "rs0": sb(224, U8), "rl0": sb(48, U16), "rq1": sb(192, Q4), "rs1": sb(192, U8), "rl1": sb(48, U16),
    "mq": sb(192, Q4), "ms": sb(192, U8), "ml": sb(48, U16), "dst": sb(896, BF),
    "tl": sb(1152, BF), "qt": sb(288, Q4), "st": sb(288, U8), "ot": sb(20, U16), "hm": sb(640, F32), "occb": sb(288, F32), "yb": sb(288, F32),
    "pr": ("psum", [128, 2048], F32), "ps": ("psum", [128, 2048], F32),
}
SHARED = {}
for whole, names in (("hf", "ta fw bw vr pz pw nz nw t1 reg idx iw"), ("win", "win0 win1 win2"), ("tm", "tm1 tm2 pat pq pq2")):
    at = 0
    for name in names.split():
        SHARED[name] = (whole, at, SCRATCH[name][1][1])
        at += (SCRATCH[name][1][1] + 31) // 32 * 32
        kind = SCRATCH.pop(name)[2]
    SCRATCH[whole] = sb(at, kind)
SEMAPHORES = ["sv_", "sa_", "sp_", "sg_", "lu", "lx0", "lx1", "lx2", "lw_", "lp_", "lv", "out",
              "aqa0", "aqb0", "as0", "al0", "aqa1", "aqb1", "as1", "al1", "mqa_", "mqb_", "ms_", "ml_", "loc"]
(PI, PQ, G4, H4, QOFF, FIX4, TCOL, ODX, FW, C1, C2, C3, C4, WT, WT0, WQ, AOF, KOF, IFX, F256, TMP, TM2, TM3, POW, G8, K0, K1, K2, K3) = range(29)


def relay_of(src, dst, k, topo):
    ok = [c for c in topo.cores_of(src) if c != src and topo.may_write(c, dst)]
    near = [c for c in ok if topo.die(c) == topo.die(src)] or ok
    return near[0] if k[0] == "q" else near[-1]


def relay_program(g, core, T, topo, src, dst):
    rid, pid = topo.addr(dst, core)
    n = 0
    h = PR[1] // 2
    for k in ("qa", "qb", "s", "l"):
        if relay_of(src, dst, k, topo) == core:
            g.wait_ge(T.sem["m%s_" % k], len(topo.engines(src, core)))
            a, b = T["r%s1" % k[0]][:], T["m" + k[0]][:]
            if k[0] == "q":
                at = 0 if k == "qa" else h
                a, b = T.rq1[:, at:at + h].bitcast(dt.uint8), T.mq[:, at:at + h].bitcast(dt.uint8)
            g.remote_dma(a, b, T.sem["a%s1" % k], T.sem["loc"], pid, rid, topo.mask(core, dst))
            n += len(topo.engines(core, dst))
    if n:
        g.wait_ge(T.sem["loc"], n)


def arrange(ops):
    n = len(ops)
    q, pre, cost, lat = ([o[k] for o in ops] for k in ("q", "pre", "cost", "lat"))
    costs = {c[2]: [c[2] * x for x in cost] for c in CASES}
    cost = costs[CASES[1][2]]
    after = [[] for _ in ops]
    for i in range(n):
        for p in pre[i]:
            after[p].append(i)

    def span(order, gap, hop, cost, first, done, free):
        for i in order[first:]:
            k = q[i]
            t = free[k]
            for p in pre[i]:
                if done[p] > t:
                    t = done[p]
            if k == "x":
                done[i] = t + lat[i] * hop + gap
            else:
                free[k] = t = t + cost[i]
                done[i] = t + lat[i] + gap
        return max(done)

    def score(order, first=0, known=None):
        last = {}
        for i in reversed(order[:first]):
            last.setdefault(q[i], i)
        total, times = 0.0, []
        for c, (gap, hop, rate) in enumerate(CASES):
            done = list(known[c]) if known else [0.0] * n
            free = {k: done[last[k]] - lat[last[k]] - gap if k in last and k != "x" else 0.0 for k in "vapgsx"}
            total += span(order, gap, hop, costs[rate], first, done, free)
            times.append(done)
        return total, times

    def greedy(extra, gap=CASES[1][0]):
        tail = [0.0] * n
        for i in range(n - 1, -1, -1):
            tail[i] = cost[i] + lat[i] + extra[i] + max([gap + tail[s] for s in after[i]] + [0.0])
        left = [len(p) for p in pre]
        ready = {i: 0.0 for i in range(n) if not left[i]}
        free, done, order = dict.fromkeys("vapgsx", 0.0), [0.0] * n, []
        while ready:
            a = min(ready, key=lambda i: (max(ready[i], free[q[i]]), -tail[i]))
            ta = max(ready[a], free[q[a]])
            for b in ready:
                if b != a and q[b] == q[a] != "x":
                    tb = max(ready[b], free[q[b]])
                    if max(tb + tail[b], max(tb + cost[b], ta) + tail[a]) < max(ta + tail[a], max(ta + cost[a], tb) + tail[b]):
                        a, ta = b, tb
            del ready[a]
            order.append(a)
            if q[a] != "x":
                free[q[a]] = ta + cost[a]
            done[a] = ta + cost[a] + lat[a]
            for s in after[a]:
                left[s] -= 1
                if not left[s]:
                    ready[s] = max(done[p] for p in pre[s]) + gap
        return order

    seed = [12345]

    def draw(k):
        seed[0] = (seed[0] * 6364136223846793005 + 1442695040888963407) % (1 << 64)
        return (seed[0] >> 33) % k

    def waits(order, gap, hop, rate):
        cost = costs[rate]
        free, last, done, why = dict.fromkeys("vapgsx", 0.0), {}, [0.0] * n, [None] * n
        for i in order:
            t = free[q[i]]
            if q[i] in last:
                why[i] = (last[q[i]], True)
            for p in pre[i]:
                if done[p] + gap > t:
                    t, why[i] = done[p] + gap, (p, False)
            if q[i] == "x":
                done[i] = t + lat[i] * hop
            else:
                free[q[i]], last[q[i]] = t + cost[i], i
                done[i] = t + cost[i] + lat[i]
        i, pairs = done.index(max(done)), []
        while why[i]:
            if why[i][1]:
                pairs.append((why[i][0], i))
            i = why[i][0]
        return pairs

    def swapped(order, a, b, ahead):
        i, j = order.index(a), order.index(b)
        part = order[i:j + 1]
        move = {b if ahead else a}
        for k in (reversed(part) if ahead else part):
            if k in move:
                move.update(pre[k] if ahead else after[k])
        if (a if ahead else b) in move:
            return None
        one, two = [k for k in part if k in move], [k for k in part if k not in move]
        return order[:i] + (one + two if ahead else two + one) + order[j + 1:]

    def improved(order, tries):
        best, known = score(order)
        now, cur, pairs = best, order, None
        for k in range(tries):
            if not pairs:
                pairs = waits(cur, *CASES[draw(len(CASES))])
            a, b = pairs.pop(draw(len(pairs)))
            ahead = draw(2)
            mates = [i for i in cur if q[i] == q[a]]
            far = mates.index(a) + (-draw(3) if ahead else 1 + draw(3))
            far = mates[min(max(far, 0), len(mates) - 1)]
            o = swapped(cur, far, b, True) if ahead else swapped(cur, a, far, False)
            if o:
                s, times = score(o, cur.index(far if ahead else a), known)
                if s <= now + SLACK * (1 - k / tries) * draw(1000) / 1000:
                    now, cur, pairs, known = s, o, None, times
                    if s < best:
                        best, order = s, o
        return order

    def joined(one, two, cut):
        head = one[:one.index(cut) + 1]
        done = set(head)
        return head + [i for i in two if i not in done]

    found = [improved(greedy([draw(200) for _ in ops]), TRIES[1]) for _ in range(TRIES[0])]
    for cut in [i for i in range(n) if ops[i]["sem"] in ("al0", "al1")]:
        found += sorted((joined(a, b, cut) for a in found for b in found if a is not b), key=lambda o: score(o)[0])[:TRIES[0]]
    order = improved(min(found, key=lambda o: score(o)[0]), TRIES[2])
    return list(range(LOADS)) + [i for i in order if i >= LOADS]


def issue(ops, Q, T):
    if not ORDER:
        ORDER.extend(arrange(ops))
    count, tok = {}, {}
    waited = {k: {} for k in Q}

    def wait(q, s, v):
        if waited[q].get(s, 0) < v:
            Q[q].wait_ge(T.sem[s], v)
            waited[q][s] = v

    for a in ORDER:
        o = ops[a]
        if o["q"] != "x":
            need = {}
            for p in o["pre"]:
                if tok[p] is not None:
                    need[tok[p][0]] = max(need.get(tok[p][0], 0), tok[p][1])
            for s in need:
                wait(o["q"], s, need[s])
            call = o["make"]()
            if o["sem"] != "loc":
                call.then_inc(T.sem[o["sem"]], o["n"])
        count[o["sem"]] = count.get(o["sem"], 0) + o["n"]
        tok[a] = None if o["sem"] in ("loc", "out") else (o["sem"], count[o["sem"]])
    for s in count:
        wait("s", s, count[s])


def rank_program(g, core, T, topo):
    rank = T.rank_of(core)
    if rank is None:
        for r, c in enumerate(T.cores):
            d = T.cores[r ^ 2]
            if core in topo.cores_of(c) and not topo.may_write(c, d):
                relay_program(g, core, T, topo, c, d)
        return
    Q = {"v": g.vector, "a": g.scalar, "p": g.tensor, "g": g, "s": g.sync}
    SEM = {"v": "sv_", "a": "sa_", "p": "sp_", "g": "sg_"}
    ops = []
    log = {}
    own = []

    def R(name, lo=0, hi=None, step=1):
        name, at, n = SHARED.get(name) or (name, 0, SCRATCH[name][1][1])
        lo, hi = at + lo, at + (n if hi is None else hi)
        ap = T[name][:, lo:hi] if step == 1 else T[name][:, lo:hi:step]
        if SCRATCH[name][0] == "psum":
            return (ap, [(name, lo // 512 * 512, lo // 512 * 512 + 512, 1, True)], hi - lo)
        return (ap, [(name, lo, hi, step, False)], len(range(lo, hi, step)))

    def back(name, lo, hi):
        name, at, n = SHARED.get(name) or (name, 0, 0)
        lo, hi = at + lo, at + hi
        return (T[name][:, hi - 1:(lo - 1 if lo else None):-1], [(name, lo, hi, 1, False)], hi - lo)

    def col(c):
        return R("col", c, c + 1)

    def ind(w, o):
        return (w[0].indirect(o[0]), w[1] + o[1], 16 * o[2])

    def meet(a, b):
        if a[1] >= b[2] or b[1] >= a[2]:
            return False
        return not (a[3] == b[3] and a[3] > 1 and (a[1] - b[1]) % a[3] != 0)

    def emit(q, make, outs, ins, cost, sem=None, n=1, lat=0.0, pre=()):
        acc = [(a, True) for o in outs for a in o[1]] + [(a, False) for o in ins if isinstance(o, tuple) for a in o[1]]
        pre = set(pre)
        for a, wr in acc:
            for old, owr, i, oq in log.get(a[0], []):
                if (wr or owr or (a[4] and oq != q)) and meet(a, old):
                    pre.add(i)
        for a, wr in acc:
            log.setdefault(a[0], []).append((a, wr, len(ops), q))
        ops.append({"q": q, "make": make, "pre": sorted(pre), "cost": cost, "lat": lat, "sem": sem or SEM[q], "n": n})
        return len(ops) - 1

    def length(o, ins, rate=None):
        if any(len(i[1]) > 1 for i in ins):
            return 50 + 1.6 * o[2]
        if rate is None:
            rate = 0.5 if all(SCRATCH[x[1][0][0]][2] in (BF, F16, U16) for x in [o] + ins) else 1.0
        return max(64.0, rate * o[2])

    def ap(x):
        return x[0] if isinstance(x, tuple) else x

    def ts(o, i, s1, op0, s2=None, op1=None):
        if op1 is None:
            emit("v", lambda: g.vector.tensor_scalar(o[0], i[0], ap(s1), None, op0), [o], [i, s1], length(o, [i]))
        else:
            emit("v", lambda: g.vector.tensor_scalar(o[0], i[0], ap(s1), ap(s2), op0, op1), [o], [i, s1, s2], length(o, [i]))

    def tt(o, a, b, op):
        emit("v", lambda: g.vector.tensor_tensor(o[0], a[0], b[0], op), [o], [a, b], length(o, [a, b], 1.0 if a[1][0][4] else 2.0))

    def cp(o, i):
        emit("v", lambda: g.vector.tensor_copy(o[0], i[0]), [o], [i], length(o, [i]))

    def scat(w, offs, src, z, a, b, step=512):
        for k in range(a, b, step):
            o, i = R(offs, k // 16, min(k + step, b) // 16), R(src, z + k, z + min(k + step, b))
            emit("v", lambda o=o, i=i: g.vector.tensor_copy(w[0].indirect(o[0]), i[0]), [w], [i, o], 50 + 3.8 * i[2])

    def scan(o, a, b, init, op0, op1):
        emit("v", lambda: g.vector.tensor_tensor_scan(o[0], a[0], b[0], ap(init), op0, op1), [o], [a, b, init], length(o, [a, b]))

    def ms(o, c):
        emit("v", lambda: g.vector.memset(o[0], c), [o], [], length(o, []))

    def tr(o, i):
        emit("v", lambda: g.vector.transpose(o[0], i[0]), [o], [i], length(o, [i]))

    def quant(qn, sn, lo, hi, i):
        a, b = R(qn, lo, hi), R(sn, lo, hi)
        emit("v", lambda: g.vector.quantize_mx(a[0], b[0], i[0]), [a, b], [i], 15 + 0.27 * i[2])

    def mm(o, wq, ws, w0, xq, xs, lo, hi):
        a, b, c, d = R(wq, w0, w0 + 128), R(ws, w0, w0 + 128), R(xq, lo, hi), R(xs, lo, hi)
        emit("p", lambda: g.tensor.matmul_mx(o[0], a[0], b[0], c[0], d[0], True, True), [o], [a, b, c, d], 1.2 * (hi - lo + 16))

    def act(o, i, f, scale=1.0, bias=None):
        c = 15 + length(o, [i], 1.0) + (1300 if f == ACT.Exp else 0)
        if bias is None:
            emit("a", lambda: g.scalar.activation(o[0], i[0], f, scale=ap(scale)), [o], [i, scale], c)
        else:
            emit("a", lambda: g.scalar.activation(o[0], i[0], f, bias=ap(bias), scale=ap(scale)), [o], [i, scale, bias], c)

    def lin(c, a, scale, bias):
        act(col(c), col(a), ACT.Identity, scale, bias)

    def iota(o, pat, base, cm, small=True):
        if small:
            own.append(emit("g", lambda: g.iota(o[0], pat, base, cm, allow_small_or_imprecise_dtypes=True), [o], [], 130 + 2.2 * o[2]))
        else:
            own.append(emit("g", lambda: g.iota(o[0], pat, base, cm), [o], [], 130 + 2.2 * o[2]))

    def keep(o, pat, op, base, cm):
        i = R("one", 0, o[2])
        own.append(emit("g", lambda: g.affine_select(o[0], i[0], pat, op, 0.0, base, cm), [o], [i], 170 + 2.2 * o[2]))

    def load(q, o, src, sem, late, codes=False, pre=()):
        emit(q, lambda: Q[q].dma_start(o[0].bitcast(dt.uint8) if codes else o[0], src), [o], [], 100, sem, 16, DMA + late, pre)

    def picked(a, b, o, codes):
        if codes:
            emit("v", lambda: g.vector.tensor_copy(a[0].bitcast(dt.uint32), b[0].bitcast(dt.uint32).indirect(o[0])), [a], [b, o], 250)
        else:
            emit("a", lambda: g.scalar.activation(a[0], b[0].indirect(o[0]), ACT.Copy), [a], [b, o], 270)

    peer = [T.cores[rank ^ 1], T.cores[rank ^ 2]]

    def send(k, t, parts, pre):
        direct = topo.may_write(core, peer[t])
        if direct:
            dst, land, far = peer[t], "r%s%d" % (k[0], t), "a%s%d" % (k, t)
        else:
            dst, land, far = relay_of(core, peer[t], k, topo), "m" + k[0], "m%s_" % k
        rid, pid = topo.addr(dst, core)
        use = topo.engines(core, dst)
        each = len(use) // len(parts)
        sides = [(T[land][:, at:at + i[2]], i[0]) for i, at in parts]
        if k[0] == "q":
            sides = [(a.bitcast(dt.uint8), b.bitcast(dt.uint8)) for a, b in sides]

        def make():
            if len(parts) == 1:
                return g.remote_dma(sides[0][0], sides[0][1], T.sem[far], T.sem["loc"], pid, rid, topo.mask(core, dst))
            return g.remote_dma_fused([RemoteDMATransfer(
                dst_ids=[DstId(rid=rid, pnc=pid)], dma_engine_mask=sum(1 << e for e in use[each * j:each * j + each]),
                remote_sem=T.sem[far], src=b, dst=a) for j, (a, b) in enumerate(sides)], local_sem=T.sem["loc"])

        s = emit("g", make, [], [i for i, at in parts], 1000, "loc", len(use), 0.0, pre)
        last = peer[t] if direct else relay_of(peer[t], core, k, topo)
        emit("x", None, [R("r%s%d" % (k[0], t), at, at + i[2]) for i, at in parts], [], 0.0, "a%s%d" % (k, t), len(topo.engines(last, core)),
             (HOP if direct else 2 * HOP + 1000) + (1500 if k[0] == "q" else 0), [s])
        return s

    def store(q, o, i, src):
        emit(q, lambda: Q[q].dma_start(o, i), [], [src], 100, "out", 16, DMA + src[2])

    def pick(o, c, x, n, b=B):
        scan(R(o[0], o[1], o[1] + n), R(c, 0, n), x, -b, ALU.add, ALU.min)

    load("s", R("ut"), T.u[:], "lu", 1000)
    for k, (a, b) in enumerate(PIECES):
        load("as"[k % 2], R("xt", 4 * a, 4 * b), T.x[:, 4 * a:4 * b], "lx%d" % k, 800 + 4 * b)
    load("s", R("wq"), T.wc[:], "lw_", 1500, True, [LOADS - 1])
    load("s", R("wp"), T.ws[:], "lp_", 2000, False, [LOADS - 1])
    load("s", R("vt"), T.v[:], "lv", 2500, False, [LOADS - 1])

    iota(R("ii", 40, 41), [[0, 1]], 0, 1, False)
    iota(R("jh"), [[1, 35], [0, 4]], -3, 0)
    iota(R("jq"), [[8, 8], [0, 4], [-1, 4]], 0, 0)
    iota(R("iof", 0, 128), [[1, 128]], 0, 0)
    iota(R("iof", 128, 224), [[1, 96]], 128, 0)
    iota(R("ii", 0, 32), [[1, 32]], 256, -2, False)
    iota(R("cq"), [[64, 32]], 0, 0)
    for a, b, first, step in RUNS:
        iota(R("idr", a, b), [[-step, b - a]], -first, 0)
    for k in (0, 320):
        iota(R("idp", k, min(k + 320, 608)), [[8192, min(320, 608 - k)]], 8192 * (BASE[1] + k), 0)
    ms(R("one"), 1.0)
    keep(R("r16"), [[0, 14], [1, 16]], ALU.not_equal, 0, 0)
    keep(R("r64"), [[0, 6], [1, 64]], ALU.not_equal, 0, 0)
    keep(R("r4"), [[0, 128], [1, 4]], ALU.not_equal, 0, 0)
    iota(R("ii", 32, 40), [[16, 8]], 7, 0, False)
    iota(R("jg"), [[4, 8], [0, 16]], 0, 0)
    iota(R("wb0"), [[0, 512]], 0, 0)
    iota(R("bt"), [[0, 896]], 0, 0)
    for b in range(4):
        keep(R("et", 512 * b, 512 * b + 512), [[0, 1], [1, 512]], ALU.is_equal, -b, -4)
        quant("qe", "se", 128 * b, 128 * b + 128, R("et", 512 * b, 512 * b + 512))
    p_ = R("ii", 40, 41)
    ts(R("ij", 40, 41), p_, 15, ALU.bitwise_and)
    ts(R("ij", 41, 42), p_, 3, ALU.bitwise_and)
    ts(R("ij", 42, 43), p_, 2, ALU.logical_shift_right, 28, ALU.bitwise_and)
    ts(R("ij", 43, 44), p_, 2, ALU.logical_shift_right, 3, ALU.bitwise_and)
    cp(R("col", PI, H4 + 1), R("ij", 40, 44))
    ts(R("tm2", 0, 8), R("iof", 0, 8), col(PI), ALU.is_lt, 1.0, ALU.add)
    scan(R("tm1", 0, 8), R("tm2", 0, 8), R("one", 0, 8), 1.0, ALU.mult, ALU.mult)
    ts(col(QOFF), col(PQ), -16.0, ALU.mult, 48.0, ALU.add)
    ms(R("bt0", 128, 512), 0.0)
    ms(R("y0", 0, 4), 256.0)
    ts(col(TCOL), col(PI), 48.0, ALU.add)
    ts(col(FIX4), col(H4), 2.5, ALU.is_lt, B, ALU.mult)
    ts(R("tm1", 36, 37), col(PI), 14.5, ALU.is_lt, -B2, ALU.mult)
    ts(R("sg", 0, 128), R("iof", 0, 128), col(TCOL), ALU.is_equal, -9.0, ALU.mult)
    ts(R("tab", 0, 128), R("sg", 0, 128), 1.0, ALU.add)
    ts(R("ij", 0, 32), R("ii", 0, 32), 31, ALU.bitwise_and)
    ts(R("ii", 42, 46), R("iof", 4, 8), col(H4), ALU.subtract)
    ts(R("ij", 32, 36), R("ii", 42, 46), 3, ALU.bitwise_and)
    ts(col(TMP), col(PI), 7.0, ALU.is_equal, 128.0, ALU.mult)
    ts(col(WT0), col(PI), 5.5, ALU.is_lt, R("tm1", 7, 8), ALU.mult)
    ts(col(TM3), col(PI), 3.5, ALU.is_gt, 0.0625, ALU.mult)
    tt(col(WQ), col(WT0), col(TM3), ALU.mult)
    lin(WT, WT0, 1.0, col(TMP))
    lin(G8, G4, 2.0, 0.0)
    ts(R("col", K0, K3 + 1), R("iof", 0, 4), -1.0, ALU.mult, col(G8), ALU.add)
    for t in range(4):
        ts(R("wc0", t, 512, 4), R("jh", 12 - 4 * t, 140 - 4 * t), col(G4), ALU.is_equal, col(WT0), ALU.mult)
        ts(R("wq0", t, 512, 4), R("jq"), col(K0 + t), ALU.is_equal, col(WQ), ALU.mult)
    quant("qwc", "swc", 0, 128, R("wc0"))
    quant("qwq", "swq", 0, 128, R("wq0"))
    ts(R("wb0", 0, 512, 4), R("jg"), col(G4), ALU.is_equal, col(WT), ALU.mult)
    quant("qwb", "swb", 0, 128, R("wb0"))
    scan(R("nj"), R("one", 0, 480), R("one", 0, 480), -255.0, ALU.mult, ALU.subtract)
    act(R("tab", 128, 256), R("one", 0, 128), ACT.Copy)
    act(R("tab", 512, 768), R("one", 0, 256), ACT.Copy)
    for r in (2, 3):
        act(R("tab", 128 * r, 128 * r + 128), R("tab", 0, 128), ACT.Copy)
    for k in (0, 240):
        act(R("idp0", k, k + 240), R("idr", k, k + 240), ACT.Copy, -8192.0)
    for k in (0, 320):
        act(R("ids", k, min(k + 320, 608)), R("idp", k, min(k + 320, 608)), ACT.Copy, 1.0 / 8192)
    act(R("kfr"), R("iof"), ACT.Copy, 1.0 / 256)
    act(col(ODX), R("tm1", 36, 37), ACT.Identity, 1.0, -1.0)
    lin(TM2, PI, 4.0, col(FIX4))
    act(R("cq"), R("cq"), ACT.Identity, 1.0, col(TM2))
    lin(FW, FIX4, BW, 0.0)
    lin(C1, PQ, 1.0, 8192.0)
    lin(TM2, PQ, 2048.0, col(FW))
    lin(C2, TM2, 1.0, 860.0)
    lin(C3, TM2, 1.0, -8192.0 * (BASE[2] - 4))
    lin(C4, FIX4, -4.0, col(PQ))
    lin(IFX, FIX4, 1.0, col(QOFF))
    lin(F256, FIX4, 256.0, 0.0)
    lin(KOF, PQ, 224.0, 0.0)
    lin(AOF, IFX, 1.0, 128.0 - 0.44)
    ts(R("tm1", 0, 32), R("ij", 0, 32), 0.0, ALU.is_equal, 4 * B2, ALU.mult)
    ts(R("tm2", 0, 32), R("ij", 0, 32), 2.0, ALU.is_equal, -B2, ALU.mult)
    tt(R("c32", 0, 32), R("tm1", 0, 32), R("tm2", 0, 32), ALU.add)
    for a, b in ((32, 64), (64, 128), (128, 256), (256, 448)):
        act(R("c32", a, b), R("c32", 0, b - a), ACT.Copy)
    ts(R("tm1", 32, 36), R("ij", 32, 36), 0.0, ALU.is_equal, 4 * B, ALU.mult)
    ts(R("tm2", 32, 36), R("ij", 32, 36), 1.0, ALU.is_equal, -B, ALU.mult)
    tt(R("pat"), R("tm1", 32, 36), R("tm2", 32, 36), ALU.add)
    for k in range(4):
        act(R("c4", k, 224, 4), R("one", 0, 56), ACT.Copy, R("pat", k, k + 1))
    act(R("c4x"), R("c4"), ACT.Copy, BW)
    act(R("pool", 0, 16), R("one", 0, 16), ACT.Copy, 0.0)
    act(R("sm", 0, 16), R("one", 0, 16), ACT.Copy, 0.0)
    act(R("tl", 256, 512), R("one", 0, 256), ACT.Copy, 0.0)
    act(R("tl", 640, 1152), R("one", 0, 512), ACT.Copy, 0.0)
    act(R("occb", NA + PR[2], 288), R("one", 0, 64), ACT.Copy, 0.0)
    for t in range(3):
        act(R("win%d" % t, 0, PR[t]), R("one", 0, PR[t]), ACT.Copy, -1.0)
    for a, b, first, step in RUNS:
        if step == 1:
            for k in range(a, b, 56):
                act(R("pool", 4 * (first + k), 4 * (first + k + 56)), R("xt", 4 * k, 4 * (k + 56)), ACT.Copy, 0.5)
        else:
            for t in range(4):
                act(R("pool", 4 * first + t, 4 * (first + step * (b - a)), 4 * step), R("xt", 4 * a + t, 4 * b, 4), ACT.Copy, 0.5)
    quant("qu", "su", 0, 128, R("ut"))
    quant("qv", "sv", 0, 128, R("vt"))
    cp(R("o7"), R("ii", 32, 40))
    picked(R("qu7"), R("qu"), R("o7"), True)
    picked(R("su7"), R("su"), R("o7"), False)

    def marks(offs, z, s0, s1, m):
        m += s0
        if m > s0:
            cp(R("d0", 4 * s0, 4 * m), ind(R("tab"), R(offs, (s0 - z) // 4, (m - z) // 4)))
            ts(R("e", 4 * s0, 4 * m), R("d0", 4 * s0, 4 * m), -1.0, ALU.add, 1.0 / 9, ALU.mult)
        act(R("d0", 4 * m, 4 * s1), ind(R("tab"), R(offs, (m - z) // 4, (s1 - z) // 4)), ACT.Copy)
        act(R("e", 4 * m, 4 * s1), R("d0", 4 * m, 4 * s1), ACT.Identity, 1.0 / 9, -1.0 / 9)

    def rows(t, s0, s1):
        a, b = 4 * s0, 4 * s1
        z = BASE[t] - BASE[1]
        for q in range(4):
            scan(R("yy", 4 + a + q, 4 + b, 4), R("d0", a + q, b, 4), R("ids", z + s0, z + s1), R("yy", a + q, a + q + 1), ALU.mult, ALU.min)
        scan(R("vv", a, b), R("yy", a, b), R("e", a, b), 0.0, ALU.max, ALU.mult)

    def places(z, w, o, nf, s0, s1):
        scan(R(z, 2 * s0, 2 * s1, 2), nf, R("one", 0, s1 - s0), R(z, 2 * s0 - 2, 2 * s0 - 1) if s0 else 0.0, ALU.add, ALU.subtract)
        scan(R(z, 2 * s0 + 1, 2 * s1, 2), nf, R("nj", s0, s1), 0.0, ALU.max, ALU.mult)
        pick((w, 2 * s0), "c32", R(z, 2 * s0, 2 * s1), 2 * (s1 - s0), B2)
        ts(R(o, s0 // 16, s1 // 16), R(w, 2 * s0 + 31, 2 * s1, 32), -1.0, ALU.mult, col(ODX), ALU.add)

    def number(t, s0, s1, last):
        x = "" if t else "0"
        n = s1 - s0
        if t and last:
            for q in range(4):
                tr(R("q4", 4 * s0 + q, 4 * s1, 4), R("vv", 4 * s0 + q, 4 * s1, 4))
            scan(R("f4"), R("r64"), R("q4", 4 * s0, 4 * s1), 0.0, ALU.mult, ALU.min)
            fw = (T.f4[:, 4 * n - 1:2:-4], R("f4")[1], n)
        else:
            if t:
                scan(R("q4", 4 * s0, 4 * s1), R("r4", 0, 4 * n), R("vv", 4 * s0, 4 * s1), 0.0, ALU.mult, ALU.min)
            tr(R("ta" + x, s0, s1), R("q4", 4 * s0 + 3, 4 * s1, 4) if t else R("gq", s0, s1))
            scan(R("fw" + x, s0, s1), R("r16", 0, n), R("ta" + x, s0, s1), 0.0, ALU.mult, ALU.min)
            fw = back("fw" + x, s0, s1)
        scan(back("bw" + x, s0, s1), R("r16", 0, n), fw, 0.0, ALU.mult, ALU.min)
        v = R("vr" + x, s0, s1)
        tr(v, R("bw" + x, s0, s1))
        if t and last:
            ts(R("nf", s0, s1), v, -0.5, ALU.is_gt)
        else:
            act(R("nf", s0, s1), v, ACT.Relu, 1.0, 1.0)
        places("pz", "pw", "od", R("nf", s0, s1), s0, s1)
        z = BASE[t] - BASE[1]
        if t < 2:
            scan(R("pk", s0, s1), v, R("idp", z + s0, z + s1) if t else R("idp0", s0, s1), 0.0, ALU.min, ALU.add)
            scat(R("win%d" % t), "od", "pk", 0, s0, s1, 64 if t and not last else 512)
        else:
            pick(("p4", s0), "c4", v, n)
            ts(R("l4", s0 // 4, s1 // 4), R("p4", s0 + 3, s1, 4), -4.0, ALU.mult, col(C4), ALU.add)
            k = 24 if last else 32
            for a in range(s0, s1, k):
                tt(R("sm", 16 + 4 * a, 16 + 4 * (a + k)), ind(R("pool", 0, 4 * (BASE[t] + s1)), R("l4", a // 4, (a + k) // 4)),
                   R("tok", 4 * a, 4 * (a + k)), ALU.add)
            scat(R("win2"), "od", "idp", z, s0, s1)

    def members(t, lo, hi, top, cuts):
        m0, m = lo // 4, hi // 4
        pick(("w4", lo), "c4x", R("win%d" % t, lo, hi), hi - lo, BW * B)
        w = R("w4", lo + 3, hi, 4)
        ts(R("o2", m0, m), w, col(C2), ALU.add, 1.0 / 2048, ALU.mult)
        ts(R("wi", m0, m), w, col(FW), ALU.add)
        ts(R("wi", 56 + m0, 56 + m), R("wi", m0, m), 2047, ALU.bitwise_and)
        ts(R("o1", m0, m), R("wi", 56 + m0, 56 + m), -4.0, ALU.mult, col(C1), ALU.add)
        for a, b in zip(cuts, cuts[1:] + (m,)):
            if a > m0:
                act(R("two", 16 * a, 16 * b), ind(R("pool", 0, top), R("o2", a, b)), ACT.Copy)
            else:
                cp(R("two", 16 * a, 16 * b), ind(R("pool", 0, top), R("o2", a, b)))
            tt(R("bb", 16 * a, 16 * b), ind(R("pool", 0, top), R("o1", a, b)), R("two", 16 * a, 16 * b), ALU.add)

    def leave(t, a, b):
        qh, sh, y, lo = "qh%d" % t, "sh%d" % t, "ps" if a else "pr", 128 - (b - a)
        quant("qbb", "sbq", a, a + 128, R("bb", 4 * (b - 128), 4 * b))
        for c in range(4):
            mm(R(y, 512 * c, 512 * c + 128), "wq", "wp", 128 * c, "qbb", "sbq", a, a + 128)
            act(R("hh", 4 * a + c, 4 * b, 4), R(y, 512 * c + lo, 512 * c + 128), ACT.Relu, 0.03125)
        quant(qh, sh, a, a + 128, R("hh", 4 * (b - 128), 4 * b))
        mm(R(y, 0, 128), "qu", "su", 0, qh, sh, a, a + 128)
        mm(R(y, 512, 640), "qu7", "su7", 0, qh, sh, a, a + 128)
        ts(R("bt", 4 * a, 4 * b, 4), R(y, lo, 128), 0.0, ALU.is_gt)
        w = R("win%d" % t, a, b)
        act(R("thr", a, b), w, ACT.Relu, -1e26)
        act(R("nh", a, b), w, ACT.Relu, -512.0)
        tt(R("nc", a, b), R(y, 512 + lo, 640), R("thr", a, b), ALU.is_le)
        quant("qb", "sbb", a, a + 128, R("bt", 4 * (b - 128), 4 * b))
        mm(R(y, 1024, 1152), "qwb", "swb", 0, "qb", "sbb", a, a + 128)
        places("nz", "nw", "ol", R("nc", a, b), a, b)
        tt(R("val", a, b), R(y, 1024 + lo, 1152), R("kfr", a, b), ALU.add)
        scat(R("lwin"), "ol", "val", 0, a, b)
        return R(y, 1024 + lo, 1152)

    act(R("lwin", 0, L), R("one", 0, L), ACT.Copy, 0.0)
    for h, (a, b) in enumerate(PIECES):
        quant("qx", "sx", a, b, R("xt", 4 * a, 4 * b))
        y, z = ("pr", "ps")[h % 2], 1024 * (h // 2)
        s = R(y, z, z + b - a)
        mm(s, "qu", "su", 0, "qx", "sx", a, b)
        ts(R("bt0", a, b), s, 0.0, ALU.is_gt)
        quant("qb", "sbb", 128 * h, 128 * h + 128, R("bt0"))
        mm(R(y, z, z + 128), "qwc", "swc", 0, "qb", "sbb", 128 * h, 128 * h + 128)
        ts(R("oe", a // 4, b // 4), R(y, z + a // 4, z + b // 4), col(QOFF), ALU.add)
        if h == 0:
            continue
        a = a if h > 1 else 0
        mm(R(y, z + 512, z + 640), "qwq", "swq", 0, "qb", "sbb", 128 * h, 128 * h + 128)
        pick(("pq", a // 4), "c4", R(y, z + 512 + a // 4, z + 512 + b // 4), (b - a) // 4)
        tt(R("pq2", a // 16, b // 16), R("pq", a // 4 + 3, b // 4, 4), R("cq", a // 16, b // 16), ALU.add)
        cp(R("ql", a // 16, b // 16), R("pq2", a // 16, b // 16))
    for h, (s0, s1) in enumerate(PIECES):
        a, b, m = 4 * s0, 4 * s1, s0 + SHARE[h]
        if m > s0:
            cp(R("d0", a, 4 * m), ind(R("tab", 0, 128), R("oe", s0 // 4, m // 4)))
        act(R("d0", 4 * m, b), ind(R("tab", 0, 128), R("oe", m // 4, s1 // 4)), ACT.Copy)
        for q in range(4):
            scan(R("y0", 4 + a + q, 4 + b, 4), R("d0", a + q, b, 4), R("idr", s0, s1), R("y0", a + q, a + q + 1), ALU.mult, ALU.max)
        o = R("ql", s0 // 16, s1 // 16)
        act(R("mk", s0, s1), ind(R("d0", 0, b), o), ACT.Relu, -0.125)
        tt(R("gq", s0, s1), ind(R("y0", 0, b), o), R("mk", s0, s1), ALU.mult)
        number(0, s0, s1, s1 == C)
        if s1 == NA + 2 * 128:
            members(0, 0, 128, 4 * (RUNS[1][2] + RUNS[1][3] * (s1 - RUNS[1][0])), CUTS[0])
            ad = [leave(0, 0, 128)]
    act(R("yy", 0, 4), R("y0", 4 * C, 4 * C + 4), ACT.Copy, -1.0)
    n = C
    for t in range(2):
        P = PR[t]
        qh, sh, ls, rl = "qh%d" % t, "sh%d" % t, "ls%d" % t, "rl%d" % t
        came, n = n, P + L
        if t:
            act(R("lwin", 0, L), R("one", 0, L), ACT.Copy, 0.0)
            members(1, 0, P, 4 * (BASE[1] + came), CUTS[2])
            ad = [leave(1, 0, 128), leave(1, 128, P)]
        else:
            members(0, 128, P, 4 * BASE[1], CUTS[1])
            ad.append(leave(0, 128, P))
        h = P // 2
        s = send("qa", t, [(R(qh, 0, h), 0)], own)
        s = send("qb", t, [(R(qh, 256 - h, 256), h)], [s])
        s = send("s", t, [(R(sh, 0, h), 0), (R(sh, 256 - h, 256), h)], [s])
        nb = BASE[t + 1]
        if t:
            act(R("yy", 0, 4), R("yy", 4 * came, 4 * came + 4), ACT.Copy)
        for k in range(0, 4 * P, 2 * P):
            act(R("pool", 4 * nb + k, 4 * nb + k + 2 * P), R("hh", k, k + 2 * P), ACT.Copy, 0.5)
            if t:
                act(R("tok", k, k + 2 * P), R("hh", k, k + 2 * P), ACT.Copy, 0.5)
        pick(("lw", 0), "c4", R("lwin", 0, L), L)
        ts(R(ls, 0, 24), R("lw", 3, L, 4), col(AOF), ALU.add)
        ts(R(ls, 24, 48), R("lw", 3, L, 4), 256.0, ALU.mult, col(F256), ALU.add)
        send("l", t, [(R(ls), 0)], [s])
        for (a, b), y in zip(((0, 128), (128, P)), ad):
            ts(R("t1", a, b), R("nz", 2 * a, 2 * b, 2), -L - 0.5, ALU.is_lt, 256.0, ALU.mult)
            scan(R("reg", a, b), R("t1", a, b), R("nh", a, b), 0.0, ALU.max, ALU.max)
            tt(R("idx", a, b), y, R("reg", a, b), ALU.add)
            pick(("iw", a), "c4", R("idx", a, b), b - a)
            ts(R("oe", a // 4, b // 4), R("iw", a + 3, b, 4), col(IFX), ALU.add)
        for (s0, s1), m in zip(((0, 128), (128, P)), OWN):
            marks("oe", 0, s0, s1, m)
            rows(t + 1, s0, s1)
            number(t + 1, s0, s1, False)
        cp(R("li", 0, 24), R(rl, 24, 48))
        ts(R("li", 24, 48), R("li", 0, 24), 255, ALU.bitwise_and)
        ts(R("ko"), R("li", 24, 48), col(KOF), ALU.add)
        for b in range(4):
            mm(R("pr", 512 * b, 512 * b + P), "qe", "se", 128 * b, "rq%d" % t, "rs%d" % t, 0, P)
            act(R("dst", 224 * b, 224 * b + P), R("pr", 512 * b, 512 * b + P), ACT.Copy, 0.5)
        marks(rl, P, P, n, CAME)
        act(R("pool", 4 * (nb + P), 4 * (nb + n)), ind(R("dst"), R("ko")), ACT.Copy)
        if t:
            act(R("tok", 4 * P, 4 * n), R("pool", 4 * (nb + P), 4 * (nb + n)), ACT.Copy)
        rows(t + 1, P, n)
        number(t + 1, P, n, True)
    P = PR[2]
    w = R("win2", 0, P)
    pick(("w4", 0), "c4x", w, P, BW * B)
    ts(R("o1", 0, 40), R("w4", 3, P, 4), col(C3), ALU.add, 1.0 / 2048, ALU.mult)
    act(R("bb", 0, 320), ind(R("sm"), R("o1", 0, 20)), ACT.Copy)
    cp(R("bb", 320, 640), ind(R("sm"), R("o1", 20, 40)))
    quant("qbb", "sbq", 0, P, R("bb", 0, 4 * P))
    for c in range(4):
        mm(R("pr", 512 * c, 512 * c + P), "wq", "wp", 128 * c, "qbb", "sbq", 0, P)
    ys = R("yy", 4 * n, 4 * n + 4)
    for k in range(4):
        ts(R("ot", 4 * k, 4 * k + 4), ys, 4.0, ALU.mult, float(k), ALU.add)
        act(R("tl", k, 4 * NA, 4), ind(R("pool"), R("ot", 4 * k, 4 * k + 4)), ACT.Copy, 2.0)
    ts(R("ot", 16, 20), ys, 1.0, ALU.min)
    act(R("thr", 0, P), w, ACT.Relu, 1e22)
    act(R("occb", 0, NA), ind(R("iof"), R("ot", 16, 20)), ACT.Copy)
    act(R("occb", NA, NA + P), w, ACT.Sign, 1.0, 1.0)
    store("s", T.occ[:], T.occb[0:128:16, :], R("occb"))
    quant("qt", "st", 160, 288, R("tl", 640, 1152))
    quant("qt", "st", 0, 128, R("tl", 0, 512))
    mm(R("ps", 1024, 1152), "qv", "sv", 0, "qt", "st", 160, 288)
    mm(R("ps", 512, 640), "qv", "sv", 0, "qt", "st", 0, 128)
    cp(R("yb", 0, NA), R("ps", 512, 512 + NA))
    cp(R("yb", NA + P, 288), R("ps", 1088, 1152))
    for a in (0, NA + P):
        store("s", T.oc[:, 4 * a:4 * a + 256], T.qt[:, a:a + 64].bitcast(dt.uint8), R("qt", a, a + 64))
        store("s", T.y[:, a:a + 64], T.yb[:, a:a + 64], R("yb", a, a + 64))
    for b in range(4):
        tt(R("hm", P * b, P * b + P), R("pr", 512 * b, 512 * b + P), R("thr", 0, P), ALU.min)
        act(R("tl", 4 * NA + b, 4 * (NA + P), 4), R("hm", P * b, P * b + P), ACT.Relu, 0.03125)
    quant("qt", "st", NA, NA + P, R("tl", 4 * NA, 4 * (NA + P)))
    mm(R("ps", 0, P), "qv", "sv", 0, "qt", "st", NA, NA + P)
    store("s", T.oc[:, 4 * NA:4 * (NA + P)], T.qt[:, NA:NA + P].bitcast(dt.uint8), R("qt"))
    for k in range(4):
        store("s", T.osc[4 * k:4 * k + 4, :], T.st[32 * k:32 * k + 4, :], R("st"))
    cp(R("yb", NA, NA + P), R("ps", 0, P))
    store("a", T.y[:, NA:NA + P], T.yb[:, NA:NA + P], R("yb", NA, NA + P))
    issue(ops, Q, T)
